import numpy as np
import ml_dtypes


def mxq(x, axis, fmt="e4m3"):
    dtype, down = {"e4m3": (ml_dtypes.float8_e4m3fn, 7), "e5m2": (ml_dtypes.float8_e5m2, 14)}[fmt]
    v = np.moveaxis(np.asarray(x, np.float32).astype(ml_dtypes.bfloat16).astype(np.float64), axis, -1)
    blocks = v.reshape(v.shape[:-1] + (-1, 32))
    amax = np.abs(blocks).max(-1, keepdims=True)
    byte = np.maximum(np.where(amax > 0, np.frexp(amax)[1] - 1 + 127, 0) - down, 1)
    scale = np.exp2(byte - 127.0)
    codes = (blocks / scale).astype(np.float32).astype(dtype).astype(np.float64)
    return np.moveaxis((codes * scale).reshape(v.shape), -1, axis)


WIDE = False


def mx_kscale(k):
    if not WIDE:
        return np.ones(k)
    levels = np.array([10, -10, 5, -5, 0])
    if k % 512:
        return np.exp2(np.random.permutation(np.resize(levels, k // 32))).repeat(32)
    a = np.empty((k // 512, 16))
    for p in range(k // 512):
        a[p, :8] = np.random.permutation(np.resize(levels, 8))
        for g in range(8):
            far = levels[np.abs(levels - a[p, g]) >= 10]
            a[p, g + 8] = far[np.random.randint(len(far))]
    return np.exp2(a.ravel()).repeat(32)


def f64(x):
    return np.asarray(x).astype(np.float64)


def striped(idx):
    return np.tile(idx.reshape(-1, 16).T, (8, 1)).astype(np.uint16)


def unstriped(offs):
    return offs[:16].T.reshape(-1).astype(np.int64)


E2M1 = np.array([0.0, 0.5, 1.0, 1.5, 2.0, 3.0, 4.0, 6.0, -0.0, -0.5, -1.0, -1.5, -2.0, -3.0, -4.0, -6.0])


def pack_weight(w, fmt):
    k, n = w.shape
    w = f64(np.asarray(w, np.float32).astype(ml_dtypes.bfloat16)).reshape(k // 32, 32, n)
    amax = np.abs(w).max(1)
    if fmt == "e4m3":
        byte = np.frexp(amax)[1] - 1 + 127 - 7
    else:
        mant, ex = np.frexp(amax / 6.0)
        byte = np.where(mant > 0.5, ex, ex - 1) + 127
    byte = np.clip(np.where(amax > 0, byte, 1), 1, 254)
    scaled = (w * np.exp2(127.0 - byte)[:, None, :]).reshape(k, n).astype(np.float32)
    by_word = np.ascontiguousarray(scaled.reshape(k // 512, 128, 4, n).transpose(0, 1, 3, 2))
    if fmt == "e4m3":
        words = by_word.astype(ml_dtypes.float8_e4m3fn).view(np.uint8)
    else:
        c = by_word.astype(ml_dtypes.float4_e2m1fn).view(np.uint8) & 0xF
        words = (c[..., 0::2] | (c[..., 1::2] << 4)).reshape(k // 512, 128, 2 * n)
    return np.ascontiguousarray(words), np.ascontiguousarray(byte.astype(np.uint8).reshape(k // 512, 16, n))


def unpack_weight(words, scales, fmt):
    g, _, n = scales.shape
    words = np.ascontiguousarray(words).reshape(g, 128, n, -1)
    if fmt == "e4m3":
        vals = words.view(ml_dtypes.float8_e4m3fn).astype(np.float64)
    else:
        nib = np.empty((g, 128, n, 4), np.uint8)
        nib[..., 0::2] = words & 0xF
        nib[..., 1::2] = words >> 4
        vals = E2M1[nib]
    vals = vals * np.repeat(np.exp2(scales.astype(np.float64) - 127.0), 8, axis=1)[..., None]
    return vals.transpose(0, 1, 3, 2).reshape(g * 512, n)


def gelu(v):
    return 0.5 * v * (1.0 + np.tanh(np.sqrt(2.0 / np.pi) * (v + 0.044715 * v**3)))


K, K3, H, N, T, T3, S = 1024, 512, 1024, 512, 2048, 1024, 512

def setup_inputs():
    n = np.random.standard_normal
    s = mx_kscale(K)[:, None]
    s3 = mx_kscale(K3)[:, None]
    u = mx_kscale(H)[:, None]
    tab_words, tab_scales = pack_weight(n((K, T)) * s, "e4m3")
    tab2_words, tab2_scales = pack_weight(n((K, T)) * s, "e4m3")
    tab3_words, tab3_scales = pack_weight(n((K3, T3)) * s3, "e2m1")
    ws_words, ws_scales = pack_weight(0.5 * n((K, H)) / np.sqrt(K) / s, "e2m1")
    wo_words, wo_scales = pack_weight(1.5 * n((H, N)) / np.sqrt(H) / u, "e4m3")
    return {
        "tab_words": tab_words, "tab_scales": tab_scales,
        "tab2_words": tab2_words, "tab2_scales": tab2_scales,
        "tab3_words": tab3_words, "tab3_scales": tab3_scales,
        "offs": striped(np.random.permutation(T)[:S]),
        "offs2": striped(np.random.permutation(T)[:S]),
        "offs3": striped(np.random.permutation(T3)[:S]),
        "ws_words": ws_words, "ws_scales": ws_scales,
        "wt": (n((K3, H)) / np.sqrt(K3) / s3).astype(np.float32),
        "gh": (np.exp(0.3 * n(H)) * u[:, 0]).astype(np.float32),
        "wo_words": wo_words, "wo_scales": wo_scales,
    }

def reference(tab_words, tab_scales, tab2_words, tab2_scales, tab3_words, tab3_scales, offs, offs2, offs3, ws_words, ws_scales, wt, gh, wo_words, wo_scales):
    v = unpack_weight(tab_words, tab_scales, "e4m3")[:, unstriped(offs)]
    v2 = unpack_weight(tab2_words, tab2_scales, "e4m3")[:, unstriped(offs2)]
    v3 = unpack_weight(tab3_words, tab3_scales, "e2m1")[:, unstriped(offs3)]
    ws = unpack_weight(ws_words, ws_scales, "e2m1")
    wo = unpack_weight(wo_words, wo_scales, "e4m3")
    d = (ws.T @ v) - (ws.T @ v2)
    e = mxq(f64(wt), 0, "e4m3").T @ v3
    h = f64(gh)[:, None] * np.tanh(d * (1.0 + np.tanh(e)))
    return wo.T @ mxq(h, 0, "e4m3")

@@ -1,0 +1,294 @@
+from contextlib import ExitStack
+
+import concourse.mybir as mybir
+from concourse.masks import make_identity
+
+FLOPS = 3221225472
+
+F32 = mybir.dt.float32
+BF16 = mybir.dt.bfloat16
+I32 = mybir.dt.int32
+U32 = mybir.dt.uint32
+U16 = mybir.dt.uint16
+U8 = mybir.dt.uint8
+FP8X4 = mybir.dt.float8_e4m3fn_x4
+FP4X4 = mybir.dt.float4_e2m1fn_x4
+ALU = mybir.AluOpType
+ACT = mybir.ActivationFunctionType
+
+P = 128
+PACK = 4
+PASS = P * PACK
+S = 512
+JT = S // P
+T = 2048
+T3 = 1024
+H = 1024
+N = 512
+HALVES = H // PASS
+WT_CHUNK = 256
+CAST_ENGINE = "sg"
+GAIN_ENGINE = "vvvvvvvv"
+AWAY_Q = "s"
+SHIFT_Q = "s"
+ORDER = [(0, 0), (1, 0), (2, 0), (3, 0), (0, 1), (1, 1), (2, 1), (3, 1)]
+
+
+def tile_list_league_market_features_kernel(
+    tc, tab_words, tab_scales, tab2_words, tab2_scales, tab3_words, tab3_scales,
+    offs, offs2, offs3, ws_words, ws_scales, wt, gh, wo_words, wo_scales, out,
+):
+    nc = tc.nc
+    with ExitStack() as ctx:
+        keep = ctx.enter_context(tc.tile_pool(name="keep", bufs=1))
+        ring = ctx.enter_context(tc.tile_pool(name="ring", bufs=3))
+        psum = ctx.enter_context(tc.psum_pool(name="psum", bufs=1))
+
+        def held(name, shape, dtype):
+            return keep.tile(shape, dtype, name=name, align_bytes=64)
+
+        def zeroed(name, width):
+            plane = held(name, [P, width], U8)
+            nc.vector.memset(plane[:].bitcast(I32), 0)
+            return plane
+
+        def load_packed_scales(queue, plane, scales):
+            passes = scales.shape[0]
+            for q in range(4):
+                queue.dma_start(
+                    out=plane[32 * q : 32 * q + 4 * passes, :].bitcast(I32),
+                    in_=scales[:, 4 * q : 4 * q + 4, :].bitcast(I32),
+                )
+
+        def load_scales_side_by_side(queue, plane, scales):
+            for q in range(4):
+                queue.dma_start(
+                    out=plane[32 * q : 32 * q + 4, :].rearrange("r (a c) -> r a c", a=2).bitcast(I32),
+                    in_=scales[:, 4 * q : 4 * q + 4, :].rearrange("a r c -> r a c").bitcast(I32),
+                )
+
+        def load_words(name, words_of_pass):
+            tile = held(name, [P, words_of_pass.shape[1]], I32)
+            nc.sync.dma_start(out=tile[:], in_=words_of_pass.rearrange("p t i -> p (t i)").bitcast(I32))
+            return tile
+
+        def load_list(name, lst):
+            tile = keep.tile([P, S // 16], U16, name=name)
+            nc.sync.dma_start(tile[:], lst)
+            return tile
+
+        queue_of = {"s": nc.sync, "g": nc.gpsimd, "a": nc.scalar}
+        home_sc = zeroed("home_sc", 2 * T)
+        ws_sc = zeroed("ws_sc", 2 * H)
+        away_sc = zeroed("away_sc", T)
+        away_sc1 = zeroed("away_sc1", S)
+        stad_sc = zeroed("stad_sc", T3)
+        wo_sc = zeroed("wo_sc", N)
+
+        home_list = load_list("home_list", offs)
+        home_w0 = load_words("home_w0", tab_words[0])
+        load_scales_side_by_side(nc.sync, home_sc, tab_scales)
+        ws_w = held("ws_w", [P, 2, 2 * H], U8)
+        nc.sync.dma_start(out=ws_w[:].bitcast(I32), in_=ws_words.rearrange("a p c -> p a c").bitcast(I32))
+        load_scales_side_by_side(nc.sync, ws_sc, ws_scales)
+        home_w1 = load_words("home_w1", tab_words[1])
+        away_list = load_list("away_list", offs2)
+        load_packed_scales(queue_of[AWAY_Q], away_sc, tab2_scales)
+        away_w0 = load_words("away_w0", tab2_words[0])
+        stad_list = load_list("stad_list", offs3)
+        stad_w = held("stad_w", [P, 2 * T3], U8)
+        nc.sync.dma_start(out=stad_w[:].bitcast(I32), in_=tab3_words[0].bitcast(I32))
+        load_packed_scales(nc.sync, stad_sc, tab3_scales)
+        away_w1 = load_words("away_w1", tab2_words[1])
+        wt_rows = wt.rearrange("(p j) c -> p j c", j=PACK)
+        wt_raw = []
+        for c in range(H // WT_CHUNK):
+            raw = held("wt_raw%d" % c, [P, PACK, WT_CHUNK], F32)
+            nc.sync.dma_start(out=raw[:], in_=wt_rows[:, :, c * WT_CHUNK : (c + 1) * WT_CHUNK])
+            wt_raw.append(raw)
+        wo_w = held("wo_w", [P, HALVES, N], I32)
+        nc.sync.dma_start(out=wo_w[:], in_=wo_words.rearrange("a p c i -> p a (c i)").bitcast(I32))
+
+        def gather(name, window, lst, dtype, pieces=1):
+            tile = held(name, [P, S], dtype)
+            step = S // pieces
+            for i in range(pieces):
+                nc.vector.tensor_copy(
+                    out=tile[:, i * step : (i + 1) * step],
+                    in_=window.indirect(lst[:, i * step // 16 : (i + 1) * step // 16]),
+                )
+            return tile
+
+        def lower_second_pass(dst, src):
+            queue_of[SHIFT_Q].dma_start(out=dst[0:100, :].bitcast(I32), in_=src[4:104, :].bitcast(I32))
+
+        home_g0 = gather("home_g0", home_w0[:].bitcast(U32), home_list, U32)
+        home_gs = gather("home_gs", home_sc[:, :T], home_list, U8)
+        home_sc1 = gather("home_sc1", home_sc[:, T:], home_list, U8)
+        gain = held("gain", [P, HALVES, PACK], F32)
+        nc.gpsimd.dma_start(out=gain[:], in_=gh.rearrange("(b p t) -> p b t", b=HALVES, t=PACK))
+        load_packed_scales(nc.gpsimd, wo_sc, wo_scales)
+        ident = held("ident", [P, P], F32)
+        make_identity(nc, ident[:])
+        home_g1 = gather("home_g1", home_w1[:].bitcast(U32), home_list, U32, pieces=2)
+        away_gs = gather("away_gs", away_sc[:], away_list, U8)
+        lower_second_pass(away_sc1, away_gs)
+
+        units = [(jt, b) for b in range(HALVES) for jt in range(JT)]
+
+        def side_pass(bank, words, scales, a, jt, b):
+            cols = slice(jt * P, (jt + 1) * P)
+            nc.tensor.matmul_mx(
+                out=bank[:],
+                lhsT=words[:, cols].bitcast(FP8X4),
+                lhsT_scale=scales[:, cols],
+                rhs=ws_w[:, a, 2 * PASS * b : 2 * PASS * (b + 1)].bitcast(FP4X4),
+                rhs_scale=ws_sc[:, a * H + b * PASS : a * H + (b + 1) * PASS],
+                start=(a == 0),
+                stop=(a == 1),
+            )
+
+        def by_slot(bank):
+            return bank[:].rearrange("j (m t) -> j t m", t=PACK)
+
+        home_d = {}
+        for jt, b in units:
+            bank = psum.tile([P, PASS], F32, name="side", tag="side", bufs=4)
+            side_pass(bank, home_g0, home_gs, 0, jt, b)
+            side_pass(bank, home_g1, home_sc1, 1, jt, b)
+            home_d[jt, b] = held("home_d%d%d" % (jt, b), [P, PACK, P], F32)
+            nc.scalar.activation(out=home_d[jt, b][:], in_=by_slot(bank), func=ACT.Copy)
+
+        away_g0 = gather("away_g0", away_w0[:].bitcast(U32), away_list, U32)
+        stad_gs = gather("stad_gs", stad_sc[:], stad_list, U8)
+        stad_g = held("stad_g", [P, 2 * S], U8)
+        nc.vector.tensor_copy(out=stad_g[:].bitcast(U16), in_=stad_w[:].bitcast(U16).indirect(stad_list[:]))
+        away_g1 = gather("away_g1", away_w1[:].bitcast(U32), away_list, U32, pieces=2)
+
+        wt_bf = [held("wt_bf%d" % b, [P, PACK, P, PACK], BF16) for b in range(HALVES)]
+        wt_codes = [held("wt_codes%d" % b, [P, PASS], U32) for b in range(HALVES)]
+        wt_sc = [held("wt_sc%d" % b, [P, PASS], U8) for b in range(HALVES)]
+        m_chunk = WT_CHUNK // PACK
+
+        def round_wt(b):
+            for h in range(PASS // WT_CHUNK):
+                dst = wt_bf[b][:, :, h * m_chunk : (h + 1) * m_chunk, :].rearrange("p t m j -> p m t j")
+                src = wt_raw[b * (PASS // WT_CHUNK) + h][:].rearrange("p j (m t) -> p m t j", t=PACK)
+                if CAST_ENGINE[b] == "s":
+                    nc.scalar.activation(out=dst, in_=src, func=ACT.Copy)
+                elif CAST_ENGINE[b] == "v":
+                    nc.vector.tensor_copy(out=dst, in_=src)
+                else:
+                    nc.gpsimd.tensor_scalar(out=dst, in0=src, scalar1=1.0, scalar2=0.0, op0=ALU.mult, op1=ALU.add)
+
+        def quantise_wt(b):
+            nc.vector.quantize_mx(
+                out=wt_codes[b][:].bitcast(FP8X4),
+                scales=wt_sc[b][:],
+                in_=wt_bf[b][:].rearrange("p t m j -> p (t m j)"),
+            )
+
+        gate = {}
+
+        def stadium(jt, b):
+            bank = psum.tile([P, PACK, P], F32, name="stad", tag="stad", bufs=2)
+            for t in range(PACK):
+                nc.tensor.matmul_mx(
+                    out=bank[:, t, :],
+                    lhsT=wt_codes[b][:, t * P : (t + 1) * P].bitcast(FP8X4),
+                    lhsT_scale=wt_sc[b][:, t * P : (t + 1) * P],
+                    rhs=stad_g[:, 2 * P * jt : 2 * P * (jt + 1)].bitcast(FP4X4),
+                    rhs_scale=stad_gs[:, jt * P : (jt + 1) * P],
+                    start=True,
+                    stop=True,
+                )
+            gate[jt, b] = held("gate%d%d" % (jt, b), [P, P, PACK], F32)
+            nc.scalar.activation(out=gate[jt, b][:], in_=bank[:].rearrange("p t j -> p j t"), func=ACT.Tanh)
+
+        diff = {}
+
+        def difference(jt, b):
+            bank = psum.tile([P, PASS], F32, name="side", tag="side", bufs=4)
+            side_pass(bank, away_g0, away_gs, 0, jt, b)
+            side_pass(bank, away_g1, away_sc1, 1, jt, b)
+            diff[jt, b] = held("diff%d%d" % (jt, b), [P, PACK, P], F32)
+            nc.vector.tensor_tensor(out=diff[jt, b][:], in0=home_d[jt, b][:], in1=by_slot(bank), op=ALU.subtract)
+
+        late = [(jt, b) for b in range(HALVES) for jt in range(JT)]
+        round_wt(0)
+        round_wt(1)
+        for i, (jt, b) in enumerate(late):
+            difference(jt, b)
+            if i == 4:
+                quantise_wt(0)
+        for jt in range(JT):
+            stadium(jt, 0)
+        quantise_wt(1)
+
+        squashed = {}
+        h_bf = {}
+        h_codes = [held("h_codes%d" % jt, [P, HALVES, P], U32) for jt in range(JT)]
+        h_sc = [held("h_sc%d" % jt, [P, HALVES, P], U8) for jt in range(JT)]
+
+        def scale_and_squash(jt, b):
+            bank = psum.tile([P, PACK, P], F32, name="turned", tag="turned", bufs=2)
+            for t in range(PACK):
+                nc.tensor.transpose(bank[:, t, :], diff[jt, b][:, t, :], ident[:])
+            u = ring.tile([P, P, PACK], F32, name="u", align_bytes=64)
+            nc.vector.scalar_tensor_tensor(
+                out=u[:], in0=gate[jt, b][:], scalar=1.0, in1=bank[:].rearrange("p t j -> p j t"),
+                op0=ALU.add, op1=ALU.mult,
+            )
+            squashed[jt, b] = ring.tile([P, P, PACK], F32, name="squashed", align_bytes=64)
+            nc.scalar.activation(out=squashed[jt, b][:], in_=u[:], func=ACT.Tanh)
+
+        def apply_gain(jt, b):
+            h_bf[jt, b] = ring.tile([P, P, PACK], BF16, name="h_bf", align_bytes=64)
+            engine = nc.gpsimd if GAIN_ENGINE[b * JT + jt] == "g" else nc.vector
+            engine.tensor_tensor(
+                out=h_bf[jt, b][:], in0=squashed[jt, b][:],
+                in1=gain[:, b : b + 1, :].to_broadcast([P, P, PACK]), op=ALU.mult,
+            )
+
+        def quantise_h(jt, b):
+            nc.vector.quantize_mx(
+                out=h_codes[jt][:, b, :].bitcast(FP8X4), scales=h_sc[jt][:, b, :],
+                in_=h_bf[jt, b][:].rearrange("p j t -> p (j t)"),
+            )
+
+        out_rows = out.rearrange("(nt p) j -> p nt j", p=P)
+
+        out_bank = {}
+
+        def features(jt, b):
+            if b == 0:
+                out_bank[jt] = psum.tile([P, N // P, P], F32, name="side", tag="side", bufs=4)
+            bank = out_bank[jt]
+            for nt in range(N // P):
+                nc.tensor.matmul_mx(
+                    out=bank[:, nt, :],
+                    lhsT=wo_w[:, b, nt * P : (nt + 1) * P].bitcast(FP8X4),
+                    lhsT_scale=wo_sc[4 * b :, nt * P : (nt + 1) * P],
+                    rhs=h_codes[jt][:, b, :].bitcast(FP8X4),
+                    rhs_scale=h_sc[jt][:, b, :],
+                    start=(b == 0 and nt == 0),
+                    stop=(b == HALVES - 1 and nt == N // P - 1),
+                )
+            if b == HALVES - 1:
+                res = ring.tile([P, N // P, P], F32, name="res")
+                nc.scalar.copy(out=res[:], in_=bank[:])
+                nc.sync.dma_start(out=out_rows[:, :, jt * P : (jt + 1) * P], in_=res[:])
+
+        order = ORDER
+        n = len(order)
+        for i in range(n + 2):
+            if i + 2 < n and order[i + 2][1] == 1:
+                stadium(*order[i + 2])
+            if i < n:
+                scale_and_squash(*order[i])
+            if 1 <= i <= n:
+                apply_gain(*order[i - 1])
+            if i >= 2:
+                jt, b = order[i - 2]
+                quantise_h(jt, b)
+                features(jt, b)

@@ -1,7 +1,6 @@
 from contextlib import ExitStack
 
 import concourse.mybir as mybir
-from concourse.masks import make_identity
 
 FLOPS = 3221225472
 
@@ -27,10 +26,12 @@ H = 1024
 N = 512
 HALVES = H // PASS
 WT_CHUNK = 256
-CAST_ENGINE = "sg"
+CAST_ENGINE = "ssvs"
 GAIN_ENGINE = "vvvvvvvv"
-AWAY_Q = "s"
-SHIFT_Q = "s"
+HOME_MEMSET = "v"
+HOME_Q = "s"
+AWAY_Q = "g"
+SHIFT_Q = "g"
 ORDER = [(0, 0), (1, 0), (2, 0), (3, 0), (0, 1), (1, 1), (2, 1), (3, 1)]
 
 
@@ -47,9 +48,9 @@ def tile_list_league_market_features_kernel(
         def held(name, shape, dtype):
             return keep.tile(shape, dtype, name=name, align_bytes=64)
 
-        def zeroed(name, width):
+        def zeroed(name, width, engine=nc.vector):
             plane = held(name, [P, width], U8)
-            nc.vector.memset(plane[:].bitcast(I32), 0)
+            engine.memset(plane[:].bitcast(I32), 0)
             return plane
 
         def load_packed_scales(queue, plane, scales):
@@ -58,13 +59,6 @@ def tile_list_league_market_features_kernel(
                 queue.dma_start(
                     out=plane[32 * q : 32 * q + 4 * passes, :].bitcast(I32),
                     in_=scales[:, 4 * q : 4 * q + 4, :].bitcast(I32),
-                )
-
-        def load_scales_side_by_side(queue, plane, scales):
-            for q in range(4):
-                queue.dma_start(
-                    out=plane[32 * q : 32 * q + 4, :].rearrange("r (a c) -> r a c", a=2).bitcast(I32),
-                    in_=scales[:, 4 * q : 4 * q + 4, :].rearrange("a r c -> r a c").bitcast(I32),
                 )
 
         def load_words(name, words_of_pass):
@@ -77,20 +71,22 @@ def tile_list_league_market_features_kernel(
             nc.sync.dma_start(tile[:], lst)
             return tile
 
-        queue_of = {"s": nc.sync, "g": nc.gpsimd, "a": nc.scalar}
-        home_sc = zeroed("home_sc", 2 * T)
-        ws_sc = zeroed("ws_sc", 2 * H)
-        away_sc = zeroed("away_sc", T)
+        queue_of = {"s": nc.sync, "g": nc.gpsimd, "a": nc.scalar, "v": nc.vector}
+        home_sc = zeroed("home_sc", T, queue_of[HOME_MEMSET])
+        ws_sc = zeroed("ws_sc", H)
+        away_sc = zeroed("away_sc", T, nc.gpsimd)
+        ws_sc1 = zeroed("ws_sc1", H)
+        home_sc1 = zeroed("home_sc1", S)
         away_sc1 = zeroed("away_sc1", S)
         stad_sc = zeroed("stad_sc", T3)
         wo_sc = zeroed("wo_sc", N)
 
         home_list = load_list("home_list", offs)
         home_w0 = load_words("home_w0", tab_words[0])
-        load_scales_side_by_side(nc.sync, home_sc, tab_scales)
+        load_packed_scales(queue_of[HOME_Q], home_sc, tab_scales)
+        load_packed_scales(nc.sync, ws_sc, ws_scales)
         ws_w = held("ws_w", [P, 2, 2 * H], U8)
         nc.sync.dma_start(out=ws_w[:].bitcast(I32), in_=ws_words.rearrange("a p c -> p a c").bitcast(I32))
-        load_scales_side_by_side(nc.sync, ws_sc, ws_scales)
         home_w1 = load_words("home_w1", tab_words[1])
         away_list = load_list("away_list", offs2)
         load_packed_scales(queue_of[AWAY_Q], away_sc, tab2_scales)
@@ -123,40 +119,55 @@ def tile_list_league_market_features_kernel(
             queue_of[SHIFT_Q].dma_start(out=dst[0:100, :].bitcast(I32), in_=src[4:104, :].bitcast(I32))
 
         home_g0 = gather("home_g0", home_w0[:].bitcast(U32), home_list, U32)
-        home_gs = gather("home_gs", home_sc[:, :T], home_list, U8)
-        home_sc1 = gather("home_sc1", home_sc[:, T:], home_list, U8)
-        gain = held("gain", [P, HALVES, PACK], F32)
-        nc.gpsimd.dma_start(out=gain[:], in_=gh.rearrange("(b p t) -> p b t", b=HALVES, t=PACK))
-        load_packed_scales(nc.gpsimd, wo_sc, wo_scales)
-        ident = held("ident", [P, P], F32)
-        make_identity(nc, ident[:])
+        ws_sc0 = held("ws_sc0", [P, H], U8)
+        nc.vector.tensor_copy(
+            out=ws_sc0[:].rearrange("p (b t m) -> p b t m", b=HALVES, t=PACK),
+            in_=ws_sc[:].rearrange("p (b m t) -> p b t m", b=HALVES, t=PACK),
+        )
+        lower_second_pass(ws_sc1, ws_sc0)
+        home_gs = gather("home_gs", home_sc[:], home_list, U8)
+        lower_second_pass(home_sc1, home_gs)
+        ws_by_slot = []
+        for a in range(2):
+            words = held("ws_by_slot%d" % a, [P, 2 * H], U8)
+            nc.vector.tensor_copy(
+                out=words[:].bitcast(U16).rearrange("p (b t m) -> p b t m", b=HALVES, t=PACK),
+                in_=ws_w[:, a, :].bitcast(U16).rearrange("p (b m t) -> p b t m", b=HALVES, t=PACK),
+            )
+            ws_by_slot.append(words)
+        ws_planes = [ws_sc0, ws_sc1]
         home_g1 = gather("home_g1", home_w1[:].bitcast(U32), home_list, U32, pieces=2)
         away_gs = gather("away_gs", away_sc[:], away_list, U8)
         lower_second_pass(away_sc1, away_gs)
+        gain = held("gain", [P, HALVES, PACK], F32)
+        nc.gpsimd.dma_start(out=gain[:], in_=gh.rearrange("(b p t) -> p b t", b=HALVES, t=PACK))
+        load_packed_scales(nc.gpsimd, wo_sc, wo_scales)
 
         units = [(jt, b) for b in range(HALVES) for jt in range(JT)]
 
         def side_pass(bank, words, scales, a, jt, b):
             cols = slice(jt * P, (jt + 1) * P)
-            nc.tensor.matmul_mx(
-                out=bank[:],
-                lhsT=words[:, cols].bitcast(FP8X4),
-                lhsT_scale=scales[:, cols],
-                rhs=ws_w[:, a, 2 * PASS * b : 2 * PASS * (b + 1)].bitcast(FP4X4),
-                rhs_scale=ws_sc[:, a * H + b * PASS : a * H + (b + 1) * PASS],
-                start=(a == 0),
-                stop=(a == 1),
-            )
+            for t in range(PACK):
+                c0 = b * PASS + t * P
+                nc.tensor.matmul_mx(
+                    out=bank[:, t, :],
+                    lhsT=ws_by_slot[a][:, 2 * c0 : 2 * (c0 + P)].bitcast(FP4X4),
+                    lhsT_scale=ws_planes[a][:, c0 : c0 + P],
+                    rhs=words[:, cols].bitcast(FP8X4),
+                    rhs_scale=scales[:, cols],
+                    start=(a == 0 and t == 0),
+                    stop=(a == 1 and t == PACK - 1),
+                )
 
         def by_slot(bank):
-            return bank[:].rearrange("j (m t) -> j t m", t=PACK)
+            return bank[:].rearrange("p t j -> p j t")
 
         home_d = {}
         for jt, b in units:
-            bank = psum.tile([P, PASS], F32, name="side", tag="side", bufs=4)
+            bank = psum.tile([P, PACK, P], F32, name="side", tag="side", bufs=6)
             side_pass(bank, home_g0, home_gs, 0, jt, b)
             side_pass(bank, home_g1, home_sc1, 1, jt, b)
-            home_d[jt, b] = held("home_d%d%d" % (jt, b), [P, PACK, P], F32)
+            home_d[jt, b] = held("home_d%d%d" % (jt, b), [P, P, PACK], F32)
             nc.scalar.activation(out=home_d[jt, b][:], in_=by_slot(bank), func=ACT.Copy)
 
         away_g0 = gather("away_g0", away_w0[:].bitcast(U32), away_list, U32)
@@ -174,9 +185,9 @@ def tile_list_league_market_features_kernel(
             for h in range(PASS // WT_CHUNK):
                 dst = wt_bf[b][:, :, h * m_chunk : (h + 1) * m_chunk, :].rearrange("p t m j -> p m t j")
                 src = wt_raw[b * (PASS // WT_CHUNK) + h][:].rearrange("p j (m t) -> p m t j", t=PACK)
-                if CAST_ENGINE[b] == "s":
+                if CAST_ENGINE[b * 2 + h] == "s":
                     nc.scalar.activation(out=dst, in_=src, func=ACT.Copy)
-                elif CAST_ENGINE[b] == "v":
+                elif CAST_ENGINE[b * 2 + h] == "v":
                     nc.vector.tensor_copy(out=dst, in_=src)
                 else:
                     nc.gpsimd.tensor_scalar(out=dst, in0=src, scalar1=1.0, scalar2=0.0, op0=ALU.mult, op1=ALU.add)
@@ -208,10 +219,10 @@ def tile_list_league_market_features_kernel(
         diff = {}
 
         def difference(jt, b):
-            bank = psum.tile([P, PASS], F32, name="side", tag="side", bufs=4)
+            bank = psum.tile([P, PACK, P], F32, name="side", tag="side", bufs=6)
             side_pass(bank, away_g0, away_gs, 0, jt, b)
             side_pass(bank, away_g1, away_sc1, 1, jt, b)
-            diff[jt, b] = held("diff%d%d" % (jt, b), [P, PACK, P], F32)
+            diff[jt, b] = held("diff%d%d" % (jt, b), [P, P, PACK], F32)
             nc.vector.tensor_tensor(out=diff[jt, b][:], in0=home_d[jt, b][:], in1=by_slot(bank), op=ALU.subtract)
 
         late = [(jt, b) for b in range(HALVES) for jt in range(JT)]
@@ -231,12 +242,9 @@ def tile_list_league_market_features_kernel(
         h_sc = [held("h_sc%d" % jt, [P, HALVES, P], U8) for jt in range(JT)]
 
         def scale_and_squash(jt, b):
-            bank = psum.tile([P, PACK, P], F32, name="turned", tag="turned", bufs=2)
-            for t in range(PACK):
-                nc.tensor.transpose(bank[:, t, :], diff[jt, b][:, t, :], ident[:])
             u = ring.tile([P, P, PACK], F32, name="u", align_bytes=64)
             nc.vector.scalar_tensor_tensor(
-                out=u[:], in0=gate[jt, b][:], scalar=1.0, in1=bank[:].rearrange("p t j -> p j t"),
+                out=u[:], in0=gate[jt, b][:], scalar=1.0, in1=diff[jt, b][:],
                 op0=ALU.add, op1=ALU.mult,
             )
             squashed[jt, b] = ring.tile([P, P, PACK], F32, name="squashed", align_bytes=64)
@@ -262,7 +270,7 @@ def tile_list_league_market_features_kernel(
 
         def features(jt, b):
             if b == 0:
-                out_bank[jt] = psum.tile([P, N // P, P], F32, name="side", tag="side", bufs=4)
+                out_bank[jt] = psum.tile([P, N // P, P], F32, name="side", tag="side", bufs=6)
             bank = out_bank[jt]
             for nt in range(N // P):
                 nc.tensor.matmul_mx(

@@ -26,13 +26,9 @@ H = 1024
 N = 512
 HALVES = H // PASS
 WT_CHUNK = 256
-CAST_ENGINE = "ssvs"
-GAIN_ENGINE = "vvvvvvvv"
-HOME_MEMSET = "v"
-HOME_Q = "s"
-AWAY_Q = "g"
-SHIFT_Q = "g"
-ORDER = [(0, 0), (1, 0), (2, 0), (3, 0), (0, 1), (1, 1), (2, 1), (3, 1)]
+CAST_ENGINE = "ssss"
+AHEAD = 2
+GROUPS = [(0, 2, 0), (2, 4, 0), (0, 1, 1), (1, 2, 1), (2, 3, 1), (3, 4, 1)]
 
 
 def tile_list_league_market_features_kernel(
@@ -42,23 +38,22 @@ def tile_list_league_market_features_kernel(
     nc = tc.nc
     with ExitStack() as ctx:
         keep = ctx.enter_context(tc.tile_pool(name="keep", bufs=1))
-        ring = ctx.enter_context(tc.tile_pool(name="ring", bufs=3))
         psum = ctx.enter_context(tc.psum_pool(name="psum", bufs=1))
 
         def held(name, shape, dtype):
             return keep.tile(shape, dtype, name=name, align_bytes=64)
 
-        def zeroed(name, width, engine=nc.vector):
+        def zeroed(name, width, engine):
             plane = held(name, [P, width], U8)
             engine.memset(plane[:].bitcast(I32), 0)
             return plane
 
-        def load_packed_scales(queue, plane, scales):
+        def load_scales(plane, scales):
             passes = scales.shape[0]
             for q in range(4):
-                queue.dma_start(
-                    out=plane[32 * q : 32 * q + 4 * passes, :].bitcast(I32),
-                    in_=scales[:, 4 * q : 4 * q + 4, :].bitcast(I32),
+                nc.sync.dma_start(
+                    out=plane[32 * q : 32 * q + 4, :].rearrange("r (a c) -> r a c", a=passes).bitcast(I32),
+                    in_=scales[:, 4 * q : 4 * q + 4, :].rearrange("a r c -> r a c").bitcast(I32),
                 )
 
         def load_words(name, words_of_pass):
@@ -71,30 +66,26 @@ def tile_list_league_market_features_kernel(
             nc.sync.dma_start(tile[:], lst)
             return tile
 
-        queue_of = {"s": nc.sync, "g": nc.gpsimd, "a": nc.scalar, "v": nc.vector}
-        home_sc = zeroed("home_sc", T, queue_of[HOME_MEMSET])
-        ws_sc = zeroed("ws_sc", H)
-        away_sc = zeroed("away_sc", T, nc.gpsimd)
-        ws_sc1 = zeroed("ws_sc1", H)
-        home_sc1 = zeroed("home_sc1", S)
-        away_sc1 = zeroed("away_sc1", S)
-        stad_sc = zeroed("stad_sc", T3)
-        wo_sc = zeroed("wo_sc", N)
+        ws_sc = zeroed("ws_sc", 2 * H, nc.vector)
+        home_sc = zeroed("home_sc", 2 * T, nc.gpsimd)
+        away_sc = zeroed("away_sc", 2 * T, nc.vector)
+        stad_sc = zeroed("stad_sc", T3, nc.vector)
+        wo_sc = zeroed("wo_sc", HALVES * N, nc.vector)
 
-        home_list = load_list("home_list", offs)
-        home_w0 = load_words("home_w0", tab_words[0])
-        load_packed_scales(queue_of[HOME_Q], home_sc, tab_scales)
-        load_packed_scales(nc.sync, ws_sc, ws_scales)
         ws_w = held("ws_w", [P, 2, 2 * H], U8)
         nc.sync.dma_start(out=ws_w[:].bitcast(I32), in_=ws_words.rearrange("a p c -> p a c").bitcast(I32))
-        home_w1 = load_words("home_w1", tab_words[1])
+        home_list = load_list("home_list", offs)
+        load_scales(ws_sc, ws_scales)
+        load_scales(home_sc, tab_scales)
+        home_w0 = load_words("home_w0", tab_words[0])
         away_list = load_list("away_list", offs2)
-        load_packed_scales(queue_of[AWAY_Q], away_sc, tab2_scales)
-        away_w0 = load_words("away_w0", tab2_words[0])
+        load_scales(away_sc, tab2_scales)
+        home_w1 = load_words("home_w1", tab_words[1])
         stad_list = load_list("stad_list", offs3)
+        load_scales(stad_sc, tab3_scales)
         stad_w = held("stad_w", [P, 2 * T3], U8)
         nc.sync.dma_start(out=stad_w[:].bitcast(I32), in_=tab3_words[0].bitcast(I32))
-        load_packed_scales(nc.sync, stad_sc, tab3_scales)
+        away_w0 = load_words("away_w0", tab2_words[0])
         away_w1 = load_words("away_w1", tab2_words[1])
         wt_rows = wt.rearrange("(p j) c -> p j c", j=PACK)
         wt_raw = []
@@ -102,8 +93,11 @@ def tile_list_league_market_features_kernel(
             raw = held("wt_raw%d" % c, [P, PACK, WT_CHUNK], F32)
             nc.sync.dma_start(out=raw[:], in_=wt_rows[:, :, c * WT_CHUNK : (c + 1) * WT_CHUNK])
             wt_raw.append(raw)
+        gain = held("gain", [P, HALVES, PACK], F32)
+        nc.sync.dma_start(out=gain[:], in_=gh.rearrange("(b p t) -> p b t", b=HALVES, t=PACK))
         wo_w = held("wo_w", [P, HALVES, N], I32)
         nc.sync.dma_start(out=wo_w[:], in_=wo_words.rearrange("a p c i -> p a (c i)").bitcast(I32))
+        load_scales(wo_sc, wo_scales)
 
         def gather(name, window, lst, dtype, pieces=1):
             tile = held(name, [P, S], dtype)
@@ -115,82 +109,79 @@ def tile_list_league_market_features_kernel(
                 )
             return tile
 
-        def lower_second_pass(dst, src):
-            queue_of[SHIFT_Q].dma_start(out=dst[0:100, :].bitcast(I32), in_=src[4:104, :].bitcast(I32))
-
-        home_g0 = gather("home_g0", home_w0[:].bitcast(U32), home_list, U32)
-        ws_sc0 = held("ws_sc0", [P, H], U8)
-        nc.vector.tensor_copy(
-            out=ws_sc0[:].rearrange("p (b t m) -> p b t m", b=HALVES, t=PACK),
-            in_=ws_sc[:].rearrange("p (b m t) -> p b t m", b=HALVES, t=PACK),
-        )
-        lower_second_pass(ws_sc1, ws_sc0)
-        home_gs = gather("home_gs", home_sc[:], home_list, U8)
-        lower_second_pass(home_sc1, home_gs)
-        ws_by_slot = []
-        for a in range(2):
-            words = held("ws_by_slot%d" % a, [P, 2 * H], U8)
+        def by_slot_copy(dst, src):
             nc.vector.tensor_copy(
-                out=words[:].bitcast(U16).rearrange("p (b t m) -> p b t m", b=HALVES, t=PACK),
-                in_=ws_w[:, a, :].bitcast(U16).rearrange("p (b m t) -> p b t m", b=HALVES, t=PACK),
+                out=dst.rearrange("p (b t m) -> p b t m", t=PACK, m=P),
+                in_=src.rearrange("p (b m t) -> p b t m", t=PACK, m=P),
             )
-            ws_by_slot.append(words)
-        ws_planes = [ws_sc0, ws_sc1]
-        home_g1 = gather("home_g1", home_w1[:].bitcast(U32), home_list, U32, pieces=2)
-        away_gs = gather("away_gs", away_sc[:], away_list, U8)
-        lower_second_pass(away_sc1, away_gs)
-        gain = held("gain", [P, HALVES, PACK], F32)
-        nc.gpsimd.dma_start(out=gain[:], in_=gh.rearrange("(b p t) -> p b t", b=HALVES, t=PACK))
-        load_packed_scales(nc.gpsimd, wo_sc, wo_scales)
+
+        ws_by_slot = held("ws_by_slot", [P, 2 * 2 * H], U8)
+        by_slot_copy(ws_by_slot[:].bitcast(U16), ws_w[:].rearrange("p a c -> p (a c)").bitcast(U16))
+        ws_plane = held("ws_plane", [P, 2 * H], U8)
+        by_slot_copy(ws_plane[:], ws_sc[:])
+        home_gs = [gather("home_gs%d" % a, home_sc[:, a * T : (a + 1) * T], home_list, U8) for a in range(2)]
+        home_g = [gather("home_g0", home_w0[:].bitcast(U32), home_list, U32)]
+        away_gs = [gather("away_gs%d" % a, away_sc[:, a * T : (a + 1) * T], away_list, U8) for a in range(2)]
+        home_g.append(gather("home_g1", home_w1[:].bitcast(U32), home_list, U32, pieces=2))
 
         units = [(jt, b) for b in range(HALVES) for jt in range(JT)]
 
-        def side_pass(bank, words, scales, a, jt, b):
+        def side_product(words, scales, jt, b):
+            bank = psum.tile([P, PACK, P], F32, name="side", tag="side", bufs=6)
             cols = slice(jt * P, (jt + 1) * P)
-            for t in range(PACK):
-                c0 = b * PASS + t * P
-                nc.tensor.matmul_mx(
-                    out=bank[:, t, :],
-                    lhsT=ws_by_slot[a][:, 2 * c0 : 2 * (c0 + P)].bitcast(FP4X4),
-                    lhsT_scale=ws_planes[a][:, c0 : c0 + P],
-                    rhs=words[:, cols].bitcast(FP8X4),
-                    rhs_scale=scales[:, cols],
-                    start=(a == 0 and t == 0),
-                    stop=(a == 1 and t == PACK - 1),
-                )
+            for a in range(2):
+                for t in range(PACK):
+                    c0 = a * H + b * PASS + t * P
+                    nc.tensor.matmul_mx(
+                        out=bank[:, t, :],
+                        lhsT=ws_by_slot[:, 2 * c0 : 2 * (c0 + P)].bitcast(FP4X4),
+                        lhsT_scale=ws_plane[:, c0 : c0 + P],
+                        rhs=words[a][:, cols].bitcast(FP8X4),
+                        rhs_scale=scales[a][:, cols],
+                        start=(a == 0 and t == 0),
+                        stop=(a == 1 and t == PACK - 1),
+                    )
+            return bank
 
-        def by_slot(bank):
+        def interleaved(bank):
             return bank[:].rearrange("p t j -> p j t")
 
-        home_d = {}
-        for jt, b in units:
-            bank = psum.tile([P, PACK, P], F32, name="side", tag="side", bufs=6)
-            side_pass(bank, home_g0, home_gs, 0, jt, b)
-            side_pass(bank, home_g1, home_sc1, 1, jt, b)
-            home_d[jt, b] = held("home_d%d%d" % (jt, b), [P, P, PACK], F32)
-            nc.scalar.activation(out=home_d[jt, b][:], in_=by_slot(bank), func=ACT.Copy)
+        def stage(name, dtype):
+            return [held("%s%d" % (name, b), [P, S * PACK], dtype) for b in range(HALVES)]
 
-        away_g0 = gather("away_g0", away_w0[:].bitcast(U32), away_list, U32)
+        def markets(tile, j0, j1):
+            return tile[:, j0 * PASS : j1 * PASS].rearrange("p (j t) -> p j t", t=PACK)
+
+        home_d = stage("home_d", F32)
+        diff = stage("diff", F32)
+        gate = stage("gate", F32)
+        scaled = stage("scaled", F32)
+        squashed = stage("squashed", F32)
+        h_bf = stage("h_bf", BF16)
+
+        for jt, b in units:
+            bank = side_product(home_g, home_gs, jt, b)
+            nc.scalar.activation(out=markets(home_d[b], jt, jt + 1), in_=interleaved(bank), func=ACT.Copy)
+
         stad_gs = gather("stad_gs", stad_sc[:], stad_list, U8)
         stad_g = held("stad_g", [P, 2 * S], U8)
         nc.vector.tensor_copy(out=stad_g[:].bitcast(U16), in_=stad_w[:].bitcast(U16).indirect(stad_list[:]))
-        away_g1 = gather("away_g1", away_w1[:].bitcast(U32), away_list, U32, pieces=2)
+        away_g = [gather("away_g0", away_w0[:].bitcast(U32), away_list, U32)]
+        away_g.append(gather("away_g1", away_w1[:].bitcast(U32), away_list, U32, pieces=2))
 
         wt_bf = [held("wt_bf%d" % b, [P, PACK, P, PACK], BF16) for b in range(HALVES)]
         wt_codes = [held("wt_codes%d" % b, [P, PASS], U32) for b in range(HALVES)]
         wt_sc = [held("wt_sc%d" % b, [P, PASS], U8) for b in range(HALVES)]
         m_chunk = WT_CHUNK // PACK
 
-        def round_wt(b):
-            for h in range(PASS // WT_CHUNK):
-                dst = wt_bf[b][:, :, h * m_chunk : (h + 1) * m_chunk, :].rearrange("p t m j -> p m t j")
-                src = wt_raw[b * (PASS // WT_CHUNK) + h][:].rearrange("p j (m t) -> p m t j", t=PACK)
-                if CAST_ENGINE[b * 2 + h] == "s":
-                    nc.scalar.activation(out=dst, in_=src, func=ACT.Copy)
-                elif CAST_ENGINE[b * 2 + h] == "v":
-                    nc.vector.tensor_copy(out=dst, in_=src)
-                else:
-                    nc.gpsimd.tensor_scalar(out=dst, in0=src, scalar1=1.0, scalar2=0.0, op0=ALU.mult, op1=ALU.add)
+        def round_wt(c):
+            b, h = divmod(c, PASS // WT_CHUNK)
+            dst = wt_bf[b][:, :, h * m_chunk : (h + 1) * m_chunk, :].rearrange("p t m j -> p m t j")
+            src = wt_raw[c][:].rearrange("p j (m t) -> p m t j", t=PACK)
+            if CAST_ENGINE[c] == "s":
+                nc.scalar.activation(out=dst, in_=src, func=ACT.Copy)
+            else:
+                nc.vector.tensor_copy(out=dst, in_=src)
 
         def quantise_wt(b):
             nc.vector.quantize_mx(
@@ -198,8 +189,6 @@ def tile_list_league_market_features_kernel(
                 scales=wt_sc[b][:],
                 in_=wt_bf[b][:].rearrange("p t m j -> p (t m j)"),
             )
-
-        gate = {}
 
         def stadium(jt, b):
             bank = psum.tile([P, PACK, P], F32, name="stad", tag="stad", bufs=2)
@@ -213,90 +202,76 @@ def tile_list_league_market_features_kernel(
                     start=True,
                     stop=True,
                 )
-            gate[jt, b] = held("gate%d%d" % (jt, b), [P, P, PACK], F32)
-            nc.scalar.activation(out=gate[jt, b][:], in_=bank[:].rearrange("p t j -> p j t"), func=ACT.Tanh)
-
-        diff = {}
+            nc.scalar.activation(out=markets(gate[b], jt, jt + 1), in_=interleaved(bank), func=ACT.Tanh)
 
         def difference(jt, b):
-            bank = psum.tile([P, PACK, P], F32, name="side", tag="side", bufs=6)
-            side_pass(bank, away_g0, away_gs, 0, jt, b)
-            side_pass(bank, away_g1, away_sc1, 1, jt, b)
-            diff[jt, b] = held("diff%d%d" % (jt, b), [P, P, PACK], F32)
-            nc.vector.tensor_tensor(out=diff[jt, b][:], in0=home_d[jt, b][:], in1=by_slot(bank), op=ALU.subtract)
+            bank = side_product(away_g, away_gs, jt, b)
+            nc.vector.tensor_tensor(
+                out=markets(diff[b], jt, jt + 1), in0=markets(home_d[b], jt, jt + 1), in1=interleaved(bank),
+                op=ALU.subtract,
+            )
 
-        late = [(jt, b) for b in range(HALVES) for jt in range(JT)]
-        round_wt(0)
-        round_wt(1)
-        for i, (jt, b) in enumerate(late):
-            difference(jt, b)
-            if i == 4:
-                quantise_wt(0)
+        for c in range(H // WT_CHUNK):
+            round_wt(c)
+        quantise_wt(0)
         for jt in range(JT):
             stadium(jt, 0)
         quantise_wt(1)
+        for jt, b in units:
+            difference(jt, b)
 
-        squashed = {}
-        h_bf = {}
-        h_codes = [held("h_codes%d" % jt, [P, HALVES, P], U32) for jt in range(JT)]
-        h_sc = [held("h_sc%d" % jt, [P, HALVES, P], U8) for jt in range(JT)]
+        h_codes = [held("h_codes%d" % b, [P, S], U32) for b in range(HALVES)]
+        h_sc = [held("h_sc%d" % b, [P, S], U8) for b in range(HALVES)]
 
-        def scale_and_squash(jt, b):
-            u = ring.tile([P, P, PACK], F32, name="u", align_bytes=64)
+        def scale_and_squash(j0, j1, b):
+            cols = slice(j0 * PASS, j1 * PASS)
             nc.vector.scalar_tensor_tensor(
-                out=u[:], in0=gate[jt, b][:], scalar=1.0, in1=diff[jt, b][:],
+                out=scaled[b][:, cols], in0=gate[b][:, cols], scalar=1.0, in1=diff[b][:, cols],
                 op0=ALU.add, op1=ALU.mult,
             )
-            squashed[jt, b] = ring.tile([P, P, PACK], F32, name="squashed", align_bytes=64)
-            nc.scalar.activation(out=squashed[jt, b][:], in_=u[:], func=ACT.Tanh)
+            nc.scalar.activation(out=squashed[b][:, cols], in_=scaled[b][:, cols], func=ACT.Tanh)
 
-        def apply_gain(jt, b):
-            h_bf[jt, b] = ring.tile([P, P, PACK], BF16, name="h_bf", align_bytes=64)
-            engine = nc.gpsimd if GAIN_ENGINE[b * JT + jt] == "g" else nc.vector
-            engine.tensor_tensor(
-                out=h_bf[jt, b][:], in0=squashed[jt, b][:],
-                in1=gain[:, b : b + 1, :].to_broadcast([P, P, PACK]), op=ALU.mult,
-            )
-
-        def quantise_h(jt, b):
-            nc.vector.quantize_mx(
-                out=h_codes[jt][:, b, :].bitcast(FP8X4), scales=h_sc[jt][:, b, :],
-                in_=h_bf[jt, b][:].rearrange("p j t -> p (j t)"),
+        def apply_gain(j0, j1, b):
+            nc.vector.tensor_tensor(
+                out=markets(h_bf[b], j0, j1), in0=markets(squashed[b], j0, j1),
+                in1=gain[:, b : b + 1, :].to_broadcast([P, (j1 - j0) * P, PACK]), op=ALU.mult,
             )
 
         out_rows = out.rearrange("(nt p) j -> p nt j", p=P)
-
         out_bank = {}
 
-        def features(jt, b):
-            if b == 0:
-                out_bank[jt] = psum.tile([P, N // P, P], F32, name="side", tag="side", bufs=6)
-            bank = out_bank[jt]
-            for nt in range(N // P):
-                nc.tensor.matmul_mx(
-                    out=bank[:, nt, :],
-                    lhsT=wo_w[:, b, nt * P : (nt + 1) * P].bitcast(FP8X4),
-                    lhsT_scale=wo_sc[4 * b :, nt * P : (nt + 1) * P],
-                    rhs=h_codes[jt][:, b, :].bitcast(FP8X4),
-                    rhs_scale=h_sc[jt][:, b, :],
-                    start=(b == 0 and nt == 0),
-                    stop=(b == HALVES - 1 and nt == N // P - 1),
-                )
-            if b == HALVES - 1:
-                res = ring.tile([P, N // P, P], F32, name="res")
-                nc.scalar.copy(out=res[:], in_=bank[:])
-                nc.sync.dma_start(out=out_rows[:, :, jt * P : (jt + 1) * P], in_=res[:])
+        def features(j0, j1, b):
+            nc.vector.quantize_mx(
+                out=h_codes[b][:, j0 * P : j1 * P].bitcast(FP8X4), scales=h_sc[b][:, j0 * P : j1 * P],
+                in_=h_bf[b][:, j0 * PASS : j1 * PASS],
+            )
+            for jt in range(j0, j1):
+                cols = slice(jt * P, (jt + 1) * P)
+                if b == 0:
+                    out_bank[jt] = psum.tile([P, N // P, P], F32, name="side", tag="side", bufs=6)
+                for nt in range(N // P):
+                    nc.tensor.matmul_mx(
+                        out=out_bank[jt][:, nt, :],
+                        lhsT=wo_w[:, b, nt * P : (nt + 1) * P].bitcast(FP8X4),
+                        lhsT_scale=wo_sc[:, b * N + nt * P : b * N + (nt + 1) * P],
+                        rhs=h_codes[b][:, cols].bitcast(FP8X4),
+                        rhs_scale=h_sc[b][:, cols],
+                        start=(b == 0 and nt == 0),
+                        stop=(b == HALVES - 1 and nt == N // P - 1),
+                    )
+                if b == HALVES - 1:
+                    res = held("res%d" % jt, [P, N // P, P], F32)
+                    nc.scalar.copy(out=res[:], in_=out_bank[jt][:])
+                    nc.sync.dma_start(out=out_rows[:, :, cols], in_=res[:])
 
-        order = ORDER
-        n = len(order)
+        n = len(GROUPS)
         for i in range(n + 2):
-            if i + 2 < n and order[i + 2][1] == 1:
-                stadium(*order[i + 2])
+            if i + AHEAD < n and GROUPS[i + AHEAD][2] == 1:
+                for jt in range(GROUPS[i + AHEAD][0], GROUPS[i + AHEAD][1]):
+                    stadium(jt, 1)
             if i < n:
-                scale_and_squash(*order[i])
+                scale_and_squash(*GROUPS[i])
             if 1 <= i <= n:
-                apply_gain(*order[i - 1])
+                apply_gain(*GROUPS[i - 1])
             if i >= 2:
-                jt, b = order[i - 2]
-                quantise_h(jt, b)
-                features(jt, b)
+                features(*GROUPS[i - 2])

@@ -1,6 +1,7 @@
 from contextlib import ExitStack
 
 import concourse.mybir as mybir
+from concourse.masks import make_identity
 
 FLOPS = 3221225472
 
@@ -25,10 +26,7 @@ T3 = 1024
 H = 1024
 N = 512
 HALVES = H // PASS
-WT_CHUNK = 256
-CAST_ENGINE = "ssss"
-AHEAD = 2
-GROUPS = [(0, 2, 0), (2, 4, 0), (0, 1, 1), (1, 2, 1), (2, 3, 1), (3, 4, 1)]
+GATED_FIRST = (False, False)
 
 
 def tile_list_league_market_features_kernel(
@@ -50,10 +48,11 @@ def tile_list_league_market_features_kernel(
 
         def load_scales(plane, scales):
             passes = scales.shape[0]
-            for q in range(4):
+            by_row = scales.rearrange("a (q r) c -> r q a c", r=4)
+            for r in range(4):
                 nc.sync.dma_start(
-                    out=plane[32 * q : 32 * q + 4, :].rearrange("r (a c) -> r a c", a=passes).bitcast(I32),
-                    in_=scales[:, 4 * q : 4 * q + 4, :].rearrange("a r c -> r a c").bitcast(I32),
+                    out=plane[r:P:32, :].rearrange("q (a c) -> q a c", a=passes).bitcast(I32),
+                    in_=by_row[r].bitcast(I32),
                 )
 
         def load_words(name, words_of_pass):
@@ -66,38 +65,40 @@ def tile_list_league_market_features_kernel(
             nc.sync.dma_start(tile[:], lst)
             return tile
 
-        ws_sc = zeroed("ws_sc", 2 * H, nc.vector)
-        home_sc = zeroed("home_sc", 2 * T, nc.gpsimd)
-        away_sc = zeroed("away_sc", 2 * T, nc.vector)
-        stad_sc = zeroed("stad_sc", T3, nc.vector)
-        wo_sc = zeroed("wo_sc", HALVES * N, nc.vector)
-
-        ws_w = held("ws_w", [P, 2, 2 * H], U8)
-        nc.sync.dma_start(out=ws_w[:].bitcast(I32), in_=ws_words.rearrange("a p c -> p a c").bitcast(I32))
-        home_list = load_list("home_list", offs)
-        load_scales(ws_sc, ws_scales)
-        load_scales(home_sc, tab_scales)
-        home_w0 = load_words("home_w0", tab_words[0])
-        away_list = load_list("away_list", offs2)
-        load_scales(away_sc, tab2_scales)
-        home_w1 = load_words("home_w1", tab_words[1])
-        stad_list = load_list("stad_list", offs3)
-        load_scales(stad_sc, tab3_scales)
-        stad_w = held("stad_w", [P, 2 * T3], U8)
-        nc.sync.dma_start(out=stad_w[:].bitcast(I32), in_=tab3_words[0].bitcast(I32))
-        away_w0 = load_words("away_w0", tab2_words[0])
-        away_w1 = load_words("away_w1", tab2_words[1])
         wt_rows = wt.rearrange("(p j) c -> p j c", j=PACK)
-        wt_raw = []
-        for c in range(H // WT_CHUNK):
-            raw = held("wt_raw%d" % c, [P, PACK, WT_CHUNK], F32)
-            nc.sync.dma_start(out=raw[:], in_=wt_rows[:, :, c * WT_CHUNK : (c + 1) * WT_CHUNK])
-            wt_raw.append(raw)
-        gain = held("gain", [P, HALVES, PACK], F32)
-        nc.sync.dma_start(out=gain[:], in_=gh.rearrange("(b p t) -> p b t", b=HALVES, t=PACK))
-        wo_w = held("wo_w", [P, HALVES, N], I32)
-        nc.sync.dma_start(out=wo_w[:], in_=wo_words.rearrange("a p c i -> p a (c i)").bitcast(I32))
-        load_scales(wo_sc, wo_scales)
+
+        def load_wt(b):
+            raw = held("wt_raw%d" % b, [P, PACK, PASS], F32)
+            nc.sync.dma_start(out=raw[:], in_=wt_rows[:, :, b * PASS : (b + 1) * PASS])
+            return raw
+
+        def spread_rows(name, engine):
+            rows = held(name, [P, T], U8)
+            engine.memset(rows[32:64, :].bitcast(I32), 0)
+            engine.memset(rows[64:P, :].bitcast(I32), 0)
+            return rows
+
+        def load_spread(rows, scales):
+            nc.sync.dma_start(out=rows[0:32, :].bitcast(I32), in_=scales.rearrange("a q c -> q a c").bitcast(I32))
+
+        def place_rows(plane, picked):
+            for q in range(4):
+                nc.sync.dma_start(
+                    out=plane[32 * q : 32 * q + 4, :].bitcast(I32), in_=picked[8 * q : 8 * q + 8, :].bitcast(I32),
+                )
+            return [plane[:, a * S : (a + 1) * S] for a in range(2)]
+
+        stad_sc = zeroed("stad_sc", T3, nc.gpsimd)
+        home_sc = spread_rows("home_sc", nc.vector)
+        away_sc = spread_rows("away_sc", nc.vector)
+        ws_sc = zeroed("ws_sc", 2 * H, nc.gpsimd)
+        home_plane = zeroed("home_plane", 2 * S, nc.gpsimd)
+        away_plane = zeroed("away_plane", 2 * S, nc.gpsimd)
+        wo_sc = zeroed("wo_sc", HALVES * N, nc.gpsimd)
+        ident = held("ident", [P, P], F32)
+        make_identity(nc, ident[:])
+        warm = held("warm", [P, 1], F32)
+        nc.scalar.activation(out=warm[:], in_=ident[:, 0:1], func=ACT.Sigmoid)
 
         def gather(name, window, lst, dtype, pieces=1):
             tile = held(name, [P, S], dtype)
@@ -109,169 +110,201 @@ def tile_list_league_market_features_kernel(
                 )
             return tile
 
-        def by_slot_copy(dst, src):
-            nc.vector.tensor_copy(
-                out=dst.rearrange("p (b t m) -> p b t m", t=PACK, m=P),
-                in_=src.rearrange("p (b m t) -> p b t m", t=PACK, m=P),
-            )
-
-        ws_by_slot = held("ws_by_slot", [P, 2 * 2 * H], U8)
-        by_slot_copy(ws_by_slot[:].bitcast(U16), ws_w[:].rearrange("p a c -> p (a c)").bitcast(U16))
-        ws_plane = held("ws_plane", [P, 2 * H], U8)
-        by_slot_copy(ws_plane[:], ws_sc[:])
-        home_gs = [gather("home_gs%d" % a, home_sc[:, a * T : (a + 1) * T], home_list, U8) for a in range(2)]
-        home_g = [gather("home_g0", home_w0[:].bitcast(U32), home_list, U32)]
-        away_gs = [gather("away_gs%d" % a, away_sc[:, a * T : (a + 1) * T], away_list, U8) for a in range(2)]
-        home_g.append(gather("home_g1", home_w1[:].bitcast(U32), home_list, U32, pieces=2))
-
-        units = [(jt, b) for b in range(HALVES) for jt in range(JT)]
-
-        def side_product(words, scales, jt, b):
-            bank = psum.tile([P, PACK, P], F32, name="side", tag="side", bufs=6)
-            cols = slice(jt * P, (jt + 1) * P)
-            for a in range(2):
-                for t in range(PACK):
-                    c0 = a * H + b * PASS + t * P
-                    nc.tensor.matmul_mx(
-                        out=bank[:, t, :],
-                        lhsT=ws_by_slot[:, 2 * c0 : 2 * (c0 + P)].bitcast(FP4X4),
-                        lhsT_scale=ws_plane[:, c0 : c0 + P],
-                        rhs=words[a][:, cols].bitcast(FP8X4),
-                        rhs_scale=scales[a][:, cols],
-                        start=(a == 0 and t == 0),
-                        stop=(a == 1 and t == PACK - 1),
-                    )
-            return bank
-
-        def interleaved(bank):
-            return bank[:].rearrange("p t j -> p j t")
-
-        def stage(name, dtype):
-            return [held("%s%d" % (name, b), [P, S * PACK], dtype) for b in range(HALVES)]
-
-        def markets(tile, j0, j1):
-            return tile[:, j0 * PASS : j1 * PASS].rearrange("p (j t) -> p j t", t=PACK)
-
-        home_d = stage("home_d", F32)
-        diff = stage("diff", F32)
-        gate = stage("gate", F32)
-        scaled = stage("scaled", F32)
-        squashed = stage("squashed", F32)
-        h_bf = stage("h_bf", BF16)
-
-        for jt, b in units:
-            bank = side_product(home_g, home_gs, jt, b)
-            nc.scalar.activation(out=markets(home_d[b], jt, jt + 1), in_=interleaved(bank), func=ACT.Copy)
-
+        home_list = load_list("home_list", offs)
+        load_spread(home_sc, tab_scales)
+        wt_raw = [load_wt(0)]
+        stad_list = load_list("stad_list", offs3)
+        load_scales(stad_sc, tab3_scales)
+        stad_w = held("stad_w", [P, 2 * T3], U8)
+        nc.sync.dma_start(out=stad_w[:].bitcast(I32), in_=tab3_words[0].bitcast(I32))
+        ws_w = held("ws_w", [P, 2, 2 * H], U8)
+        nc.sync.dma_start(out=ws_w[:].bitcast(I32), in_=ws_words.rearrange("a p c -> p a c").bitcast(I32))
+        away_list = load_list("away_list", offs2)
+        load_spread(away_sc, tab2_scales)
+        home_w0 = load_words("home_w0", tab_words[0])
+        home_picked = gather("home_gs", home_sc[:], home_list, U8)
+        home_gs = place_rows(home_plane, home_picked)
         stad_gs = gather("stad_gs", stad_sc[:], stad_list, U8)
         stad_g = held("stad_g", [P, 2 * S], U8)
         nc.vector.tensor_copy(out=stad_g[:].bitcast(U16), in_=stad_w[:].bitcast(U16).indirect(stad_list[:]))
-        away_g = [gather("away_g0", away_w0[:].bitcast(U32), away_list, U32)]
-        away_g.append(gather("away_g1", away_w1[:].bitcast(U32), away_list, U32, pieces=2))
+        home_w1 = load_words("home_w1", tab_words[1])
+        load_scales(ws_sc, ws_scales)
+        away_w0 = load_words("away_w0", tab2_words[0])
+        away_gs = place_rows(away_plane, gather("away_gs", away_sc[:], away_list, U8))
+        away_w1 = load_words("away_w1", tab2_words[1])
+        wt_raw.append(load_wt(1))
+        gain = held("gain", [P, HALVES, PACK], F32)
+        nc.sync.dma_start(out=gain[:], in_=gh.rearrange("(b p t) -> p b t", b=HALVES, t=PACK))
+        wo_w = held("wo_w", [P, HALVES, N], I32)
+        nc.sync.dma_start(out=wo_w[:], in_=wo_words.rearrange("a p c i -> p a (c i)").bitcast(I32))
+        load_scales(wo_sc, wo_scales)
 
-        wt_bf = [held("wt_bf%d" % b, [P, PACK, P, PACK], BF16) for b in range(HALVES)]
+        def unit_tiles(name, dtype):
+            return {(jt, b): held("%s%d%d" % (name, jt, b), [P, PASS], dtype) for jt in range(JT) for b in range(HALVES)}
+
+        gate = unit_tiles("gate", F32)
+        home_d = unit_tiles("home_d", F32)
+        away_d = unit_tiles("away_d", F32)
+        scaled = unit_tiles("scaled", F32)
+        squashed = unit_tiles("squashed", F32)
+        h_bf = [held("h_bf%d" % b, [P, S * PACK], BF16) for b in range(HALVES)]
+        h_codes = [held("h_codes%d" % b, [P, S], U32) for b in range(HALVES)]
+        h_sc = [held("h_sc%d" % b, [P, S], U8) for b in range(HALVES)]
+
+        def mx_bank():
+            return psum.tile([P, PASS], F32, name="mx", tag="mx", bufs=4)
+
+        def by_slot(bank):
+            return bank[:].rearrange("p (m t) -> p t m", t=PACK)
+
+        def slots(tile):
+            return tile[:].rearrange("p (t m) -> p t m", t=PACK)
+
+        def by_market(bank):
+            return bank[:].rearrange("p (t j) -> p j t", t=PACK)
+
+        def markets(tile):
+            return tile.rearrange("p (j t) -> p j t", t=PACK)
+
+        wt_bf = [held("wt_bf%d" % b, [P, PASS * PACK], BF16) for b in range(HALVES)]
         wt_codes = [held("wt_codes%d" % b, [P, PASS], U32) for b in range(HALVES)]
         wt_sc = [held("wt_sc%d" % b, [P, PASS], U8) for b in range(HALVES)]
-        m_chunk = WT_CHUNK // PACK
 
-        def round_wt(c):
-            b, h = divmod(c, PASS // WT_CHUNK)
-            dst = wt_bf[b][:, :, h * m_chunk : (h + 1) * m_chunk, :].rearrange("p t m j -> p m t j")
-            src = wt_raw[c][:].rearrange("p j (m t) -> p m t j", t=PACK)
-            if CAST_ENGINE[c] == "s":
+        def round_wt(b):
+            if GATED_FIRST[b]:
+                dst = wt_bf[b][:].rearrange("p (c i j) -> p c j i", i=PACK, j=PACK)
+            else:
+                dst = wt_bf[b][:].rearrange("p (i c j) -> p c j i", i=PACK, j=PACK)
+            src = wt_raw[b][:].rearrange("p j (c i) -> p c j i", i=PACK)
+            if b == 0:
                 nc.scalar.activation(out=dst, in_=src, func=ACT.Copy)
             else:
                 nc.vector.tensor_copy(out=dst, in_=src)
 
         def quantise_wt(b):
-            nc.vector.quantize_mx(
-                out=wt_codes[b][:].bitcast(FP8X4),
-                scales=wt_sc[b][:],
-                in_=wt_bf[b][:].rearrange("p t m j -> p (t m j)"),
-            )
+            nc.vector.quantize_mx(out=wt_codes[b][:].bitcast(FP8X4), scales=wt_sc[b][:], in_=wt_bf[b][:])
 
         def stadium(jt, b):
-            bank = psum.tile([P, PACK, P], F32, name="stad", tag="stad", bufs=2)
-            for t in range(PACK):
+            bank = mx_bank()
+            codes = stad_g[:, 2 * P * jt : 2 * P * (jt + 1)].bitcast(FP4X4)
+            plane = stad_gs[:, jt * P : (jt + 1) * P]
+            if GATED_FIRST[b]:
                 nc.tensor.matmul_mx(
-                    out=bank[:, t, :],
-                    lhsT=wt_codes[b][:, t * P : (t + 1) * P].bitcast(FP8X4),
-                    lhsT_scale=wt_sc[b][:, t * P : (t + 1) * P],
-                    rhs=stad_g[:, 2 * P * jt : 2 * P * (jt + 1)].bitcast(FP4X4),
-                    rhs_scale=stad_gs[:, jt * P : (jt + 1) * P],
-                    start=True,
-                    stop=True,
+                    out=bank[:], lhsT=codes, lhsT_scale=plane,
+                    rhs=wt_codes[b][:].bitcast(FP8X4), rhs_scale=wt_sc[b][:], start=True, stop=True,
                 )
-            nc.scalar.activation(out=markets(gate[b], jt, jt + 1), in_=interleaved(bank), func=ACT.Tanh)
+                nc.scalar.activation(out=slots(gate[jt, b]), in_=by_slot(bank), func=ACT.Sigmoid, scale=2.0)
+            else:
+                for t in range(PACK):
+                    nc.tensor.matmul_mx(
+                        out=bank[:, t * P : (t + 1) * P],
+                        lhsT=wt_codes[b][:, t * P : (t + 1) * P].bitcast(FP8X4),
+                        lhsT_scale=wt_sc[b][:, t * P : (t + 1) * P],
+                        rhs=codes, rhs_scale=plane, start=True, stop=True,
+                    )
+                nc.scalar.activation(out=markets(gate[jt, b][:]), in_=by_market(bank), func=ACT.Sigmoid, scale=2.0)
 
-        def difference(jt, b):
-            bank = side_product(away_g, away_gs, jt, b)
+        def side(words, planes, sign, dst, jt, b):
+            bank = mx_bank()
+            cols = slice(jt * P, (jt + 1) * P)
+            for a in range(2):
+                nc.tensor.matmul_mx(
+                    out=bank[:],
+                    lhsT=words[a][:, cols].bitcast(FP8X4),
+                    lhsT_scale=planes[a][:, cols],
+                    rhs=ws_w[:, a, 2 * b * PASS : 2 * (b + 1) * PASS].bitcast(FP4X4),
+                    rhs_scale=ws_sc[:, a * H + b * PASS : a * H + (b + 1) * PASS],
+                    start=(a == 0),
+                    stop=(a == 1),
+                )
+            if GATED_FIRST[b]:
+                nc.vector.scalar_tensor_tensor(
+                    out=slots(dst[jt, b]), in0=by_slot(bank), scalar=sign, in1=slots(gate[jt, b]),
+                    op0=ALU.mult, op1=ALU.mult,
+                )
+            else:
+                nc.scalar.activation(out=slots(dst[jt, b]), in_=by_slot(bank), func=ACT.Copy, scale=sign)
+
+        sum_bank = {}
+
+        def turn(src, first, jt, b):
+            if first:
+                sum_bank[jt, b] = psum.tile([P, PASS], F32, name="sum", tag="sum", bufs=4)
+            for t in range(PACK):
+                nc.tensor.matmul(
+                    out=sum_bank[jt, b][:, t * P : (t + 1) * P], lhsT=src[jt, b][:, t * P : (t + 1) * P], rhs=ident[:],
+                    is_transpose=True, start=(first and t == 0), stop=(not first and t == PACK - 1),
+                )
+
+        def squash(jt, b):
+            if GATED_FIRST[b]:
+                nc.scalar.activation(out=markets(squashed[jt, b][:]), in_=by_market(sum_bank[jt, b]), func=ACT.Tanh)
+            else:
+                nc.vector.tensor_tensor(
+                    out=markets(scaled[jt, b][:]), in0=by_market(sum_bank[jt, b]), in1=markets(gate[jt, b][:]), op=ALU.mult,
+                )
+                nc.scalar.activation(out=squashed[jt, b][:], in_=scaled[jt, b][:], func=ACT.Tanh)
+
+        def apply_gain(jt, b):
             nc.vector.tensor_tensor(
-                out=markets(diff[b], jt, jt + 1), in0=markets(home_d[b], jt, jt + 1), in1=interleaved(bank),
-                op=ALU.subtract,
-            )
-
-        for c in range(H // WT_CHUNK):
-            round_wt(c)
-        quantise_wt(0)
-        for jt in range(JT):
-            stadium(jt, 0)
-        quantise_wt(1)
-        for jt, b in units:
-            difference(jt, b)
-
-        h_codes = [held("h_codes%d" % b, [P, S], U32) for b in range(HALVES)]
-        h_sc = [held("h_sc%d" % b, [P, S], U8) for b in range(HALVES)]
-
-        def scale_and_squash(j0, j1, b):
-            cols = slice(j0 * PASS, j1 * PASS)
-            nc.vector.scalar_tensor_tensor(
-                out=scaled[b][:, cols], in0=gate[b][:, cols], scalar=1.0, in1=diff[b][:, cols],
-                op0=ALU.add, op1=ALU.mult,
-            )
-            nc.scalar.activation(out=squashed[b][:, cols], in_=scaled[b][:, cols], func=ACT.Tanh)
-
-        def apply_gain(j0, j1, b):
-            nc.vector.tensor_tensor(
-                out=markets(h_bf[b], j0, j1), in0=markets(squashed[b], j0, j1),
-                in1=gain[:, b : b + 1, :].to_broadcast([P, (j1 - j0) * P, PACK]), op=ALU.mult,
+                out=markets(h_bf[b][:, jt * PASS : (jt + 1) * PASS]), in0=markets(squashed[jt, b][:]),
+                in1=gain[:, b : b + 1, :].to_broadcast([P, P, PACK]), op=ALU.mult,
             )
 
         out_rows = out.rearrange("(nt p) j -> p nt j", p=P)
-        out_bank = {}
 
-        def features(j0, j1, b):
+        def quantise_h(j0, j1, b):
             nc.vector.quantize_mx(
                 out=h_codes[b][:, j0 * P : j1 * P].bitcast(FP8X4), scales=h_sc[b][:, j0 * P : j1 * P],
                 in_=h_bf[b][:, j0 * PASS : j1 * PASS],
             )
-            for jt in range(j0, j1):
-                cols = slice(jt * P, (jt + 1) * P)
-                if b == 0:
-                    out_bank[jt] = psum.tile([P, N // P, P], F32, name="side", tag="side", bufs=6)
+
+        def features(jt):
+            bank = psum.tile([P, N // P, P], F32, name="mx", tag="mx", bufs=4)
+            for b in range(HALVES):
                 for nt in range(N // P):
                     nc.tensor.matmul_mx(
-                        out=out_bank[jt][:, nt, :],
+                        out=bank[:, nt, :],
                         lhsT=wo_w[:, b, nt * P : (nt + 1) * P].bitcast(FP8X4),
                         lhsT_scale=wo_sc[:, b * N + nt * P : b * N + (nt + 1) * P],
-                        rhs=h_codes[b][:, cols].bitcast(FP8X4),
-                        rhs_scale=h_sc[b][:, cols],
+                        rhs=h_codes[b][:, jt * P : (jt + 1) * P].bitcast(FP8X4),
+                        rhs_scale=h_sc[b][:, jt * P : (jt + 1) * P],
                         start=(b == 0 and nt == 0),
                         stop=(b == HALVES - 1 and nt == N // P - 1),
                     )
-                if b == HALVES - 1:
-                    res = held("res%d" % jt, [P, N // P, P], F32)
-                    nc.scalar.copy(out=res[:], in_=out_bank[jt][:])
-                    nc.sync.dma_start(out=out_rows[:, :, cols], in_=res[:])
+            res = held("res%d" % jt, [P, N // P, P], F32)
+            nc.scalar.copy(out=res[:], in_=bank[:])
+            nc.sync.dma_start(out=out_rows[:, :, jt * P : (jt + 1) * P], in_=res[:])
 
-        n = len(GROUPS)
-        for i in range(n + 2):
-            if i + AHEAD < n and GROUPS[i + AHEAD][2] == 1:
-                for jt in range(GROUPS[i + AHEAD][0], GROUPS[i + AHEAD][1]):
-                    stadium(jt, 1)
+        round_wt(0)
+        quantise_wt(0)
+        home_g = [gather("home_g0", home_w0[:].bitcast(U32), home_list, U32)]
+        home_g.append(gather("home_g1", home_w1[:].bitcast(U32), home_list, U32, pieces=2))
+        away_g = [gather("away_g0", away_w0[:].bitcast(U32), away_list, U32)]
+        away_g.append(gather("away_g1", away_w1[:].bitcast(U32), away_list, U32, pieces=2))
+        units = [(jt, b) for b in range(HALVES) for jt in range(JT)]
+        for jt in range(JT):
+            stadium(jt, 0)
+        for u in units:
+            side(home_g, home_gs, 2.0, home_d, *u)
+        n = len(units)
+        for i in range(n + 4):
+            if i == 1:
+                round_wt(1)
+                quantise_wt(1)
             if i < n:
-                scale_and_squash(*GROUPS[i])
+                side(away_g, away_gs, -2.0, away_d, *units[i])
+            if 2 <= i < 2 + JT:
+                stadium(i - 2, 1)
             if 1 <= i <= n:
-                apply_gain(*GROUPS[i - 1])
-            if i >= 2:
-                features(*GROUPS[i - 2])
+                turn(home_d, True, *units[i - 1])
+                turn(away_d, False, *units[i - 1])
+            if 2 <= i <= n + 1:
+                squash(*units[i - 2])
+            if 3 <= i <= n + 2:
+                apply_gain(*units[i - 3])
+            if i == JT + 3:
+                quantise_h(0, JT, 0)
+            if i >= JT + 4:
+                quantise_h(i - JT - 4, i - JT - 3, 1)
+                features(i - JT - 4)

@@ -26,7 +26,10 @@ T3 = 1024
 H = 1024
 N = 512
 HALVES = H // PASS
-GATED_FIRST = (False, False)
+SUBTRACT_ON_VECTOR = []
+ROUND_ON_VECTOR = [(0, 0), (0, 1), (1, 0), (1, 1)]
+GAIN_ON_VECTOR = [(jt, b) for jt in range(JT) for b in range(HALVES)]
+WT_PARTS = 2
 
 
 def tile_list_league_market_features_kernel(
@@ -98,7 +101,7 @@ def tile_list_league_market_features_kernel(
         ident = held("ident", [P, P], F32)
         make_identity(nc, ident[:])
         warm = held("warm", [P, 1], F32)
-        nc.scalar.activation(out=warm[:], in_=ident[:, 0:1], func=ACT.Sigmoid)
+        nc.scalar.activation(out=warm[:], in_=ident[:, 0:1], func=ACT.Tanh)
 
         def gather(name, window, lst, dtype, pieces=1):
             tile = held(name, [P, S], dtype)
@@ -110,34 +113,6 @@ def tile_list_league_market_features_kernel(
                 )
             return tile
 
-        home_list = load_list("home_list", offs)
-        load_spread(home_sc, tab_scales)
-        wt_raw = [load_wt(0)]
-        stad_list = load_list("stad_list", offs3)
-        load_scales(stad_sc, tab3_scales)
-        stad_w = held("stad_w", [P, 2 * T3], U8)
-        nc.sync.dma_start(out=stad_w[:].bitcast(I32), in_=tab3_words[0].bitcast(I32))
-        ws_w = held("ws_w", [P, 2, 2 * H], U8)
-        nc.sync.dma_start(out=ws_w[:].bitcast(I32), in_=ws_words.rearrange("a p c -> p a c").bitcast(I32))
-        away_list = load_list("away_list", offs2)
-        load_spread(away_sc, tab2_scales)
-        home_w0 = load_words("home_w0", tab_words[0])
-        home_picked = gather("home_gs", home_sc[:], home_list, U8)
-        home_gs = place_rows(home_plane, home_picked)
-        stad_gs = gather("stad_gs", stad_sc[:], stad_list, U8)
-        stad_g = held("stad_g", [P, 2 * S], U8)
-        nc.vector.tensor_copy(out=stad_g[:].bitcast(U16), in_=stad_w[:].bitcast(U16).indirect(stad_list[:]))
-        home_w1 = load_words("home_w1", tab_words[1])
-        load_scales(ws_sc, ws_scales)
-        away_w0 = load_words("away_w0", tab2_words[0])
-        away_gs = place_rows(away_plane, gather("away_gs", away_sc[:], away_list, U8))
-        away_w1 = load_words("away_w1", tab2_words[1])
-        wt_raw.append(load_wt(1))
-        gain = held("gain", [P, HALVES, PACK], F32)
-        nc.sync.dma_start(out=gain[:], in_=gh.rearrange("(b p t) -> p b t", b=HALVES, t=PACK))
-        wo_w = held("wo_w", [P, HALVES, N], I32)
-        nc.sync.dma_start(out=wo_w[:], in_=wo_words.rearrange("a p c i -> p a (c i)").bitcast(I32))
-        load_scales(wo_sc, wo_scales)
 
         def unit_tiles(name, dtype):
             return {(jt, b): held("%s%d%d" % (name, jt, b), [P, PASS], dtype) for jt in range(JT) for b in range(HALVES)}
@@ -171,15 +146,14 @@ def tile_list_league_market_features_kernel(
         wt_sc = [held("wt_sc%d" % b, [P, PASS], U8) for b in range(HALVES)]
 
         def round_wt(b):
-            if GATED_FIRST[b]:
-                dst = wt_bf[b][:].rearrange("p (c i j) -> p c j i", i=PACK, j=PACK)
-            else:
-                dst = wt_bf[b][:].rearrange("p (i c j) -> p c j i", i=PACK, j=PACK)
-            src = wt_raw[b][:].rearrange("p j (c i) -> p c j i", i=PACK)
-            if b == 0:
-                nc.scalar.activation(out=dst, in_=src, func=ACT.Copy)
-            else:
-                nc.vector.tensor_copy(out=dst, in_=src)
+            step = P // WT_PARTS
+            for h in range(WT_PARTS):
+                dst = wt_bf[b][:].rearrange("p (t m j) -> p m t j", t=PACK, j=PACK)[:, h * step : (h + 1) * step, :, :]
+                src = wt_raw[b][:].rearrange("p j (m t) -> p m t j", t=PACK)[:, h * step : (h + 1) * step, :, :]
+                if (b, h) in ROUND_ON_VECTOR:
+                    nc.vector.tensor_copy(out=dst, in_=src)
+                else:
+                    nc.scalar.activation(out=dst, in_=src, func=ACT.Copy)
 
         def quantise_wt(b):
             nc.vector.quantize_mx(out=wt_codes[b][:].bitcast(FP8X4), scales=wt_sc[b][:], in_=wt_bf[b][:])
@@ -188,23 +162,16 @@ def tile_list_league_market_features_kernel(
             bank = mx_bank()
             codes = stad_g[:, 2 * P * jt : 2 * P * (jt + 1)].bitcast(FP4X4)
             plane = stad_gs[:, jt * P : (jt + 1) * P]
-            if GATED_FIRST[b]:
+            for t in range(PACK):
                 nc.tensor.matmul_mx(
-                    out=bank[:], lhsT=codes, lhsT_scale=plane,
-                    rhs=wt_codes[b][:].bitcast(FP8X4), rhs_scale=wt_sc[b][:], start=True, stop=True,
+                    out=bank[:, t * P : (t + 1) * P],
+                    lhsT=wt_codes[b][:, t * P : (t + 1) * P].bitcast(FP8X4),
+                    lhsT_scale=wt_sc[b][:, t * P : (t + 1) * P],
+                    rhs=codes, rhs_scale=plane, start=True, stop=True,
                 )
-                nc.scalar.activation(out=slots(gate[jt, b]), in_=by_slot(bank), func=ACT.Sigmoid, scale=2.0)
-            else:
-                for t in range(PACK):
-                    nc.tensor.matmul_mx(
-                        out=bank[:, t * P : (t + 1) * P],
-                        lhsT=wt_codes[b][:, t * P : (t + 1) * P].bitcast(FP8X4),
-                        lhsT_scale=wt_sc[b][:, t * P : (t + 1) * P],
-                        rhs=codes, rhs_scale=plane, start=True, stop=True,
-                    )
-                nc.scalar.activation(out=markets(gate[jt, b][:]), in_=by_market(bank), func=ACT.Sigmoid, scale=2.0)
+            nc.scalar.activation(out=markets(gate[jt, b][:]), in_=by_market(bank), func=ACT.Tanh)
 
-        def side(words, planes, sign, dst, jt, b):
+        def side(words, planes, jt, b):
             bank = mx_bank()
             cols = slice(jt * P, (jt + 1) * P)
             for a in range(2):
@@ -217,36 +184,41 @@ def tile_list_league_market_features_kernel(
                     start=(a == 0),
                     stop=(a == 1),
                 )
-            if GATED_FIRST[b]:
-                nc.vector.scalar_tensor_tensor(
-                    out=slots(dst[jt, b]), in0=by_slot(bank), scalar=sign, in1=slots(gate[jt, b]),
-                    op0=ALU.mult, op1=ALU.mult,
-                )
+            return bank
+
+        def home(jt, b):
+            bank = side(home_g, home_gs, jt, b)
+            nc.scalar.activation(out=slots(home_d[jt, b]), in_=by_slot(bank), func=ACT.Copy)
+
+        def away(jt, b):
+            bank = side(away_g, away_gs, jt, b)
+            if (jt, b) in SUBTRACT_ON_VECTOR:
+                nc.vector.tensor_tensor(out=slots(away_d[jt, b]), in0=slots(home_d[jt, b]), in1=by_slot(bank), op=ALU.subtract)
             else:
-                nc.scalar.activation(out=slots(dst[jt, b]), in_=by_slot(bank), func=ACT.Copy, scale=sign)
+                nc.scalar.activation(out=slots(away_d[jt, b]), in_=by_slot(bank), func=ACT.Copy, scale=-1.0)
 
         sum_bank = {}
 
-        def turn(src, first, jt, b):
-            if first:
-                sum_bank[jt, b] = psum.tile([P, PASS], F32, name="sum", tag="sum", bufs=4)
-            for t in range(PACK):
-                nc.tensor.matmul(
-                    out=sum_bank[jt, b][:, t * P : (t + 1) * P], lhsT=src[jt, b][:, t * P : (t + 1) * P], rhs=ident[:],
-                    is_transpose=True, start=(first and t == 0), stop=(not first and t == PACK - 1),
-                )
+        def turn(jt, b):
+            terms = [away_d] if (jt, b) in SUBTRACT_ON_VECTOR else [home_d, away_d]
+            sum_bank[jt, b] = psum.tile([P, PASS], F32, name="sum", tag="sum", bufs=4)
+            for i, src in enumerate(terms):
+                for t in range(PACK):
+                    nc.tensor.matmul(
+                        out=sum_bank[jt, b][:, t * P : (t + 1) * P], lhsT=src[jt, b][:, t * P : (t + 1) * P], rhs=ident[:],
+                        is_transpose=True, start=(i == 0 and t == 0), stop=(i == len(terms) - 1 and t == PACK - 1),
+                    )
 
         def squash(jt, b):
-            if GATED_FIRST[b]:
-                nc.scalar.activation(out=markets(squashed[jt, b][:]), in_=by_market(sum_bank[jt, b]), func=ACT.Tanh)
-            else:
-                nc.vector.tensor_tensor(
-                    out=markets(scaled[jt, b][:]), in0=by_market(sum_bank[jt, b]), in1=markets(gate[jt, b][:]), op=ALU.mult,
-                )
-                nc.scalar.activation(out=squashed[jt, b][:], in_=scaled[jt, b][:], func=ACT.Tanh)
+            nc.vector.scalar_tensor_tensor(
+                out=markets(scaled[jt, b][:]), in0=markets(gate[jt, b][:]), scalar=1.0, in1=by_market(sum_bank[jt, b]),
+                op0=ALU.add, op1=ALU.mult,
+            )
+            nc.scalar.activation(out=squashed[jt, b][:], in_=scaled[jt, b][:], func=ACT.Tanh)
 
         def apply_gain(jt, b):
-            nc.vector.tensor_tensor(
+            engine = nc.vector if (jt, b) in GAIN_ON_VECTOR else nc.gpsimd
+            engine.tensor_tensor(
                 out=markets(h_bf[b][:, jt * PASS : (jt + 1) * PASS]), in0=markets(squashed[jt, b][:]),
                 in1=gain[:, b : b + 1, :].to_broadcast([P, P, PACK]), op=ALU.mult,
             )
@@ -260,51 +232,82 @@ def tile_list_league_market_features_kernel(
             )
 
         def features(jt):
-            bank = psum.tile([P, N // P, P], F32, name="mx", tag="mx", bufs=4)
+            parts = 2 if jt == JT - 1 else 1
+            rows = N // P // parts
+            banks = [mx_bank() for part in range(parts)]
             for b in range(HALVES):
                 for nt in range(N // P):
+                    part, k = divmod(nt, rows)
                     nc.tensor.matmul_mx(
-                        out=bank[:, nt, :],
+                        out=banks[part][:, k * P : (k + 1) * P],
                         lhsT=wo_w[:, b, nt * P : (nt + 1) * P].bitcast(FP8X4),
                         lhsT_scale=wo_sc[:, b * N + nt * P : b * N + (nt + 1) * P],
                         rhs=h_codes[b][:, jt * P : (jt + 1) * P].bitcast(FP8X4),
                         rhs_scale=h_sc[b][:, jt * P : (jt + 1) * P],
-                        start=(b == 0 and nt == 0),
-                        stop=(b == HALVES - 1 and nt == N // P - 1),
+                        start=(b == 0 and k == 0),
+                        stop=(b == HALVES - 1 and k == rows - 1),
                     )
-            res = held("res%d" % jt, [P, N // P, P], F32)
-            nc.scalar.copy(out=res[:], in_=bank[:])
-            nc.sync.dma_start(out=out_rows[:, :, jt * P : (jt + 1) * P], in_=res[:])
+            for part in range(parts):
+                res = held("res%d%d" % (jt, part), [P, rows, P], F32)
+                if part == 0:
+                    nc.scalar.copy(out=res[:], in_=banks[part][:, 0 : rows * P].rearrange("p (n j) -> p n j", j=P))
+                else:
+                    nc.vector.tensor_copy(out=res[:], in_=banks[part][:, 0 : rows * P].rearrange("p (n j) -> p n j", j=P))
+                nc.sync.dma_start(out=out_rows[:, part * rows : (part + 1) * rows, jt * P : (jt + 1) * P], in_=res[:])
 
-        round_wt(0)
-        quantise_wt(0)
+        units = [(jt, b) for b in range(HALVES) for jt in range(JT)]
+        home_list = load_list("home_list", offs)
+        load_spread(home_sc, tab_scales)
+        ws_w = held("ws_w", [P, 2, 2 * H], U8)
+        nc.sync.dma_start(out=ws_w[:].bitcast(I32), in_=ws_words.rearrange("a p c -> p a c").bitcast(I32))
+        home_w0 = load_words("home_w0", tab_words[0])
+        load_scales(ws_sc, ws_scales)
+        away_list = load_list("away_list", offs2)
+        load_spread(away_sc, tab2_scales)
+        home_w1 = load_words("home_w1", tab_words[1])
+        home_picked = gather("home_gs", home_sc[:], home_list, U8)
+        home_gs = place_rows(home_plane, home_picked)
+        stad_list = load_list("stad_list", offs3)
+        away_w0 = load_words("away_w0", tab2_words[0])
+        load_scales(stad_sc, tab3_scales)
+        stad_w = held("stad_w", [P, 2 * T3], U8)
+        nc.sync.dma_start(out=stad_w[:].bitcast(I32), in_=tab3_words[0].bitcast(I32))
+        away_w1 = load_words("away_w1", tab2_words[1])
+        away_picked = gather("away_gs", away_sc[:], away_list, U8)
+        away_gs = place_rows(away_plane, away_picked)
+        wt_raw = [load_wt(0)]
+        wt_raw.append(load_wt(1))
+        gain = held("gain", [P, HALVES, PACK], F32)
+        nc.sync.dma_start(out=gain[:], in_=gh.rearrange("(b p t) -> p b t", b=HALVES, t=PACK))
+        wo_w = held("wo_w", [P, HALVES, N], I32)
+        nc.sync.dma_start(out=wo_w[:], in_=wo_words.rearrange("a p c i -> p a (c i)").bitcast(I32))
+        load_scales(wo_sc, wo_scales)
         home_g = [gather("home_g0", home_w0[:].bitcast(U32), home_list, U32)]
-        home_g.append(gather("home_g1", home_w1[:].bitcast(U32), home_list, U32, pieces=2))
+        home_g.append(gather("home_g1", home_w1[:].bitcast(U32), home_list, U32))
+        for u in units:
+            home(*u)
+        stad_gs = gather("stad_gs", stad_sc[:], stad_list, U8)
+        stad_g = held("stad_g", [P, 2 * S], U8)
+        nc.vector.tensor_copy(out=stad_g[:].bitcast(U16), in_=stad_w[:].bitcast(U16).indirect(stad_list[:]))
         away_g = [gather("away_g0", away_w0[:].bitcast(U32), away_list, U32)]
         away_g.append(gather("away_g1", away_w1[:].bitcast(U32), away_list, U32, pieces=2))
-        units = [(jt, b) for b in range(HALVES) for jt in range(JT)]
-        for jt in range(JT):
-            stadium(jt, 0)
-        for u in units:
-            side(home_g, home_gs, 2.0, home_d, *u)
+        round_wt(0)
+        quantise_wt(0)
+        round_wt(1)
+        quantise_wt(1)
         n = len(units)
-        for i in range(n + 4):
-            if i == 1:
-                round_wt(1)
-                quantise_wt(1)
+        for i in range(n + 5):
             if i < n:
-                side(away_g, away_gs, -2.0, away_d, *units[i])
-            if 2 <= i < 2 + JT:
-                stadium(i - 2, 1)
+                away(*units[i])
             if 1 <= i <= n:
-                turn(home_d, True, *units[i - 1])
-                turn(away_d, False, *units[i - 1])
+                stadium(*units[i - 1])
+                turn(*units[i - 1])
             if 2 <= i <= n + 1:
                 squash(*units[i - 2])
             if 3 <= i <= n + 2:
                 apply_gain(*units[i - 3])
-            if i == JT + 3:
+            if i == JT + 4:
                 quantise_h(0, JT, 0)
-            if i >= JT + 4:
-                quantise_h(i - JT - 4, i - JT - 3, 1)
-                features(i - JT - 4)
+            if i >= JT + 5:
+                quantise_h(i - JT - 5, i - JT - 4, 1)
+                features(i - JT - 5)

@@ -26,9 +26,8 @@ T3 = 1024
 H = 1024
 N = 512
 HALVES = H // PASS
-SUBTRACT_ON_VECTOR = []
+SUBTRACT_ON_VECTOR = [(1, 0)]
 ROUND_ON_VECTOR = [(0, 0), (0, 1), (1, 0), (1, 1)]
-GAIN_ON_VECTOR = [(jt, b) for jt in range(JT) for b in range(HALVES)]
 WT_PARTS = 2
 
 
@@ -209,19 +208,25 @@ def tile_list_league_market_features_kernel(
                         is_transpose=True, start=(i == 0 and t == 0), stop=(i == len(terms) - 1 and t == PACK - 1),
                     )
 
+        def pieces_of(jt, b):
+            count = 2 if (jt, b) == (JT - 1, HALVES - 1) else 1
+            return [slice(i * P // count, (i + 1) * P // count) for i in range(count)]
+
         def squash(jt, b):
-            nc.vector.scalar_tensor_tensor(
-                out=markets(scaled[jt, b][:]), in0=markets(gate[jt, b][:]), scalar=1.0, in1=by_market(sum_bank[jt, b]),
-                op0=ALU.add, op1=ALU.mult,
-            )
-            nc.scalar.activation(out=squashed[jt, b][:], in_=scaled[jt, b][:], func=ACT.Tanh)
+            for js in pieces_of(jt, b):
+                nc.vector.scalar_tensor_tensor(
+                    out=markets(scaled[jt, b][:])[:, js, :], in0=markets(gate[jt, b][:])[:, js, :], scalar=1.0,
+                    in1=by_market(sum_bank[jt, b])[:, js, :], op0=ALU.add, op1=ALU.mult,
+                )
+                cols = slice(js.start * PACK, js.stop * PACK)
+                nc.scalar.activation(out=squashed[jt, b][:, cols], in_=scaled[jt, b][:, cols], func=ACT.Tanh)
 
         def apply_gain(jt, b):
-            engine = nc.vector if (jt, b) in GAIN_ON_VECTOR else nc.gpsimd
-            engine.tensor_tensor(
-                out=markets(h_bf[b][:, jt * PASS : (jt + 1) * PASS]), in0=markets(squashed[jt, b][:]),
-                in1=gain[:, b : b + 1, :].to_broadcast([P, P, PACK]), op=ALU.mult,
-            )
+            for js in pieces_of(jt, b):
+                nc.vector.tensor_tensor(
+                    out=markets(h_bf[b][:, jt * PASS : (jt + 1) * PASS])[:, js, :], in0=markets(squashed[jt, b][:])[:, js, :],
+                    in1=gain[:, b : b + 1, :].to_broadcast([P, js.stop - js.start, PACK]), op=ALU.mult,
+                )
 
         out_rows = out.rearrange("(nt p) j -> p nt j", p=P)
 
@@ -268,14 +273,14 @@ def tile_list_league_market_features_kernel(
         home_picked = gather("home_gs", home_sc[:], home_list, U8)
         home_gs = place_rows(home_plane, home_picked)
         stad_list = load_list("stad_list", offs3)
-        away_w0 = load_words("away_w0", tab2_words[0])
-        load_scales(stad_sc, tab3_scales)
         stad_w = held("stad_w", [P, 2 * T3], U8)
         nc.sync.dma_start(out=stad_w[:].bitcast(I32), in_=tab3_words[0].bitcast(I32))
+        wt_raw = [load_wt(0)]
+        load_scales(stad_sc, tab3_scales)
+        away_w0 = load_words("away_w0", tab2_words[0])
         away_w1 = load_words("away_w1", tab2_words[1])
         away_picked = gather("away_gs", away_sc[:], away_list, U8)
         away_gs = place_rows(away_plane, away_picked)
-        wt_raw = [load_wt(0)]
         wt_raw.append(load_wt(1))
         gain = held("gain", [P, HALVES, PACK], F32)
         nc.sync.dma_start(out=gain[:], in_=gh.rearrange("(b p t) -> p b t", b=HALVES, t=PACK))
@@ -283,24 +288,28 @@ def tile_list_league_market_features_kernel(
         nc.sync.dma_start(out=wo_w[:], in_=wo_words.rearrange("a p c i -> p a (c i)").bitcast(I32))
         load_scales(wo_sc, wo_scales)
         home_g = [gather("home_g0", home_w0[:].bitcast(U32), home_list, U32)]
-        home_g.append(gather("home_g1", home_w1[:].bitcast(U32), home_list, U32))
+        home_g.append(gather("home_g1", home_w1[:].bitcast(U32), home_list, U32, pieces=2))
         for u in units:
             home(*u)
-        stad_gs = gather("stad_gs", stad_sc[:], stad_list, U8)
         stad_g = held("stad_g", [P, 2 * S], U8)
         nc.vector.tensor_copy(out=stad_g[:].bitcast(U16), in_=stad_w[:].bitcast(U16).indirect(stad_list[:]))
+        round_wt(0)
+        stad_gs = gather("stad_gs", stad_sc[:], stad_list, U8)
+        quantise_wt(0)
         away_g = [gather("away_g0", away_w0[:].bitcast(U32), away_list, U32)]
         away_g.append(gather("away_g1", away_w1[:].bitcast(U32), away_list, U32, pieces=2))
-        round_wt(0)
-        quantise_wt(0)
-        round_wt(1)
-        quantise_wt(1)
+        for jt in range(JT):
+            stadium(jt, 0)
         n = len(units)
         for i in range(n + 5):
             if i < n:
                 away(*units[i])
-            if 1 <= i <= n:
+            if i == 1:
+                round_wt(1)
+                quantise_wt(1)
+            if JT < i <= n:
                 stadium(*units[i - 1])
+            if 1 <= i <= n:
                 turn(*units[i - 1])
             if 2 <= i <= n + 1:
                 squash(*units[i - 2])

@@ -17,18 +17,27 @@ ALU = mybir.AluOpType
 ACT = mybir.ActivationFunctionType
 
 P = 128
+QUAD = 32
+LIVE = 4
 PACK = 4
 PASS = P * PACK
 S = 512
 JT = S // P
 T = 2048
 T3 = 1024
+K_PASSES = 2
 H = 1024
 N = 512
 HALVES = H // PASS
-SUBTRACT_ON_VECTOR = [(1, 0)]
-ROUND_ON_VECTOR = [(0, 0), (0, 1), (1, 0), (1, 1)]
+LIST_ROWS = 16
+
+MX_BANKS = 4
+SUM_BANKS = 4
+LEAD = 3
+VECTOR_SUBTRACTS = (1, 0)
 WT_PARTS = 2
+SCALAR_ROUNDS = (1, 0)
+LAST_UNIT = (JT - 1, HALVES - 1)
 
 
 def tile_list_league_market_features_kernel(
@@ -43,27 +52,27 @@ def tile_list_league_market_features_kernel(
         def held(name, shape, dtype):
             return keep.tile(shape, dtype, name=name, align_bytes=64)
 
-        def zeroed(name, width, engine):
+        def zeroed_plane(name, width):
             plane = held(name, [P, width], U8)
-            engine.memset(plane[:].bitcast(I32), 0)
+            nc.gpsimd.memset(plane[:].bitcast(I32), 0)
             return plane
 
-        def load_scales(plane, scales):
+        def load_plane(plane, scales):
             passes = scales.shape[0]
-            by_row = scales.rearrange("a (q r) c -> r q a c", r=4)
-            for r in range(4):
+            by_row = scales.rearrange("a (q r) c -> r q a c", r=LIVE)
+            for r in range(LIVE):
                 nc.sync.dma_start(
-                    out=plane[r:P:32, :].rearrange("q (a c) -> q a c", a=passes).bitcast(I32),
+                    out=plane[r:P:QUAD, :].rearrange("q (a c) -> q a c", a=passes).bitcast(I32),
                     in_=by_row[r].bitcast(I32),
                 )
 
         def load_words(name, words_of_pass):
-            tile = held(name, [P, words_of_pass.shape[1]], I32)
+            tile = held(name, [P, T], I32)
             nc.sync.dma_start(out=tile[:], in_=words_of_pass.rearrange("p t i -> p (t i)").bitcast(I32))
             return tile
 
         def load_list(name, lst):
-            tile = keep.tile([P, S // 16], U16, name=name)
+            tile = keep.tile([P, S // LIST_ROWS], U16, name=name)
             nc.sync.dma_start(tile[:], lst)
             return tile
 
@@ -74,33 +83,33 @@ def tile_list_league_market_features_kernel(
             nc.sync.dma_start(out=raw[:], in_=wt_rows[:, :, b * PASS : (b + 1) * PASS])
             return raw
 
-        def spread_rows(name, engine):
+        def scale_rows_tile(name):
             rows = held(name, [P, T], U8)
-            engine.memset(rows[32:64, :].bitcast(I32), 0)
-            engine.memset(rows[64:P, :].bitcast(I32), 0)
+            nc.vector.memset(rows[QUAD : 2 * QUAD, :].bitcast(I32), 0)
+            nc.vector.memset(rows[2 * QUAD : P, :].bitcast(I32), 0)
             return rows
 
-        def load_spread(rows, scales):
-            nc.sync.dma_start(out=rows[0:32, :].bitcast(I32), in_=scales.rearrange("a q c -> q a c").bitcast(I32))
+        def load_scale_rows(rows, scales):
+            nc.sync.dma_start(out=rows[0:QUAD, :].bitcast(I32), in_=scales.rearrange("a q c -> q a c").bitcast(I32))
 
         def place_rows(plane, picked):
-            for q in range(4):
+            per_quad = LIVE * K_PASSES
+            for q in (0, 2, 1, 3):
                 nc.sync.dma_start(
-                    out=plane[32 * q : 32 * q + 4, :].bitcast(I32), in_=picked[8 * q : 8 * q + 8, :].bitcast(I32),
+                    out=plane[QUAD * q : QUAD * q + LIVE, :].bitcast(I32),
+                    in_=picked[per_quad * q : per_quad * (q + 1), :].bitcast(I32),
                 )
-            return [plane[:, a * S : (a + 1) * S] for a in range(2)]
+            return [plane[:, a * S : (a + 1) * S] for a in range(K_PASSES)]
 
-        stad_sc = zeroed("stad_sc", T3, nc.gpsimd)
-        home_sc = spread_rows("home_sc", nc.vector)
-        away_sc = spread_rows("away_sc", nc.vector)
-        ws_sc = zeroed("ws_sc", 2 * H, nc.gpsimd)
-        home_plane = zeroed("home_plane", 2 * S, nc.gpsimd)
-        away_plane = zeroed("away_plane", 2 * S, nc.gpsimd)
-        wo_sc = zeroed("wo_sc", HALVES * N, nc.gpsimd)
+        stad_table_plane = zeroed_plane("stad_table_plane", T3)
+        home_scale_rows = scale_rows_tile("home_scale_rows")
+        away_scale_rows = scale_rows_tile("away_scale_rows")
+        ws_plane = zeroed_plane("ws_plane", K_PASSES * H)
+        home_plane = zeroed_plane("home_plane", K_PASSES * S)
+        away_plane = zeroed_plane("away_plane", K_PASSES * S)
+        wo_plane = zeroed_plane("wo_plane", HALVES * N)
         ident = held("ident", [P, P], F32)
         make_identity(nc, ident[:])
-        warm = held("warm", [P, 1], F32)
-        nc.scalar.activation(out=warm[:], in_=ident[:, 0:1], func=ACT.Tanh)
 
         def gather(name, window, lst, dtype, pieces=1):
             tile = held(name, [P, S], dtype)
@@ -108,215 +117,225 @@ def tile_list_league_market_features_kernel(
             for i in range(pieces):
                 nc.vector.tensor_copy(
                     out=tile[:, i * step : (i + 1) * step],
-                    in_=window.indirect(lst[:, i * step // 16 : (i + 1) * step // 16]),
+                    in_=window.indirect(lst[:, i * step // LIST_ROWS : (i + 1) * step // LIST_ROWS]),
                 )
             return tile
 
+        def unit_tiles(name):
+            return {(jt, b): held("%s%d%d" % (name, jt, b), [P, PASS], F32) for jt in range(JT) for b in range(HALVES)}
 
-        def unit_tiles(name, dtype):
-            return {(jt, b): held("%s%d%d" % (name, jt, b), [P, PASS], dtype) for jt in range(JT) for b in range(HALVES)}
-
-        gate = unit_tiles("gate", F32)
-        home_d = unit_tiles("home_d", F32)
-        away_d = unit_tiles("away_d", F32)
-        scaled = unit_tiles("scaled", F32)
-        squashed = unit_tiles("squashed", F32)
+        gate = unit_tiles("gate")
+        home_term = unit_tiles("home_term")
+        away_term = unit_tiles("away_term")
+        scaled = unit_tiles("scaled")
+        squashed = unit_tiles("squashed")
         h_bf = [held("h_bf%d" % b, [P, S * PACK], BF16) for b in range(HALVES)]
         h_codes = [held("h_codes%d" % b, [P, S], U32) for b in range(HALVES)]
-        h_sc = [held("h_sc%d" % b, [P, S], U8) for b in range(HALVES)]
+        h_plane = [held("h_plane%d" % b, [P, S], U8) for b in range(HALVES)]
 
         def mx_bank():
-            return psum.tile([P, PASS], F32, name="mx", tag="mx", bufs=4)
+            return psum.tile([P, PASS], F32, name="mx", tag="mx", bufs=MX_BANKS)
 
-        def by_slot(bank):
+        def channels_by_slot(bank):
             return bank[:].rearrange("p (m t) -> p t m", t=PACK)
 
         def slots(tile):
             return tile[:].rearrange("p (t m) -> p t m", t=PACK)
 
-        def by_market(bank):
+        def slots_by_market(bank):
             return bank[:].rearrange("p (t j) -> p j t", t=PACK)
 
-        def markets(tile):
-            return tile.rearrange("p (j t) -> p j t", t=PACK)
+        def markets(view):
+            return view.rearrange("p (j t) -> p j t", t=PACK)
 
         wt_bf = [held("wt_bf%d" % b, [P, PASS * PACK], BF16) for b in range(HALVES)]
         wt_codes = [held("wt_codes%d" % b, [P, PASS], U32) for b in range(HALVES)]
-        wt_sc = [held("wt_sc%d" % b, [P, PASS], U8) for b in range(HALVES)]
+        wt_plane = [held("wt_plane%d" % b, [P, PASS], U8) for b in range(HALVES)]
 
         def round_wt(b):
             step = P // WT_PARTS
-            for h in range(WT_PARTS):
-                dst = wt_bf[b][:].rearrange("p (t m j) -> p m t j", t=PACK, j=PACK)[:, h * step : (h + 1) * step, :, :]
-                src = wt_raw[b][:].rearrange("p j (m t) -> p m t j", t=PACK)[:, h * step : (h + 1) * step, :, :]
-                if (b, h) in ROUND_ON_VECTOR:
-                    nc.vector.tensor_copy(out=dst, in_=src)
-                else:
+            for part in range(WT_PARTS):
+                ms = slice(part * step, (part + 1) * step)
+                dst = wt_bf[b][:].rearrange("p (t m j) -> p m t j", t=PACK, j=PACK)[:, ms, :, :]
+                src = wt_raw[b][:].rearrange("p j (m t) -> p m t j", t=PACK)[:, ms, :, :]
+                if (b, part) == SCALAR_ROUNDS:
                     nc.scalar.activation(out=dst, in_=src, func=ACT.Copy)
+                else:
+                    nc.vector.tensor_copy(out=dst, in_=src)
 
         def quantise_wt(b):
-            nc.vector.quantize_mx(out=wt_codes[b][:].bitcast(FP8X4), scales=wt_sc[b][:], in_=wt_bf[b][:])
+            nc.vector.quantize_mx(out=wt_codes[b][:].bitcast(FP8X4), scales=wt_plane[b][:], in_=wt_bf[b][:])
 
         def stadium(jt, b):
             bank = mx_bank()
-            codes = stad_g[:, 2 * P * jt : 2 * P * (jt + 1)].bitcast(FP4X4)
-            plane = stad_gs[:, jt * P : (jt + 1) * P]
+            codes = stad_codes[:, 2 * P * jt : 2 * P * (jt + 1)].bitcast(FP4X4)
+            plane = stad_plane[:, jt * P : (jt + 1) * P]
             for t in range(PACK):
                 nc.tensor.matmul_mx(
                     out=bank[:, t * P : (t + 1) * P],
                     lhsT=wt_codes[b][:, t * P : (t + 1) * P].bitcast(FP8X4),
-                    lhsT_scale=wt_sc[b][:, t * P : (t + 1) * P],
+                    lhsT_scale=wt_plane[b][:, t * P : (t + 1) * P],
                     rhs=codes, rhs_scale=plane, start=True, stop=True,
                 )
-            nc.scalar.activation(out=markets(gate[jt, b][:]), in_=by_market(bank), func=ACT.Tanh)
+            nc.scalar.activation(out=markets(gate[jt, b][:]), in_=slots_by_market(bank), func=ACT.Tanh)
 
-        def side(words, planes, jt, b):
+        def side_product(codes, planes, jt, b):
             bank = mx_bank()
             cols = slice(jt * P, (jt + 1) * P)
-            for a in range(2):
+            for a in range(K_PASSES):
                 nc.tensor.matmul_mx(
                     out=bank[:],
-                    lhsT=words[a][:, cols].bitcast(FP8X4),
+                    lhsT=codes[a][:, cols].bitcast(FP8X4),
                     lhsT_scale=planes[a][:, cols],
-                    rhs=ws_w[:, a, 2 * b * PASS : 2 * (b + 1) * PASS].bitcast(FP4X4),
-                    rhs_scale=ws_sc[:, a * H + b * PASS : a * H + (b + 1) * PASS],
+                    rhs=ws_codes[:, a, 2 * b * PASS : 2 * (b + 1) * PASS].bitcast(FP4X4),
+                    rhs_scale=ws_plane[:, a * H + b * PASS : a * H + (b + 1) * PASS],
                     start=(a == 0),
-                    stop=(a == 1),
+                    stop=(a == K_PASSES - 1),
                 )
             return bank
 
         def home(jt, b):
-            bank = side(home_g, home_gs, jt, b)
-            nc.scalar.activation(out=slots(home_d[jt, b]), in_=by_slot(bank), func=ACT.Copy)
+            bank = side_product(home_codes, home_planes, jt, b)
+            nc.scalar.activation(out=slots(home_term[jt, b]), in_=channels_by_slot(bank), func=ACT.Copy)
 
         def away(jt, b):
-            bank = side(away_g, away_gs, jt, b)
-            if (jt, b) in SUBTRACT_ON_VECTOR:
-                nc.vector.tensor_tensor(out=slots(away_d[jt, b]), in0=slots(home_d[jt, b]), in1=by_slot(bank), op=ALU.subtract)
+            bank = side_product(away_codes, away_planes, jt, b)
+            if (jt, b) == VECTOR_SUBTRACTS:
+                nc.vector.tensor_tensor(
+                    out=slots(away_term[jt, b]), in0=slots(home_term[jt, b]), in1=channels_by_slot(bank), op=ALU.subtract,
+                )
             else:
-                nc.scalar.activation(out=slots(away_d[jt, b]), in_=by_slot(bank), func=ACT.Copy, scale=-1.0)
+                nc.scalar.activation(out=slots(away_term[jt, b]), in_=channels_by_slot(bank), func=ACT.Copy, scale=-1.0)
 
         sum_bank = {}
 
-        def turn(jt, b):
-            terms = [away_d] if (jt, b) in SUBTRACT_ON_VECTOR else [home_d, away_d]
-            sum_bank[jt, b] = psum.tile([P, PASS], F32, name="sum", tag="sum", bufs=4)
-            for i, src in enumerate(terms):
+        def turn_and_add(jt, b):
+            terms = [away_term] if (jt, b) == VECTOR_SUBTRACTS else [home_term, away_term]
+            sum_bank[jt, b] = psum.tile([P, PASS], F32, name="sum", tag="sum", bufs=SUM_BANKS)
+            for i, term in enumerate(terms):
                 for t in range(PACK):
                     nc.tensor.matmul(
-                        out=sum_bank[jt, b][:, t * P : (t + 1) * P], lhsT=src[jt, b][:, t * P : (t + 1) * P], rhs=ident[:],
+                        out=sum_bank[jt, b][:, t * P : (t + 1) * P], lhsT=term[jt, b][:, t * P : (t + 1) * P], rhs=ident[:],
                         is_transpose=True, start=(i == 0 and t == 0), stop=(i == len(terms) - 1 and t == PACK - 1),
                     )
 
-        def pieces_of(jt, b):
-            count = 2 if (jt, b) == (JT - 1, HALVES - 1) else 1
+        def market_ranges(jt, b):
+            count = 2 if (jt, b) == LAST_UNIT else 1
             return [slice(i * P // count, (i + 1) * P // count) for i in range(count)]
 
-        def squash(jt, b):
-            for js in pieces_of(jt, b):
+        def scale_and_squash(jt, b):
+            for js in market_ranges(jt, b):
                 nc.vector.scalar_tensor_tensor(
                     out=markets(scaled[jt, b][:])[:, js, :], in0=markets(gate[jt, b][:])[:, js, :], scalar=1.0,
-                    in1=by_market(sum_bank[jt, b])[:, js, :], op0=ALU.add, op1=ALU.mult,
+                    in1=slots_by_market(sum_bank[jt, b])[:, js, :], op0=ALU.add, op1=ALU.mult,
                 )
                 cols = slice(js.start * PACK, js.stop * PACK)
                 nc.scalar.activation(out=squashed[jt, b][:, cols], in_=scaled[jt, b][:, cols], func=ACT.Tanh)
 
         def apply_gain(jt, b):
-            for js in pieces_of(jt, b):
+            for js in market_ranges(jt, b):
                 nc.vector.tensor_tensor(
-                    out=markets(h_bf[b][:, jt * PASS : (jt + 1) * PASS])[:, js, :], in0=markets(squashed[jt, b][:])[:, js, :],
+                    out=markets(h_bf[b][:, jt * PASS : (jt + 1) * PASS])[:, js, :],
+                    in0=markets(squashed[jt, b][:])[:, js, :],
                     in1=gain[:, b : b + 1, :].to_broadcast([P, js.stop - js.start, PACK]), op=ALU.mult,
                 )
 
-        out_rows = out.rearrange("(nt p) j -> p nt j", p=P)
-
-        def quantise_h(j0, j1, b):
+        def quantise_h(jt, b):
             nc.vector.quantize_mx(
-                out=h_codes[b][:, j0 * P : j1 * P].bitcast(FP8X4), scales=h_sc[b][:, j0 * P : j1 * P],
-                in_=h_bf[b][:, j0 * PASS : j1 * PASS],
+                out=h_codes[b][:, jt * P : (jt + 1) * P].bitcast(FP8X4), scales=h_plane[b][:, jt * P : (jt + 1) * P],
+                in_=h_bf[b][:, jt * PASS : (jt + 1) * PASS],
             )
+
+        out_rows = out.rearrange("(nt p) j -> p nt j", p=P)
 
         def features(jt):
             parts = 2 if jt == JT - 1 else 1
-            rows = N // P // parts
+            tiles = N // P // parts
             banks = [mx_bank() for part in range(parts)]
             for b in range(HALVES):
                 for nt in range(N // P):
-                    part, k = divmod(nt, rows)
+                    part, place = divmod(nt, tiles)
                     nc.tensor.matmul_mx(
-                        out=banks[part][:, k * P : (k + 1) * P],
-                        lhsT=wo_w[:, b, nt * P : (nt + 1) * P].bitcast(FP8X4),
-                        lhsT_scale=wo_sc[:, b * N + nt * P : b * N + (nt + 1) * P],
+                        out=banks[part][:, place * P : (place + 1) * P],
+                        lhsT=wo_codes[:, b, nt * P : (nt + 1) * P].bitcast(FP8X4),
+                        lhsT_scale=wo_plane[:, b * N + nt * P : b * N + (nt + 1) * P],
                         rhs=h_codes[b][:, jt * P : (jt + 1) * P].bitcast(FP8X4),
-                        rhs_scale=h_sc[b][:, jt * P : (jt + 1) * P],
-                        start=(b == 0 and k == 0),
-                        stop=(b == HALVES - 1 and k == rows - 1),
+                        rhs_scale=h_plane[b][:, jt * P : (jt + 1) * P],
+                        start=(b == 0 and place == 0),
+                        stop=(b == HALVES - 1 and place == tiles - 1),
                     )
             for part in range(parts):
-                res = held("res%d%d" % (jt, part), [P, rows, P], F32)
+                res = held("res%d%d" % (jt, part), [P, tiles, P], F32)
+                sums = banks[part][:, 0 : tiles * P].rearrange("p (n j) -> p n j", j=P)
                 if part == 0:
-                    nc.scalar.copy(out=res[:], in_=banks[part][:, 0 : rows * P].rearrange("p (n j) -> p n j", j=P))
+                    nc.scalar.copy(out=res[:], in_=sums)
                 else:
-                    nc.vector.tensor_copy(out=res[:], in_=banks[part][:, 0 : rows * P].rearrange("p (n j) -> p n j", j=P))
-                nc.sync.dma_start(out=out_rows[:, part * rows : (part + 1) * rows, jt * P : (jt + 1) * P], in_=res[:])
+                    nc.vector.tensor_copy(out=res[:], in_=sums)
+                nc.sync.dma_start(out=out_rows[:, part * tiles : (part + 1) * tiles, jt * P : (jt + 1) * P], in_=res[:])
 
-        units = [(jt, b) for b in range(HALVES) for jt in range(JT)]
         home_list = load_list("home_list", offs)
-        load_spread(home_sc, tab_scales)
-        ws_w = held("ws_w", [P, 2, 2 * H], U8)
-        nc.sync.dma_start(out=ws_w[:].bitcast(I32), in_=ws_words.rearrange("a p c -> p a c").bitcast(I32))
-        home_w0 = load_words("home_w0", tab_words[0])
-        load_scales(ws_sc, ws_scales)
+        load_scale_rows(home_scale_rows, tab_scales)
+        ws_codes = held("ws_codes", [P, K_PASSES, 2 * H], U8)
+        nc.sync.dma_start(out=ws_codes[:].bitcast(I32), in_=ws_words.rearrange("a p c -> p a c").bitcast(I32))
+        home_table0 = load_words("home_table0", tab_words[0])
+        load_plane(ws_plane, ws_scales)
         away_list = load_list("away_list", offs2)
-        load_spread(away_sc, tab2_scales)
-        home_w1 = load_words("home_w1", tab_words[1])
-        home_picked = gather("home_gs", home_sc[:], home_list, U8)
-        home_gs = place_rows(home_plane, home_picked)
+        load_scale_rows(away_scale_rows, tab2_scales)
+        home_table1 = load_words("home_table1", tab_words[1])
+        home_planes = place_rows(home_plane, gather("home_picked_rows", home_scale_rows[:], home_list, U8))
         stad_list = load_list("stad_list", offs3)
-        stad_w = held("stad_w", [P, 2 * T3], U8)
-        nc.sync.dma_start(out=stad_w[:].bitcast(I32), in_=tab3_words[0].bitcast(I32))
+        stad_table = held("stad_table", [P, 2 * T3], U8)
+        nc.sync.dma_start(out=stad_table[:].bitcast(I32), in_=tab3_words[0].bitcast(I32))
         wt_raw = [load_wt(0)]
-        load_scales(stad_sc, tab3_scales)
-        away_w0 = load_words("away_w0", tab2_words[0])
-        away_w1 = load_words("away_w1", tab2_words[1])
-        away_picked = gather("away_gs", away_sc[:], away_list, U8)
-        away_gs = place_rows(away_plane, away_picked)
+        load_plane(stad_table_plane, tab3_scales)
+        away_table0 = load_words("away_table0", tab2_words[0])
+        away_table1 = load_words("away_table1", tab2_words[1])
+        away_planes = place_rows(away_plane, gather("away_picked_rows", away_scale_rows[:], away_list, U8))
         wt_raw.append(load_wt(1))
         gain = held("gain", [P, HALVES, PACK], F32)
         nc.sync.dma_start(out=gain[:], in_=gh.rearrange("(b p t) -> p b t", b=HALVES, t=PACK))
-        wo_w = held("wo_w", [P, HALVES, N], I32)
-        nc.sync.dma_start(out=wo_w[:], in_=wo_words.rearrange("a p c i -> p a (c i)").bitcast(I32))
-        load_scales(wo_sc, wo_scales)
-        home_g = [gather("home_g0", home_w0[:].bitcast(U32), home_list, U32)]
-        home_g.append(gather("home_g1", home_w1[:].bitcast(U32), home_list, U32, pieces=2))
-        for u in units:
-            home(*u)
-        stad_g = held("stad_g", [P, 2 * S], U8)
-        nc.vector.tensor_copy(out=stad_g[:].bitcast(U16), in_=stad_w[:].bitcast(U16).indirect(stad_list[:]))
+        wo_codes = held("wo_codes", [P, HALVES, N], I32)
+        nc.sync.dma_start(out=wo_codes[:], in_=wo_words.rearrange("a p c i -> p a (c i)").bitcast(I32))
+        load_plane(wo_plane, wo_scales)
+
+        home_codes = [gather("home_codes0", home_table0[:].bitcast(U32), home_list, U32)]
+        home_codes.append(gather("home_codes1", home_table1[:].bitcast(U32), home_list, U32, pieces=2))
+        for b in range(HALVES):
+            for jt in range(JT):
+                home(jt, b)
+        stad_codes = held("stad_codes", [P, 2 * S], U8)
+        nc.vector.tensor_copy(out=stad_codes[:].bitcast(U16), in_=stad_table[:].bitcast(U16).indirect(stad_list[:]))
         round_wt(0)
-        stad_gs = gather("stad_gs", stad_sc[:], stad_list, U8)
+        stad_plane = gather("stad_plane", stad_table_plane[:], stad_list, U8)
         quantise_wt(0)
-        away_g = [gather("away_g0", away_w0[:].bitcast(U32), away_list, U32)]
-        away_g.append(gather("away_g1", away_w1[:].bitcast(U32), away_list, U32, pieces=2))
+        away_codes = [gather("away_codes0", away_table0[:].bitcast(U32), away_list, U32)]
+        away_codes.append(gather("away_codes1", away_table1[:].bitcast(U32), away_list, U32, pieces=2))
         for jt in range(JT):
             stadium(jt, 0)
-        n = len(units)
-        for i in range(n + 5):
+
+        order = [(jt, 0) for jt in range(LEAD)]
+        for jt in range(JT):
+            order.append((jt, 1))
+            if jt + LEAD < JT:
+                order.append((jt + LEAD, 0))
+
+        n = len(order)
+        for i in range(n + 4):
             if i < n:
-                away(*units[i])
+                away(*order[i])
             if i == 1:
                 round_wt(1)
                 quantise_wt(1)
-            if JT < i <= n:
-                stadium(*units[i - 1])
             if 1 <= i <= n:
-                turn(*units[i - 1])
+                if order[i - 1][1] == 1:
+                    stadium(*order[i - 1])
+                turn_and_add(*order[i - 1])
             if 2 <= i <= n + 1:
-                squash(*units[i - 2])
+                scale_and_squash(*order[i - 2])
             if 3 <= i <= n + 2:
-                apply_gain(*units[i - 3])
-            if i == JT + 4:
-                quantise_h(0, JT, 0)
-            if i >= JT + 5:
-                quantise_h(i - JT - 5, i - JT - 4, 1)
-                features(i - JT - 5)
+                apply_gain(*order[i - 3])
+            if i >= 4:
+                jt, b = order[i - 4]
+                quantise_h(jt, b)
+                if b == HALVES - 1:
+                    features(jt)

@@ -37,7 +37,14 @@ LEAD = 3
 VECTOR_SUBTRACTS = (1, 0)
 WT_PARTS = 2
 SCALAR_ROUNDS = (1, 0)
+VECTOR_EMPTIES = ()
+WARM_UPS = 2
 LAST_UNIT = (JT - 1, HALVES - 1)
+SHARED_AT = {
+    "home_table0": 0, "away_picked_rows": 0, "away_table0": 512,
+    "home_table1": 16384, "away_table1": 9216, "gain": 18432,
+    "wt_raw0": 24576, "wt_raw1": 24576, "wt_bf0": 32768, "wo_codes": 32768,
+}
 
 
 def tile_list_league_market_features_kernel(
@@ -47,9 +54,12 @@ def tile_list_league_market_features_kernel(
     nc = tc.nc
     with ExitStack() as ctx:
         keep = ctx.enter_context(tc.tile_pool(name="keep", bufs=1))
+        reuse = ctx.enter_context(tc.tile_pool(name="reuse", bufs=1))
         psum = ctx.enter_context(tc.psum_pool(name="psum", bufs=1))
 
         def held(name, shape, dtype):
+            if name in SHARED_AT:
+                return reuse.tile(shape, dtype, name=name, align_bytes=64, offset=SHARED_AT[name])
             return keep.tile(shape, dtype, name=name, align_bytes=64)
 
         def zeroed_plane(name, width):
@@ -107,7 +117,6 @@ def tile_list_league_market_features_kernel(
         ws_plane = zeroed_plane("ws_plane", K_PASSES * H)
         home_plane = zeroed_plane("home_plane", K_PASSES * S)
         away_plane = zeroed_plane("away_plane", K_PASSES * S)
-        wo_plane = zeroed_plane("wo_plane", HALVES * N)
         ident = held("ident", [P, P], F32)
         make_identity(nc, ident[:])
 
@@ -196,7 +205,10 @@ def tile_list_league_market_features_kernel(
 
         def home(jt, b):
             bank = side_product(home_codes, home_planes, jt, b)
-            nc.scalar.activation(out=slots(home_term[jt, b]), in_=channels_by_slot(bank), func=ACT.Copy)
+            if (jt, b) in VECTOR_EMPTIES:
+                nc.vector.tensor_copy(out=slots(home_term[jt, b]), in_=channels_by_slot(bank))
+            else:
+                nc.scalar.activation(out=slots(home_term[jt, b]), in_=channels_by_slot(bank), func=ACT.Copy)
 
         def away(jt, b):
             bank = side_product(away_codes, away_planes, jt, b)
@@ -211,6 +223,8 @@ def tile_list_league_market_features_kernel(
 
         def turn_and_add(jt, b):
             terms = [away_term] if (jt, b) == VECTOR_SUBTRACTS else [home_term, away_term]
+            if len(sum_bank) >= SUM_BANKS:
+                terms.reverse()
             sum_bank[jt, b] = psum.tile([P, PASS], F32, name="sum", tag="sum", bufs=SUM_BANKS)
             for i, term in enumerate(terms):
                 for t in range(PACK):
@@ -275,43 +289,50 @@ def tile_list_league_market_features_kernel(
 
         home_list = load_list("home_list", offs)
         load_scale_rows(home_scale_rows, tab_scales)
+        stad_list = load_list("stad_list", offs3)
+        stad_table = held("stad_table", [P, 2 * T3], U8)
+        nc.sync.dma_start(out=stad_table[:].bitcast(I32), in_=tab3_words[0].bitcast(I32))
         ws_codes = held("ws_codes", [P, K_PASSES, 2 * H], U8)
         nc.sync.dma_start(out=ws_codes[:].bitcast(I32), in_=ws_words.rearrange("a p c -> p a c").bitcast(I32))
+        load_plane(stad_table_plane, tab3_scales)
         home_table0 = load_words("home_table0", tab_words[0])
         load_plane(ws_plane, ws_scales)
         away_list = load_list("away_list", offs2)
         load_scale_rows(away_scale_rows, tab2_scales)
         home_table1 = load_words("home_table1", tab_words[1])
         home_planes = place_rows(home_plane, gather("home_picked_rows", home_scale_rows[:], home_list, U8))
-        stad_list = load_list("stad_list", offs3)
-        stad_table = held("stad_table", [P, 2 * T3], U8)
-        nc.sync.dma_start(out=stad_table[:].bitcast(I32), in_=tab3_words[0].bitcast(I32))
+        stad_codes = held("stad_codes", [P, 2 * S], U8)
+        nc.vector.tensor_copy(out=stad_codes[:].bitcast(U16), in_=stad_table[:].bitcast(U16).indirect(stad_list[:]))
+        stad_plane = gather("stad_plane", stad_table_plane[:], stad_list, U8)
         wt_raw = [load_wt(0)]
-        load_plane(stad_table_plane, tab3_scales)
+        home_codes = [gather("home_codes0", home_table0[:].bitcast(U32), home_list, U32)]
+        idle_bank = psum.tile([P, PASS], F32, name="sum", tag="sum", bufs=SUM_BANKS)
+        for i in range(WARM_UPS):
+            nc.tensor.matmul_mx(
+                out=idle_bank[:], lhsT=home_codes[0][:, 0:P].bitcast(FP8X4), lhsT_scale=ws_plane[:, 0:P],
+                rhs=ws_codes[:, 0, 0 : 2 * PASS].bitcast(FP4X4), rhs_scale=ws_plane[:, 0:PASS], start=True, stop=True,
+            )
+        away_picked = gather("away_picked_rows", away_scale_rows[:], away_list, U8)
         away_table0 = load_words("away_table0", tab2_words[0])
+        home_codes.append(gather("home_codes1", home_table1[:].bitcast(U32), home_list, U32, pieces=2))
         away_table1 = load_words("away_table1", tab2_words[1])
-        away_planes = place_rows(away_plane, gather("away_picked_rows", away_scale_rows[:], away_list, U8))
+        away_planes = place_rows(away_plane, away_picked)
+        for b in range(HALVES):
+            for jt in range(JT):
+                home(jt, b)
+        round_wt(0)
         wt_raw.append(load_wt(1))
+        quantise_wt(0)
         gain = held("gain", [P, HALVES, PACK], F32)
         nc.sync.dma_start(out=gain[:], in_=gh.rearrange("(b p t) -> p b t", b=HALVES, t=PACK))
         wo_codes = held("wo_codes", [P, HALVES, N], I32)
         nc.sync.dma_start(out=wo_codes[:], in_=wo_words.rearrange("a p c i -> p a (c i)").bitcast(I32))
+        wo_plane = zeroed_plane("wo_plane", HALVES * N)
         load_plane(wo_plane, wo_scales)
-
-        home_codes = [gather("home_codes0", home_table0[:].bitcast(U32), home_list, U32)]
-        home_codes.append(gather("home_codes1", home_table1[:].bitcast(U32), home_list, U32, pieces=2))
-        for b in range(HALVES):
-            for jt in range(JT):
-                home(jt, b)
-        stad_codes = held("stad_codes", [P, 2 * S], U8)
-        nc.vector.tensor_copy(out=stad_codes[:].bitcast(U16), in_=stad_table[:].bitcast(U16).indirect(stad_list[:]))
-        round_wt(0)
-        stad_plane = gather("stad_plane", stad_table_plane[:], stad_list, U8)
-        quantise_wt(0)
-        away_codes = [gather("away_codes0", away_table0[:].bitcast(U32), away_list, U32)]
-        away_codes.append(gather("away_codes1", away_table1[:].bitcast(U32), away_list, U32, pieces=2))
         for jt in range(JT):
             stadium(jt, 0)
+        away_codes = [gather("away_codes0", away_table0[:].bitcast(U32), away_list, U32)]
+        away_codes.append(gather("away_codes1", away_table1[:].bitcast(U32), away_list, U32, pieces=2))
 
         order = [(jt, 0) for jt in range(LEAD)]
         for jt in range(JT):

@@ -34,16 +34,15 @@ LIST_ROWS = 16
 MX_BANKS = 4
 SUM_BANKS = 4
 LEAD = 3
-VECTOR_SUBTRACTS = (1, 0)
+VECTOR_SUBTRACTS = ((0, 0), (1, 0))
 WT_PARTS = 2
-SCALAR_ROUNDS = (1, 0)
 VECTOR_EMPTIES = ()
-WARM_UPS = 2
 LAST_UNIT = (JT - 1, HALVES - 1)
 SHARED_AT = {
-    "home_table0": 0, "away_picked_rows": 0, "away_table0": 512,
-    "home_table1": 16384, "away_table1": 9216, "gain": 18432,
-    "wt_raw0": 24576, "wt_raw1": 24576, "wt_bf0": 32768, "wo_codes": 32768,
+    "home_table0": 0, "away_table0": 512,
+    "home_table1": 16384, "away_table1": 9216, "gain": 18432, "stad_plane": 18496,
+    "home_scale_rows": 24512,
+    "wt_raw0": 26624, "wt_raw1": 26624, "wt_bf0": 34816, "wo_codes": 34816,
 }
 
 
@@ -111,11 +110,11 @@ def tile_list_league_market_features_kernel(
                 )
             return [plane[:, a * S : (a + 1) * S] for a in range(K_PASSES)]
 
-        stad_table_plane = zeroed_plane("stad_table_plane", T3)
+        ws_plane = zeroed_plane("ws_plane", K_PASSES * H)
         home_scale_rows = scale_rows_tile("home_scale_rows")
         away_scale_rows = scale_rows_tile("away_scale_rows")
-        ws_plane = zeroed_plane("ws_plane", K_PASSES * H)
         home_plane = zeroed_plane("home_plane", K_PASSES * S)
+        stad_table_plane = zeroed_plane("stad_table_plane", T3)
         away_plane = zeroed_plane("away_plane", K_PASSES * S)
         ident = held("ident", [P, P], F32)
         make_identity(nc, ident[:])
@@ -167,8 +166,10 @@ def tile_list_league_market_features_kernel(
                 ms = slice(part * step, (part + 1) * step)
                 dst = wt_bf[b][:].rearrange("p (t m j) -> p m t j", t=PACK, j=PACK)[:, ms, :, :]
                 src = wt_raw[b][:].rearrange("p j (m t) -> p m t j", t=PACK)[:, ms, :, :]
-                if (b, part) == SCALAR_ROUNDS:
+                if (b, part) == (1, 0):
                     nc.scalar.activation(out=dst, in_=src, func=ACT.Copy)
+                elif b == 1:
+                    nc.gpsimd.tensor_scalar(out=dst, in0=src, scalar1=1.0, scalar2=0.0, op0=ALU.mult, op1=ALU.add)
                 else:
                     nc.vector.tensor_copy(out=dst, in_=src)
 
@@ -188,8 +189,10 @@ def tile_list_league_market_features_kernel(
                 )
             nc.scalar.activation(out=markets(gate[jt, b][:]), in_=slots_by_market(bank), func=ACT.Tanh)
 
-        def side_product(codes, planes, jt, b):
-            bank = mx_bank()
+        def sum_tile():
+            return psum.tile([P, PASS], F32, name="sum", tag="sum", bufs=SUM_BANKS)
+
+        def side_product(codes, planes, jt, b, bank):
             cols = slice(jt * P, (jt + 1) * P)
             for a in range(K_PASSES):
                 nc.tensor.matmul_mx(
@@ -204,15 +207,15 @@ def tile_list_league_market_features_kernel(
             return bank
 
         def home(jt, b):
-            bank = side_product(home_codes, home_planes, jt, b)
+            bank = side_product(home_codes, home_planes, jt, b, mx_bank())
             if (jt, b) in VECTOR_EMPTIES:
                 nc.vector.tensor_copy(out=slots(home_term[jt, b]), in_=channels_by_slot(bank))
             else:
                 nc.scalar.activation(out=slots(home_term[jt, b]), in_=channels_by_slot(bank), func=ACT.Copy)
 
         def away(jt, b):
-            bank = side_product(away_codes, away_planes, jt, b)
-            if (jt, b) == VECTOR_SUBTRACTS:
+            bank = side_product(away_codes, away_planes, jt, b, mx_bank())
+            if (jt, b) in VECTOR_SUBTRACTS:
                 nc.vector.tensor_tensor(
                     out=slots(away_term[jt, b]), in0=slots(home_term[jt, b]), in1=channels_by_slot(bank), op=ALU.subtract,
                 )
@@ -221,17 +224,27 @@ def tile_list_league_market_features_kernel(
 
         sum_bank = {}
 
+        def turn(term, jt, b, first, last):
+            for t in range(PACK):
+                nc.tensor.matmul(
+                    out=sum_bank[jt, b][:, t * P : (t + 1) * P], lhsT=term[jt, b][:, t * P : (t + 1) * P], rhs=ident[:],
+                    is_transpose=True, start=(first and t == 0), stop=(last and t == PACK - 1),
+                )
+
+        def open_sum(jt, b):
+            sum_bank[jt, b] = sum_tile()
+
         def turn_and_add(jt, b):
-            terms = [away_term] if (jt, b) == VECTOR_SUBTRACTS else [home_term, away_term]
-            if len(sum_bank) >= SUM_BANKS:
-                terms.reverse()
-            sum_bank[jt, b] = psum.tile([P, PASS], F32, name="sum", tag="sum", bufs=SUM_BANKS)
-            for i, term in enumerate(terms):
-                for t in range(PACK):
-                    nc.tensor.matmul(
-                        out=sum_bank[jt, b][:, t * P : (t + 1) * P], lhsT=term[jt, b][:, t * P : (t + 1) * P], rhs=ident[:],
-                        is_transpose=True, start=(i == 0 and t == 0), stop=(i == len(terms) - 1 and t == PACK - 1),
-                    )
+            if (jt, b) in VECTOR_SUBTRACTS:
+                if (jt, b) not in sum_bank:
+                    open_sum(jt, b)
+                turn(away_term, jt, b, True, True)
+            elif (jt, b) in sum_bank:
+                turn(away_term, jt, b, False, True)
+            else:
+                open_sum(jt, b)
+                turn(away_term, jt, b, True, False)
+                turn(home_term, jt, b, False, True)
 
         def market_ranges(jt, b):
             count = 2 if (jt, b) == LAST_UNIT else 1
@@ -289,33 +302,27 @@ def tile_list_league_market_features_kernel(
 
         home_list = load_list("home_list", offs)
         load_scale_rows(home_scale_rows, tab_scales)
-        stad_list = load_list("stad_list", offs3)
-        stad_table = held("stad_table", [P, 2 * T3], U8)
-        nc.sync.dma_start(out=stad_table[:].bitcast(I32), in_=tab3_words[0].bitcast(I32))
         ws_codes = held("ws_codes", [P, K_PASSES, 2 * H], U8)
         nc.sync.dma_start(out=ws_codes[:].bitcast(I32), in_=ws_words.rearrange("a p c -> p a c").bitcast(I32))
-        load_plane(stad_table_plane, tab3_scales)
-        home_table0 = load_words("home_table0", tab_words[0])
-        load_plane(ws_plane, ws_scales)
         away_list = load_list("away_list", offs2)
         load_scale_rows(away_scale_rows, tab2_scales)
-        home_table1 = load_words("home_table1", tab_words[1])
+        load_plane(ws_plane, ws_scales)
+        home_table0 = load_words("home_table0", tab_words[0])
+        stad_table = held("stad_table", [P, 2 * T3], U8)
+        nc.sync.dma_start(out=stad_table[:].bitcast(I32), in_=tab3_words[0].bitcast(I32))
+        stad_list = load_list("stad_list", offs3)
         home_planes = place_rows(home_plane, gather("home_picked_rows", home_scale_rows[:], home_list, U8))
+        home_table1 = load_words("home_table1", tab_words[1])
+        away_picked = gather("away_picked_rows", away_scale_rows[:], away_list, U8)
+        load_plane(stad_table_plane, tab3_scales)
+        wt_raw = [load_wt(0)]
+        home_codes = [gather("home_codes0", home_table0[:].bitcast(U32), home_list, U32, pieces=2)]
+        away_table0 = load_words("away_table0", tab2_words[0])
         stad_codes = held("stad_codes", [P, 2 * S], U8)
         nc.vector.tensor_copy(out=stad_codes[:].bitcast(U16), in_=stad_table[:].bitcast(U16).indirect(stad_list[:]))
-        stad_plane = gather("stad_plane", stad_table_plane[:], stad_list, U8)
-        wt_raw = [load_wt(0)]
-        home_codes = [gather("home_codes0", home_table0[:].bitcast(U32), home_list, U32)]
-        idle_bank = psum.tile([P, PASS], F32, name="sum", tag="sum", bufs=SUM_BANKS)
-        for i in range(WARM_UPS):
-            nc.tensor.matmul_mx(
-                out=idle_bank[:], lhsT=home_codes[0][:, 0:P].bitcast(FP8X4), lhsT_scale=ws_plane[:, 0:P],
-                rhs=ws_codes[:, 0, 0 : 2 * PASS].bitcast(FP4X4), rhs_scale=ws_plane[:, 0:PASS], start=True, stop=True,
-            )
-        away_picked = gather("away_picked_rows", away_scale_rows[:], away_list, U8)
-        away_table0 = load_words("away_table0", tab2_words[0])
         home_codes.append(gather("home_codes1", home_table1[:].bitcast(U32), home_list, U32, pieces=2))
         away_table1 = load_words("away_table1", tab2_words[1])
+        stad_plane = gather("stad_plane", stad_table_plane[:], stad_list, U8)
         away_planes = place_rows(away_plane, away_picked)
         for b in range(HALVES):
             for jt in range(JT):
@@ -331,8 +338,6 @@ def tile_list_league_market_features_kernel(
         load_plane(wo_plane, wo_scales)
         for jt in range(JT):
             stadium(jt, 0)
-        away_codes = [gather("away_codes0", away_table0[:].bitcast(U32), away_list, U32)]
-        away_codes.append(gather("away_codes1", away_table1[:].bitcast(U32), away_list, U32, pieces=2))
 
         order = [(jt, 0) for jt in range(LEAD)]
         for jt in range(JT):
@@ -340,19 +345,27 @@ def tile_list_league_market_features_kernel(
             if jt + LEAD < JT:
                 order.append((jt + LEAD, 0))
 
+        for unit in order[:SUM_BANKS]:
+            open_sum(*unit)
+            if unit not in VECTOR_SUBTRACTS:
+                turn(home_term, *unit, True, False)
+        away_codes = [gather("away_codes0", away_table0[:].bitcast(U32), away_list, U32)]
+        away_codes.append(gather("away_codes1", away_table1[:].bitcast(U32), away_list, U32, pieces=2))
+
         n = len(order)
         for i in range(n + 4):
             if i < n:
                 away(*order[i])
             if i == 1:
                 round_wt(1)
-                quantise_wt(1)
             if 1 <= i <= n:
                 if order[i - 1][1] == 1:
                     stadium(*order[i - 1])
                 turn_and_add(*order[i - 1])
             if 2 <= i <= n + 1:
                 scale_and_squash(*order[i - 2])
+            if i == 2:
+                quantise_wt(1)
             if 3 <= i <= n + 2:
                 apply_gain(*order[i - 3])
             if i >= 4:

@@ -33,8 +33,8 @@ LIST_ROWS = 16
 
 MX_BANKS = 4
 SUM_BANKS = 4
-LEAD = 3
-VECTOR_SUBTRACTS = ((0, 0), (1, 0))
+LEAD = 4
+VECTOR_SUBTRACTS = ((0, 0), (1, 0), (0, 1), (1, 1))
 WT_PARTS = 2
 VECTOR_EMPTIES = ()
 LAST_UNIT = (JT - 1, HALVES - 1)
@@ -92,14 +92,15 @@ def tile_list_league_market_features_kernel(
             nc.sync.dma_start(out=raw[:], in_=wt_rows[:, :, b * PASS : (b + 1) * PASS])
             return raw
 
-        def scale_rows_tile(name):
+        def scale_rows_tile(name, first):
             rows = held(name, [P, T], U8)
-            nc.vector.memset(rows[QUAD : 2 * QUAD, :].bitcast(I32), 0)
-            nc.vector.memset(rows[2 * QUAD : P, :].bitcast(I32), 0)
+            nc.vector.memset(rows[first + QUAD : first + 2 * QUAD, :].bitcast(I32), 0)
+            other = 2 * QUAD - first
+            nc.vector.memset(rows[other : other + 2 * QUAD, :].bitcast(I32), 0)
             return rows
 
-        def load_scale_rows(rows, scales):
-            nc.sync.dma_start(out=rows[0:QUAD, :].bitcast(I32), in_=scales.rearrange("a q c -> q a c").bitcast(I32))
+        def load_scale_rows(rows, scales, first):
+            nc.sync.dma_start(out=rows[first : first + QUAD, :].bitcast(I32), in_=scales.rearrange("a q c -> q a c").bitcast(I32))
 
         def place_rows(plane, picked):
             per_quad = LIVE * K_PASSES
@@ -111,8 +112,8 @@ def tile_list_league_market_features_kernel(
             return [plane[:, a * S : (a + 1) * S] for a in range(K_PASSES)]
 
         ws_plane = zeroed_plane("ws_plane", K_PASSES * H)
-        home_scale_rows = scale_rows_tile("home_scale_rows")
-        away_scale_rows = scale_rows_tile("away_scale_rows")
+        home_scale_rows = scale_rows_tile("home_scale_rows", 0)
+        away_scale_rows = scale_rows_tile("away_scale_rows", 2 * QUAD)
         home_plane = zeroed_plane("home_plane", K_PASSES * S)
         stad_table_plane = zeroed_plane("stad_table_plane", T3)
         away_plane = zeroed_plane("away_plane", K_PASSES * S)
@@ -260,17 +261,21 @@ def tile_list_league_market_features_kernel(
                 nc.scalar.activation(out=squashed[jt, b][:, cols], in_=scaled[jt, b][:, cols], func=ACT.Tanh)
 
         def apply_gain(jt, b):
+            engine = nc.gpsimd if b == 0 and jt < JT - 1 else nc.vector
             for js in market_ranges(jt, b):
-                nc.vector.tensor_tensor(
+                engine.tensor_tensor(
                     out=markets(h_bf[b][:, jt * PASS : (jt + 1) * PASS])[:, js, :],
                     in0=markets(squashed[jt, b][:])[:, js, :],
                     in1=gain[:, b : b + 1, :].to_broadcast([P, js.stop - js.start, PACK]), op=ALU.mult,
                 )
 
         def quantise_h(jt, b):
+            if b == 0 and jt < JT - 1:
+                return
+            first = 0 if b == 0 else jt
             nc.vector.quantize_mx(
-                out=h_codes[b][:, jt * P : (jt + 1) * P].bitcast(FP8X4), scales=h_plane[b][:, jt * P : (jt + 1) * P],
-                in_=h_bf[b][:, jt * PASS : (jt + 1) * PASS],
+                out=h_codes[b][:, first * P : (jt + 1) * P].bitcast(FP8X4), scales=h_plane[b][:, first * P : (jt + 1) * P],
+                in_=h_bf[b][:, first * PASS : (jt + 1) * PASS],
             )
 
         out_rows = out.rearrange("(nt p) j -> p nt j", p=P)
@@ -301,17 +306,17 @@ def tile_list_league_market_features_kernel(
                 nc.sync.dma_start(out=out_rows[:, part * tiles : (part + 1) * tiles, jt * P : (jt + 1) * P], in_=res[:])
 
         home_list = load_list("home_list", offs)
-        load_scale_rows(home_scale_rows, tab_scales)
+        load_scale_rows(home_scale_rows, tab_scales, 0)
         ws_codes = held("ws_codes", [P, K_PASSES, 2 * H], U8)
         nc.sync.dma_start(out=ws_codes[:].bitcast(I32), in_=ws_words.rearrange("a p c -> p a c").bitcast(I32))
         away_list = load_list("away_list", offs2)
-        load_scale_rows(away_scale_rows, tab2_scales)
+        load_scale_rows(away_scale_rows, tab2_scales, 2 * QUAD)
         load_plane(ws_plane, ws_scales)
         home_table0 = load_words("home_table0", tab_words[0])
         stad_table = held("stad_table", [P, 2 * T3], U8)
         nc.sync.dma_start(out=stad_table[:].bitcast(I32), in_=tab3_words[0].bitcast(I32))
         stad_list = load_list("stad_list", offs3)
-        home_planes = place_rows(home_plane, gather("home_picked_rows", home_scale_rows[:], home_list, U8))
+        home_planes = place_rows(home_plane, gather("home_picked_rows", home_scale_rows[:], home_list, U8)[:])
         home_table1 = load_words("home_table1", tab_words[1])
         away_picked = gather("away_picked_rows", away_scale_rows[:], away_list, U8)
         load_plane(stad_table_plane, tab3_scales)
@@ -323,7 +328,7 @@ def tile_list_league_market_features_kernel(
         home_codes.append(gather("home_codes1", home_table1[:].bitcast(U32), home_list, U32, pieces=2))
         away_table1 = load_words("away_table1", tab2_words[1])
         stad_plane = gather("stad_plane", stad_table_plane[:], stad_list, U8)
-        away_planes = place_rows(away_plane, away_picked)
+        away_planes = place_rows(away_plane, away_picked[2 * QUAD : P, :])
         for b in range(HALVES):
             for jt in range(JT):
                 home(jt, b)

@@ -31,18 +31,24 @@ N = 512
 HALVES = H // PASS
 LIST_ROWS = 16
 
-MX_BANKS = 4
-SUM_BANKS = 4
-LEAD = 4
-VECTOR_SUBTRACTS = ((0, 0), (1, 0), (0, 1), (1, 1))
+UNITS = [(jt, b) for b in range(HALVES) for jt in range(JT)]
+FUSED = UNITS[:3]
+VECTOR_SUBTRACTS = UNITS[3:]
+EARLY = UNITS[:2]
+STAD_BANKS = (0, 1, 2, 3, 2, 3, 2, 3)
+HOME_BANKS = (4, 5, 6, 7, 0, 1, 2, 3)
+AWAY_BANKS = (6, 7, 0, 6, 7, 1, 6, 7)
+SUM_BANKS = (4, 5, 0, 4, 5, 0, 4, 5)
+OUT_BANKS = ((1,), (6,), (7,), (2, 3))
 WT_PARTS = 2
-VECTOR_EMPTIES = ()
 LAST_UNIT = (JT - 1, HALVES - 1)
 SHARED_AT = {
-    "home_table0": 0, "away_table0": 512,
-    "home_table1": 16384, "away_table1": 9216, "gain": 18432, "stad_plane": 18496,
-    "home_scale_rows": 24512,
-    "wt_raw0": 26624, "wt_raw1": 26624, "wt_bf0": 34816, "wo_codes": 34816,
+    "home_table0": 0, "away_table1": 0,
+    "home_table1": 8192, "wt_raw1": 8192, "home_scale_rows": 15360, "home_picked_rows": 18432,
+    "ws_codes1": 16384, "away_table0": 18432, "gain": 18432, "wo_codes": 18496,
+    "two1": 32768, "away_codes0_0": 32768, "two2": 34816, "away_codes1_0": 34816,
+    "gate11": 36864, "h_codes0": 36864,
+    "wt_bf0": 26624, "away_picked_rows": 26624,
 }
 
 
@@ -66,10 +72,10 @@ def tile_list_league_market_features_kernel(
             nc.gpsimd.memset(plane[:].bitcast(I32), 0)
             return plane
 
-        def load_plane(plane, scales):
+        def load_plane(plane, scales, rows=range(LIVE)):
             passes = scales.shape[0]
             by_row = scales.rearrange("a (q r) c -> r q a c", r=LIVE)
-            for r in range(LIVE):
+            for r in rows:
                 nc.sync.dma_start(
                     out=plane[r:P:QUAD, :].rearrange("q (a c) -> q a c", a=passes).bitcast(I32),
                     in_=by_row[r].bitcast(I32),
@@ -83,6 +89,12 @@ def tile_list_league_market_features_kernel(
         def load_list(name, lst):
             tile = keep.tile([P, S // LIST_ROWS], U16, name=name)
             nc.sync.dma_start(tile[:], lst)
+            return tile
+
+        def load_ws(b):
+            tile = held("ws_codes%d" % b, [P, K_PASSES, 2 * PASS], U8)
+            words = ws_words.rearrange("a p c -> p a c")[:, :, 2 * b * PASS : 2 * (b + 1) * PASS]
+            nc.sync.dma_start(out=tile[:].bitcast(I32), in_=words.bitcast(I32))
             return tile
 
         wt_rows = wt.rearrange("(p j) c -> p j c", j=PACK)
@@ -111,24 +123,28 @@ def tile_list_league_market_features_kernel(
                 )
             return [plane[:, a * S : (a + 1) * S] for a in range(K_PASSES)]
 
+        stad_table_plane = zeroed_plane("stad_table_plane", T3)
         ws_plane = zeroed_plane("ws_plane", K_PASSES * H)
         home_scale_rows = scale_rows_tile("home_scale_rows", 0)
         away_scale_rows = scale_rows_tile("away_scale_rows", 2 * QUAD)
         home_plane = zeroed_plane("home_plane", K_PASSES * S)
-        stad_table_plane = zeroed_plane("stad_table_plane", T3)
         away_plane = zeroed_plane("away_plane", K_PASSES * S)
         ident = held("ident", [P, P], F32)
         make_identity(nc, ident[:])
 
-        def gather(name, window, lst, dtype, pieces=1):
-            tile = held(name, [P, S], dtype)
-            step = S // pieces
-            for i in range(pieces):
-                nc.vector.tensor_copy(
-                    out=tile[:, i * step : (i + 1) * step],
-                    in_=window.indirect(lst[:, i * step // LIST_ROWS : (i + 1) * step // LIST_ROWS]),
-                )
+        def gather(name, window, lst, dtype):
+            tile = held(name, [P, lst.shape[1] * LIST_ROWS], dtype)
+            nc.vector.tensor_copy(out=tile[:], in_=window.indirect(lst))
             return tile
+
+        def gather_words(name, table, lst, pieces):
+            step = JT // pieces
+            cols = step * P // LIST_ROWS
+            tiles = [
+                gather("%s_%d" % (name, i), table[:].bitcast(U32), lst[:, i * cols : (i + 1) * cols], U32)
+                for i in range(pieces)
+            ]
+            return [tiles[jt // step][:, jt % step * P : (jt % step + 1) * P] for jt in range(JT)]
 
         def unit_tiles(name):
             return {(jt, b): held("%s%d%d" % (name, jt, b), [P, PASS], F32) for jt in range(JT) for b in range(HALVES)}
@@ -142,8 +158,8 @@ def tile_list_league_market_features_kernel(
         h_codes = [held("h_codes%d" % b, [P, S], U32) for b in range(HALVES)]
         h_plane = [held("h_plane%d" % b, [P, S], U8) for b in range(HALVES)]
 
-        def mx_bank():
-            return psum.tile([P, PASS], F32, name="mx", tag="mx", bufs=MX_BANKS)
+        def bank_tile(k):
+            return psum.tile([P, PASS], F32, name="bank%d" % k, tag="bank%d" % k, bufs=1)
 
         def channels_by_slot(bank):
             return bank[:].rearrange("p (m t) -> p t m", t=PACK)
@@ -167,8 +183,8 @@ def tile_list_league_market_features_kernel(
                 ms = slice(part * step, (part + 1) * step)
                 dst = wt_bf[b][:].rearrange("p (t m j) -> p m t j", t=PACK, j=PACK)[:, ms, :, :]
                 src = wt_raw[b][:].rearrange("p j (m t) -> p m t j", t=PACK)[:, ms, :, :]
-                if (b, part) == (1, 0):
-                    nc.scalar.activation(out=dst, in_=src, func=ACT.Copy)
+                if part == 0:
+                    nc.scalar.copy(out=dst, in_=src)
                 elif b == 1:
                     nc.gpsimd.tensor_scalar(out=dst, in0=src, scalar1=1.0, scalar2=0.0, op0=ALU.mult, op1=ALU.add)
                 else:
@@ -178,9 +194,16 @@ def tile_list_league_market_features_kernel(
             nc.vector.quantize_mx(out=wt_codes[b][:].bitcast(FP8X4), scales=wt_plane[b][:], in_=wt_bf[b][:])
 
         def stadium(jt, b):
-            bank = mx_bank()
+            bank = bank_tile(STAD_BANKS[UNITS.index((jt, b))])
             codes = stad_codes[:, 2 * P * jt : 2 * P * (jt + 1)].bitcast(FP4X4)
             plane = stad_plane[:, jt * P : (jt + 1) * P]
+            if (jt, b) in FUSED:
+                nc.tensor.matmul_mx(
+                    out=bank[:], lhsT=codes, lhsT_scale=plane,
+                    rhs=wt_codes[b][:].bitcast(FP8X4), rhs_scale=wt_plane[b][:], start=True, stop=True,
+                )
+                nc.scalar.activation(out=gate[jt, b][:], in_=bank[:], func=ACT.Sigmoid, scale=2.0)
+                return
             for t in range(PACK):
                 nc.tensor.matmul_mx(
                     out=bank[:, t * P : (t + 1) * P],
@@ -190,33 +213,54 @@ def tile_list_league_market_features_kernel(
                 )
             nc.scalar.activation(out=markets(gate[jt, b][:]), in_=slots_by_market(bank), func=ACT.Tanh)
 
-        def sum_tile():
-            return psum.tile([P, PASS], F32, name="sum", tag="sum", bufs=SUM_BANKS)
+        def side_pass(codes, planes, jt, b, bank, a):
+            nc.tensor.matmul_mx(
+                out=bank[:],
+                lhsT=codes[a][jt].bitcast(FP8X4),
+                lhsT_scale=planes[a][:, jt * P : (jt + 1) * P],
+                rhs=ws_codes[b][:, a, :].bitcast(FP4X4),
+                rhs_scale=ws_plane[:, a * H + b * PASS : a * H + (b + 1) * PASS],
+                start=(a == 0),
+                stop=(a == K_PASSES - 1),
+            )
 
-        def side_product(codes, planes, jt, b, bank):
-            cols = slice(jt * P, (jt + 1) * P)
-            for a in range(K_PASSES):
-                nc.tensor.matmul_mx(
-                    out=bank[:],
-                    lhsT=codes[a][:, cols].bitcast(FP8X4),
-                    lhsT_scale=planes[a][:, cols],
-                    rhs=ws_codes[:, a, 2 * b * PASS : 2 * (b + 1) * PASS].bitcast(FP4X4),
-                    rhs_scale=ws_plane[:, a * H + b * PASS : a * H + (b + 1) * PASS],
-                    start=(a == 0),
-                    stop=(a == K_PASSES - 1),
-                )
-            return bank
+        def gated_read(term, bank, jt, b, factor):
+            nc.vector.scalar_tensor_tensor(
+                out=slots(term[jt, b]), in0=channels_by_slot(bank), scalar=factor, in1=slots(gate[jt, b]),
+                op0=ALU.mult, op1=ALU.mult,
+            )
+
+        two = [held("two%d" % jt, [P, 1], F32) for jt, b in FUSED]
+        for tile in two:
+            nc.gpsimd.memset(tile[:], 2.0)
+        side_bank = {}
+
+        def home_first(jt, b):
+            side_bank[jt, b] = bank_tile(HOME_BANKS[UNITS.index((jt, b))])
+            side_pass(home_codes, home_planes, jt, b, side_bank[jt, b], 0)
 
         def home(jt, b):
-            bank = side_product(home_codes, home_planes, jt, b, mx_bank())
-            if (jt, b) in VECTOR_EMPTIES:
-                nc.vector.tensor_copy(out=slots(home_term[jt, b]), in_=channels_by_slot(bank))
+            if b == 1:
+                home_first(jt, b)
+            bank = side_bank[jt, b]
+            side_pass(home_codes, home_planes, jt, b, bank, 1)
+            if (jt, b) in FUSED:
+                gated_read(home_term, bank, jt, b, two[jt][:])
             else:
                 nc.scalar.activation(out=slots(home_term[jt, b]), in_=channels_by_slot(bank), func=ACT.Copy)
 
+        def away_first(jt, b):
+            side_bank[jt, b] = bank_tile(AWAY_BANKS[UNITS.index((jt, b))])
+            side_pass(away_codes, away_planes, jt, b, side_bank[jt, b], 0)
+
         def away(jt, b):
-            bank = side_product(away_codes, away_planes, jt, b, mx_bank())
-            if (jt, b) in VECTOR_SUBTRACTS:
+            if (jt, b) not in FUSED:
+                away_first(jt, b)
+            bank = side_bank[jt, b]
+            side_pass(away_codes, away_planes, jt, b, bank, 1)
+            if (jt, b) in FUSED:
+                gated_read(away_term, bank, jt, b, -2.0)
+            elif (jt, b) in VECTOR_SUBTRACTS:
                 nc.vector.tensor_tensor(
                     out=slots(away_term[jt, b]), in0=slots(home_term[jt, b]), in1=channels_by_slot(bank), op=ALU.subtract,
                 )
@@ -233,7 +277,7 @@ def tile_list_league_market_features_kernel(
                 )
 
         def open_sum(jt, b):
-            sum_bank[jt, b] = sum_tile()
+            sum_bank[jt, b] = bank_tile(SUM_BANKS[UNITS.index((jt, b))])
 
         def turn_and_add(jt, b):
             if (jt, b) in VECTOR_SUBTRACTS:
@@ -244,14 +288,17 @@ def tile_list_league_market_features_kernel(
                 turn(away_term, jt, b, False, True)
             else:
                 open_sum(jt, b)
-                turn(away_term, jt, b, True, False)
-                turn(home_term, jt, b, False, True)
+                turn(home_term, jt, b, True, False)
+                turn(away_term, jt, b, False, True)
 
         def market_ranges(jt, b):
             count = 2 if (jt, b) == LAST_UNIT else 1
             return [slice(i * P // count, (i + 1) * P // count) for i in range(count)]
 
         def scale_and_squash(jt, b):
+            if (jt, b) in FUSED:
+                nc.scalar.activation(out=markets(squashed[jt, b][:]), in_=slots_by_market(sum_bank[jt, b]), func=ACT.Tanh)
+                return
             for js in market_ranges(jt, b):
                 nc.vector.scalar_tensor_tensor(
                     out=markets(scaled[jt, b][:])[:, js, :], in0=markets(gate[jt, b][:])[:, js, :], scalar=1.0,
@@ -261,7 +308,7 @@ def tile_list_league_market_features_kernel(
                 nc.scalar.activation(out=squashed[jt, b][:, cols], in_=scaled[jt, b][:, cols], func=ACT.Tanh)
 
         def apply_gain(jt, b):
-            engine = nc.gpsimd if b == 0 and jt < JT - 1 else nc.vector
+            engine = nc.gpsimd if b == 0 else nc.vector
             for js in market_ranges(jt, b):
                 engine.tensor_tensor(
                     out=markets(h_bf[b][:, jt * PASS : (jt + 1) * PASS])[:, js, :],
@@ -283,7 +330,7 @@ def tile_list_league_market_features_kernel(
         def features(jt):
             parts = 2 if jt == JT - 1 else 1
             tiles = N // P // parts
-            banks = [mx_bank() for part in range(parts)]
+            banks = [bank_tile(k) for k in OUT_BANKS[jt]]
             for b in range(HALVES):
                 for nt in range(N // P):
                     part, place = divmod(nt, tiles)
@@ -307,74 +354,73 @@ def tile_list_league_market_features_kernel(
 
         home_list = load_list("home_list", offs)
         load_scale_rows(home_scale_rows, tab_scales, 0)
-        ws_codes = held("ws_codes", [P, K_PASSES, 2 * H], U8)
-        nc.sync.dma_start(out=ws_codes[:].bitcast(I32), in_=ws_words.rearrange("a p c -> p a c").bitcast(I32))
-        away_list = load_list("away_list", offs2)
-        load_scale_rows(away_scale_rows, tab2_scales, 2 * QUAD)
-        load_plane(ws_plane, ws_scales)
-        home_table0 = load_words("home_table0", tab_words[0])
+        stad_list = load_list("stad_list", offs3)
         stad_table = held("stad_table", [P, 2 * T3], U8)
         nc.sync.dma_start(out=stad_table[:].bitcast(I32), in_=tab3_words[0].bitcast(I32))
-        stad_list = load_list("stad_list", offs3)
-        home_planes = place_rows(home_plane, gather("home_picked_rows", home_scale_rows[:], home_list, U8)[:])
-        home_table1 = load_words("home_table1", tab_words[1])
-        away_picked = gather("away_picked_rows", away_scale_rows[:], away_list, U8)
-        load_plane(stad_table_plane, tab3_scales)
+        load_plane(stad_table_plane, tab3_scales, range(LIVE - 1))
         wt_raw = [load_wt(0)]
-        home_codes = [gather("home_codes0", home_table0[:].bitcast(U32), home_list, U32, pieces=2)]
+        load_plane(stad_table_plane, tab3_scales, range(LIVE - 1, LIVE))
+        ws_codes = [load_ws(0)]
+        away_list = load_list("away_list", offs2)
+        load_scale_rows(away_scale_rows, tab2_scales, 2 * QUAD)
+        load_plane(ws_plane, ws_scales, range(LIVE // 2))
+        home_table0 = load_words("home_table0", tab_words[0])
+        load_plane(ws_plane, ws_scales, range(LIVE // 2, LIVE))
+        home_planes = place_rows(home_plane, gather("home_picked_rows", home_scale_rows[:], home_list[:], U8)[:])
+        home_table1 = load_words("home_table1", tab_words[1])
+        ws_codes.append(load_ws(1))
         away_table0 = load_words("away_table0", tab2_words[0])
         stad_codes = held("stad_codes", [P, 2 * S], U8)
         nc.vector.tensor_copy(out=stad_codes[:].bitcast(U16), in_=stad_table[:].bitcast(U16).indirect(stad_list[:]))
-        home_codes.append(gather("home_codes1", home_table1[:].bitcast(U32), home_list, U32, pieces=2))
-        away_table1 = load_words("away_table1", tab2_words[1])
-        stad_plane = gather("stad_plane", stad_table_plane[:], stad_list, U8)
-        away_planes = place_rows(away_plane, away_picked[2 * QUAD : P, :])
-        for b in range(HALVES):
-            for jt in range(JT):
-                home(jt, b)
+        stad_plane = gather("stad_plane", stad_table_plane[:], stad_list[:], U8)
         round_wt(0)
-        wt_raw.append(load_wt(1))
         quantise_wt(0)
+        for jt in range(JT):
+            stadium(jt, 0)
+        away_picked = gather("away_picked_rows", away_scale_rows[:], away_list[:], U8)
+        home_codes = [gather_words("home_codes0", home_table0, home_list, 1)]
+        away_table1 = load_words("away_table1", tab2_words[1])
+        away_planes = place_rows(away_plane, away_picked[2 * QUAD : P, :])
+        for unit in UNITS[:JT]:
+            home_first(*unit)
+        home_codes.append(gather_words("home_codes1", home_table1, home_list, 2))
+        wt_raw.append(load_wt(1))
+        for unit in UNITS:
+            home(*unit)
+        for unit in EARLY:
+            open_sum(*unit)
+            turn(home_term, *unit, True, False)
         gain = held("gain", [P, HALVES, PACK], F32)
         nc.sync.dma_start(out=gain[:], in_=gh.rearrange("(b p t) -> p b t", b=HALVES, t=PACK))
         wo_codes = held("wo_codes", [P, HALVES, N], I32)
         nc.sync.dma_start(out=wo_codes[:], in_=wo_words.rearrange("a p c i -> p a (c i)").bitcast(I32))
         wo_plane = zeroed_plane("wo_plane", HALVES * N)
         load_plane(wo_plane, wo_scales)
-        for jt in range(JT):
-            stadium(jt, 0)
 
-        order = [(jt, 0) for jt in range(LEAD)]
-        for jt in range(JT):
-            order.append((jt, 1))
-            if jt + LEAD < JT:
-                order.append((jt + LEAD, 0))
+        away_codes = [gather_words("away_codes0", away_table0, away_list, 1)]
+        for unit in FUSED:
+            away_first(*unit)
+        away_codes.append(gather_words("away_codes1", away_table1, away_list, 2))
 
-        for unit in order[:SUM_BANKS]:
-            open_sum(*unit)
-            if unit not in VECTOR_SUBTRACTS:
-                turn(home_term, *unit, True, False)
-        away_codes = [gather("away_codes0", away_table0[:].bitcast(U32), away_list, U32)]
-        away_codes.append(gather("away_codes1", away_table1[:].bitcast(U32), away_list, U32, pieces=2))
-
-        n = len(order)
+        n = len(UNITS)
         for i in range(n + 4):
             if i < n:
-                away(*order[i])
+                away(*UNITS[i])
             if i == 1:
                 round_wt(1)
             if 1 <= i <= n:
-                if order[i - 1][1] == 1:
-                    stadium(*order[i - 1])
-                turn_and_add(*order[i - 1])
+                if UNITS[i - 1][1] == 1:
+                    stadium(*UNITS[i - 1])
+                turn_and_add(*UNITS[i - 1])
             if 2 <= i <= n + 1:
-                scale_and_squash(*order[i - 2])
-            if i == 2:
+                scale_and_squash(*UNITS[i - 2])
+            if i == 3:
                 quantise_wt(1)
             if 3 <= i <= n + 2:
-                apply_gain(*order[i - 3])
-            if i >= 4:
-                jt, b = order[i - 4]
+                apply_gain(*UNITS[i - 3])
+            if i == JT + 3:
+                quantise_h(JT - 1, 0)
+            if i >= JT + 4:
+                jt, b = UNITS[i - 4]
                 quantise_h(jt, b)
-                if b == HALVES - 1:
-                    features(jt)
+                features(jt)

@@ -33,7 +33,7 @@ LIST_ROWS = 16
 
 UNITS = [(jt, b) for b in range(HALVES) for jt in range(JT)]
 FUSED = UNITS[:3]
-VECTOR_SUBTRACTS = UNITS[3:]
+VECTOR_SUBTRACTS = UNITS[3:6]
 EARLY = UNITS[:2]
 STAD_BANKS = (0, 1, 2, 3, 2, 3, 2, 3)
 HOME_BANKS = (4, 5, 6, 7, 0, 1, 2, 3)

@@ -33,20 +33,19 @@ LIST_ROWS = 16
 
 UNITS = [(jt, b) for b in range(HALVES) for jt in range(JT)]
 FUSED = UNITS[:3]
-VECTOR_SUBTRACTS = UNITS[3:6]
-EARLY = UNITS[:2]
+VECTOR_SUBTRACTS = UNITS[3:7]
+EARLY_SUMS = UNITS[:2]
+LAST_UNIT = UNITS[-1]
 STAD_BANKS = (0, 1, 2, 3, 2, 3, 2, 3)
 HOME_BANKS = (4, 5, 6, 7, 0, 1, 2, 3)
 AWAY_BANKS = (6, 7, 0, 6, 7, 1, 6, 7)
 SUM_BANKS = (4, 5, 0, 4, 5, 0, 4, 5)
 OUT_BANKS = ((1,), (6,), (7,), (2, 3))
 WT_PARTS = 2
-LAST_UNIT = (JT - 1, HALVES - 1)
 SHARED_AT = {
     "home_table0": 0, "away_table1": 0,
-    "home_table1": 8192, "wt_raw1": 8192, "home_scale_rows": 15360, "home_picked_rows": 18432,
-    "ws_codes1": 16384, "away_table0": 18432, "gain": 18432, "wo_codes": 18496,
-    "two1": 32768, "away_codes0_0": 32768, "two2": 34816, "away_codes1_0": 34816,
+    "home_scale_rows": 15360, "home_table1": 8192, "ws_codes1": 16384, "wt_raw1": 8192,
+    "home_picked_rows": 18432, "away_table0": 18432, "gain": 18432, "wo_codes": 18496,
     "gate11": 36864, "h_codes0": 36864,
     "wt_bf0": 26624, "away_picked_rows": 26624,
 }
@@ -112,7 +111,9 @@ def tile_list_league_market_features_kernel(
             return rows
 
         def load_scale_rows(rows, scales, first):
-            nc.sync.dma_start(out=rows[first : first + QUAD, :].bitcast(I32), in_=scales.rearrange("a q c -> q a c").bitcast(I32))
+            nc.sync.dma_start(
+                out=rows[first : first + QUAD, :].bitcast(I32), in_=scales.rearrange("a q c -> q a c").bitcast(I32)
+            )
 
         def place_rows(plane, picked):
             per_quad = LIVE * K_PASSES
@@ -230,9 +231,6 @@ def tile_list_league_market_features_kernel(
                 op0=ALU.mult, op1=ALU.mult,
             )
 
-        two = [held("two%d" % jt, [P, 1], F32) for jt, b in FUSED]
-        for tile in two:
-            nc.gpsimd.memset(tile[:], 2.0)
         side_bank = {}
 
         def home_first(jt, b):
@@ -245,7 +243,7 @@ def tile_list_league_market_features_kernel(
             bank = side_bank[jt, b]
             side_pass(home_codes, home_planes, jt, b, bank, 1)
             if (jt, b) in FUSED:
-                gated_read(home_term, bank, jt, b, two[jt][:])
+                gated_read(home_term, bank, jt, b, 2.0)
             else:
                 nc.scalar.activation(out=slots(home_term[jt, b]), in_=channels_by_slot(bank), func=ACT.Copy)
 
@@ -280,12 +278,11 @@ def tile_list_league_market_features_kernel(
             sum_bank[jt, b] = bank_tile(SUM_BANKS[UNITS.index((jt, b))])
 
         def turn_and_add(jt, b):
-            if (jt, b) in VECTOR_SUBTRACTS:
-                if (jt, b) not in sum_bank:
-                    open_sum(jt, b)
-                turn(away_term, jt, b, True, True)
-            elif (jt, b) in sum_bank:
+            if (jt, b) in EARLY_SUMS:
                 turn(away_term, jt, b, False, True)
+            elif (jt, b) in VECTOR_SUBTRACTS:
+                open_sum(jt, b)
+                turn(away_term, jt, b, True, True)
             else:
                 open_sum(jt, b)
                 turn(home_term, jt, b, True, False)
@@ -316,13 +313,11 @@ def tile_list_league_market_features_kernel(
                     in1=gain[:, b : b + 1, :].to_broadcast([P, js.stop - js.start, PACK]), op=ALU.mult,
                 )
 
-        def quantise_h(jt, b):
-            if b == 0 and jt < JT - 1:
-                return
-            first = 0 if b == 0 else jt
+        def quantise_h(b, first, last):
             nc.vector.quantize_mx(
-                out=h_codes[b][:, first * P : (jt + 1) * P].bitcast(FP8X4), scales=h_plane[b][:, first * P : (jt + 1) * P],
-                in_=h_bf[b][:, first * PASS : (jt + 1) * PASS],
+                out=h_codes[b][:, first * P : (last + 1) * P].bitcast(FP8X4),
+                scales=h_plane[b][:, first * P : (last + 1) * P],
+                in_=h_bf[b][:, first * PASS : (last + 1) * PASS],
             )
 
         out_rows = out.rearrange("(nt p) j -> p nt j", p=P)
@@ -387,7 +382,7 @@ def tile_list_league_market_features_kernel(
         wt_raw.append(load_wt(1))
         for unit in UNITS:
             home(*unit)
-        for unit in EARLY:
+        for unit in EARLY_SUMS:
             open_sum(*unit)
             turn(home_term, *unit, True, False)
         gain = held("gain", [P, HALVES, PACK], F32)
@@ -414,13 +409,13 @@ def tile_list_league_market_features_kernel(
                 turn_and_add(*UNITS[i - 1])
             if 2 <= i <= n + 1:
                 scale_and_squash(*UNITS[i - 2])
-            if i == 3:
+            if i == JT - 1:
                 quantise_wt(1)
             if 3 <= i <= n + 2:
                 apply_gain(*UNITS[i - 3])
             if i == JT + 3:
-                quantise_h(JT - 1, 0)
-            if i >= JT + 4:
-                jt, b = UNITS[i - 4]
-                quantise_h(jt, b)
+                quantise_h(0, 0, JT - 1)
+            if i > JT + 3:
+                jt = UNITS[i - 4][0]
+                quantise_h(1, jt, jt)
                 features(jt)

@@ -44,7 +44,7 @@ OUT_BANKS = ((1,), (6,), (7,), (2, 3))
 WT_PARTS = 2
 SHARED_AT = {
     "home_table0": 0, "away_table1": 0,
-    "home_scale_rows": 15360, "home_table1": 8192, "ws_codes1": 16384, "wt_raw1": 8192,
+    "home_scale_rows": 15360, "home_table1": 8192, "wt_raw1": 8192,
     "home_picked_rows": 18432, "away_table0": 18432, "gain": 18432, "wo_codes": 18496,
     "gate11": 36864, "h_codes0": 36864,
     "wt_bf0": 26624, "away_picked_rows": 26624,
@@ -90,10 +90,9 @@ def tile_list_league_market_features_kernel(
             nc.sync.dma_start(tile[:], lst)
             return tile
 
-        def load_ws(b):
-            tile = held("ws_codes%d" % b, [P, K_PASSES, 2 * PASS], U8)
-            words = ws_words.rearrange("a p c -> p a c")[:, :, 2 * b * PASS : 2 * (b + 1) * PASS]
-            nc.sync.dma_start(out=tile[:].bitcast(I32), in_=words.bitcast(I32))
+        def load_ws():
+            tile = held("ws_codes", [P, K_PASSES, 2 * H], U8)
+            nc.sync.dma_start(out=tile[:].bitcast(I32), in_=ws_words.rearrange("a p c -> p a c").bitcast(I32))
             return tile
 
         wt_rows = wt.rearrange("(p j) c -> p j c", j=PACK)
@@ -219,7 +218,7 @@ def tile_list_league_market_features_kernel(
                 out=bank[:],
                 lhsT=codes[a][jt].bitcast(FP8X4),
                 lhsT_scale=planes[a][:, jt * P : (jt + 1) * P],
-                rhs=ws_codes[b][:, a, :].bitcast(FP4X4),
+                rhs=ws_codes[:, a, 2 * b * PASS : 2 * (b + 1) * PASS].bitcast(FP4X4),
                 rhs_scale=ws_plane[:, a * H + b * PASS : a * H + (b + 1) * PASS],
                 start=(a == 0),
                 stop=(a == K_PASSES - 1),
@@ -238,8 +237,6 @@ def tile_list_league_market_features_kernel(
             side_pass(home_codes, home_planes, jt, b, side_bank[jt, b], 0)
 
         def home(jt, b):
-            if b == 1:
-                home_first(jt, b)
             bank = side_bank[jt, b]
             side_pass(home_codes, home_planes, jt, b, bank, 1)
             if (jt, b) in FUSED:
@@ -355,7 +352,7 @@ def tile_list_league_market_features_kernel(
         load_plane(stad_table_plane, tab3_scales, range(LIVE - 1))
         wt_raw = [load_wt(0)]
         load_plane(stad_table_plane, tab3_scales, range(LIVE - 1, LIVE))
-        ws_codes = [load_ws(0)]
+        ws_codes = load_ws()
         away_list = load_list("away_list", offs2)
         load_scale_rows(away_scale_rows, tab2_scales, 2 * QUAD)
         load_plane(ws_plane, ws_scales, range(LIVE // 2))
@@ -363,7 +360,6 @@ def tile_list_league_market_features_kernel(
         load_plane(ws_plane, ws_scales, range(LIVE // 2, LIVE))
         home_planes = place_rows(home_plane, gather("home_picked_rows", home_scale_rows[:], home_list[:], U8)[:])
         home_table1 = load_words("home_table1", tab_words[1])
-        ws_codes.append(load_ws(1))
         away_table0 = load_words("away_table0", tab2_words[0])
         stad_codes = held("stad_codes", [P, 2 * S], U8)
         nc.vector.tensor_copy(out=stad_codes[:].bitcast(U16), in_=stad_table[:].bitcast(U16).indirect(stad_list[:]))
@@ -373,10 +369,10 @@ def tile_list_league_market_features_kernel(
         for jt in range(JT):
             stadium(jt, 0)
         away_picked = gather("away_picked_rows", away_scale_rows[:], away_list[:], U8)
-        home_codes = [gather_words("home_codes0", home_table0, home_list, 1)]
+        home_codes = [gather_words("home_codes0", home_table0, home_list, 2)]
         away_table1 = load_words("away_table1", tab2_words[1])
         away_planes = place_rows(away_plane, away_picked[2 * QUAD : P, :])
-        for unit in UNITS[:JT]:
+        for unit in sorted(UNITS, key=lambda u: (u[0] // 2, u[1])):
             home_first(*unit)
         home_codes.append(gather_words("home_codes1", home_table1, home_list, 2))
         wt_raw.append(load_wt(1))

@@ -41,11 +41,12 @@ HOME_BANKS = (4, 5, 6, 7, 0, 1, 2, 3)
 AWAY_BANKS = (6, 7, 0, 6, 7, 1, 6, 7)
 SUM_BANKS = (4, 5, 0, 4, 5, 0, 4, 5)
 OUT_BANKS = ((1,), (6,), (7,), (2, 3))
+DMA_TILES = ("home_table", "away_table", "stad_table", "wt_raw", "ws_", "wo_", "home_scale", "away_scale", "home_plane", "away_plane", "res")
 WT_PARTS = 2
 SHARED_AT = {
     "home_table0": 0, "away_table1": 0,
     "home_scale_rows": 15360, "home_table1": 8192, "wt_raw1": 8192,
-    "home_picked_rows": 18432, "away_table0": 18432, "gain": 18432, "wo_codes": 18496,
+    "home_picked_rows": 18432, "away_table0": 18432, "gain": 18432, "wo_codes": 18688,
     "gate11": 36864, "h_codes0": 36864,
     "wt_bf0": 26624, "away_picked_rows": 26624,
 }
@@ -62,9 +63,10 @@ def tile_list_league_market_features_kernel(
         psum = ctx.enter_context(tc.psum_pool(name="psum", bufs=1))
 
         def held(name, shape, dtype):
+            align = 256 if name.startswith(DMA_TILES) else 64
             if name in SHARED_AT:
-                return reuse.tile(shape, dtype, name=name, align_bytes=64, offset=SHARED_AT[name])
-            return keep.tile(shape, dtype, name=name, align_bytes=64)
+                return reuse.tile(shape, dtype, name=name, align_bytes=align, offset=SHARED_AT[name])
+            return keep.tile(shape, dtype, name=name, align_bytes=align)
 
         def zeroed_plane(name, width):
             plane = held(name, [P, width], U8)

@@ -402,13 +402,14 @@ def tile_list_league_market_features_kernel(
             if i == 1:
                 round_wt(1)
             if 1 <= i <= n:
-                if UNITS[i - 1][1] == 1:
-                    stadium(*UNITS[i - 1])
                 turn_and_add(*UNITS[i - 1])
             if 2 <= i <= n + 1:
                 scale_and_squash(*UNITS[i - 2])
             if i == JT - 1:
                 quantise_wt(1)
+                stadium(*UNITS[JT])
+            if JT < i < n:
+                stadium(*UNITS[i])
             if 3 <= i <= n + 2:
                 apply_gain(*UNITS[i - 3])
             if i == JT + 3:

@@ -41,7 +41,6 @@ HOME_BANKS = (4, 5, 6, 7, 0, 1, 2, 3)
 AWAY_BANKS = (6, 7, 0, 6, 7, 1, 6, 7)
 SUM_BANKS = (4, 5, 0, 4, 5, 0, 4, 5)
 OUT_BANKS = ((1,), (6,), (7,), (2, 3))
-DMA_TILES = ("home_table", "away_table", "stad_table", "wt_raw", "ws_", "wo_", "home_scale", "away_scale", "home_plane", "away_plane", "res")
 WT_PARTS = 2
 SHARED_AT = {
     "home_table0": 0, "away_table1": 0,
@@ -63,7 +62,7 @@ def tile_list_league_market_features_kernel(
         psum = ctx.enter_context(tc.psum_pool(name="psum", bufs=1))
 
         def held(name, shape, dtype):
-            align = 256 if name.startswith(DMA_TILES) else 64
+            align = 256
             if name in SHARED_AT:
                 return reuse.tile(shape, dtype, name=name, align_bytes=align, offset=SHARED_AT[name])
             return keep.tile(shape, dtype, name=name, align_bytes=align)

@@ -184,6 +184,8 @@ def tile_list_league_market_features_kernel(
                 ms = slice(part * step, (part + 1) * step)
                 dst = wt_bf[b][:].rearrange("p (t m j) -> p m t j", t=PACK, j=PACK)[:, ms, :, :]
                 src = wt_raw[b][:].rearrange("p j (m t) -> p m t j", t=PACK)[:, ms, :, :]
+                if part == 0 or b == 0:
+                    dst, src = dst.rearrange("p m t j -> p m j t"), src.rearrange("p m t j -> p m j t")
                 if part == 0:
                     nc.scalar.copy(out=dst, in_=src)
                 elif b == 1:

from contextlib import ExitStack

import concourse.mybir as mybir
from concourse.masks import make_identity

FLOPS = 3221225472

F32 = mybir.dt.float32
BF16 = mybir.dt.bfloat16
I32 = mybir.dt.int32
U32 = mybir.dt.uint32
U16 = mybir.dt.uint16
U8 = mybir.dt.uint8
FP8X4 = mybir.dt.float8_e4m3fn_x4
FP4X4 = mybir.dt.float4_e2m1fn_x4
ALU = mybir.AluOpType
ACT = mybir.ActivationFunctionType

P = 128
QUAD = 32
LIVE = 4
PACK = 4
PASS = P * PACK
S = 512
JT = S // P
T = 2048
T3 = 1024
K_PASSES = 2
H = 1024
N = 512
HALVES = H // PASS
LIST_ROWS = 16

UNITS = [(jt, b) for b in range(HALVES) for jt in range(JT)]
FUSED = UNITS[:3]
VECTOR_SUBTRACTS = UNITS[3:7]
EARLY_SUMS = UNITS[:2]
LAST_UNIT = UNITS[-1]
STAD_BANKS = (0, 1, 2, 3, 2, 3, 2, 3)
HOME_BANKS = (4, 5, 6, 7, 0, 1, 2, 3)
AWAY_BANKS = (6, 7, 0, 6, 7, 1, 6, 7)
SUM_BANKS = (4, 5, 0, 4, 5, 0, 4, 5)
OUT_BANKS = ((1,), (6,), (7,), (2, 3))
WT_PARTS = 2
SHARED_AT = {
    "home_table0": 0, "away_table1": 0,
    "home_scale_rows": 15360, "home_table1": 8192, "wt_raw1": 8192,
    "home_picked_rows": 18432, "away_table0": 18432, "gain": 18432, "wo_codes": 18688,
    "gate11": 36864, "h_codes0": 36864,
    "wt_bf0": 26624, "away_picked_rows": 26624,
}


def tile_list_league_market_features_kernel(
    tc, tab_words, tab_scales, tab2_words, tab2_scales, tab3_words, tab3_scales,
    offs, offs2, offs3, ws_words, ws_scales, wt, gh, wo_words, wo_scales, out,
):
    nc = tc.nc
    with ExitStack() as ctx:
        keep = ctx.enter_context(tc.tile_pool(name="keep", bufs=1))
        reuse = ctx.enter_context(tc.tile_pool(name="reuse", bufs=1))
        psum = ctx.enter_context(tc.psum_pool(name="psum", bufs=1))

        def held(name, shape, dtype):
            align = 256
            if name in SHARED_AT:
                return reuse.tile(shape, dtype, name=name, align_bytes=align, offset=SHARED_AT[name])
            return keep.tile(shape, dtype, name=name, align_bytes=align)

        def zeroed_plane(name, width):
            plane = held(name, [P, width], U8)
            nc.gpsimd.memset(plane[:].bitcast(I32), 0)
            return plane

        def load_plane(plane, scales, rows=range(LIVE)):
            passes = scales.shape[0]
            by_row = scales.rearrange("a (q r) c -> r q a c", r=LIVE)
            for r in rows:
                nc.sync.dma_start(
                    out=plane[r:P:QUAD, :].rearrange("q (a c) -> q a c", a=passes).bitcast(I32),
                    in_=by_row[r].bitcast(I32),
                )

        def load_words(name, words_of_pass):
            tile = held(name, [P, T], I32)
            nc.sync.dma_start(out=tile[:], in_=words_of_pass.rearrange("p t i -> p (t i)").bitcast(I32))
            return tile

        def load_list(name, lst):
            tile = keep.tile([P, S // LIST_ROWS], U16, name=name)
            nc.sync.dma_start(tile[:], lst)
            return tile

        def load_ws():
            tile = held("ws_codes", [P, K_PASSES, 2 * H], U8)
            nc.sync.dma_start(out=tile[:].bitcast(I32), in_=ws_words.rearrange("a p c -> p a c").bitcast(I32))
            return tile

        wt_rows = wt.rearrange("(p j) c -> p j c", j=PACK)

        def load_wt(b):
            raw = held("wt_raw%d" % b, [P, PACK, PASS], F32)
            nc.sync.dma_start(out=raw[:], in_=wt_rows[:, :, b * PASS : (b + 1) * PASS])
            return raw

        def scale_rows_tile(name, first):
            rows = held(name, [P, T], U8)
            nc.vector.memset(rows[first + QUAD : first + 2 * QUAD, :].bitcast(I32), 0)
            other = 2 * QUAD - first
            nc.vector.memset(rows[other : other + 2 * QUAD, :].bitcast(I32), 0)
            return rows

        def load_scale_rows(rows, scales, first):
            nc.sync.dma_start(
                out=rows[first : first + QUAD, :].bitcast(I32), in_=scales.rearrange("a q c -> q a c").bitcast(I32)
            )

        def place_rows(plane, picked):
            per_quad = LIVE * K_PASSES
            for q in (0, 2, 1, 3):
                nc.sync.dma_start(
                    out=plane[QUAD * q : QUAD * q + LIVE, :].bitcast(I32),
                    in_=picked[per_quad * q : per_quad * (q + 1), :].bitcast(I32),
                )
            return [plane[:, a * S : (a + 1) * S] for a in range(K_PASSES)]

        stad_table_plane = zeroed_plane("stad_table_plane", T3)
        ws_plane = zeroed_plane("ws_plane", K_PASSES * H)
        home_scale_rows = scale_rows_tile("home_scale_rows", 0)
        away_scale_rows = scale_rows_tile("away_scale_rows", 2 * QUAD)
        home_plane = zeroed_plane("home_plane", K_PASSES * S)
        away_plane = zeroed_plane("away_plane", K_PASSES * S)
        ident = held("ident", [P, P], F32)
        make_identity(nc, ident[:])

        def gather(name, window, lst, dtype):
            tile = held(name, [P, lst.shape[1] * LIST_ROWS], dtype)
            nc.vector.tensor_copy(out=tile[:], in_=window.indirect(lst))
            return tile

        def gather_words(name, table, lst, pieces):
            step = JT // pieces
            cols = step * P // LIST_ROWS
            tiles = [
                gather("%s_%d" % (name, i), table[:].bitcast(U32), lst[:, i * cols : (i + 1) * cols], U32)
                for i in range(pieces)
            ]
            return [tiles[jt // step][:, jt % step * P : (jt % step + 1) * P] for jt in range(JT)]

        def unit_tiles(name):
            return {(jt, b): held("%s%d%d" % (name, jt, b), [P, PASS], F32) for jt in range(JT) for b in range(HALVES)}

        gate = unit_tiles("gate")
        home_term = unit_tiles("home_term")
        away_term = unit_tiles("away_term")
        scaled = unit_tiles("scaled")
        squashed = unit_tiles("squashed")
        h_bf = [held("h_bf%d" % b, [P, S * PACK], BF16) for b in range(HALVES)]
        h_codes = [held("h_codes%d" % b, [P, S], U32) for b in range(HALVES)]
        h_plane = [held("h_plane%d" % b, [P, S], U8) for b in range(HALVES)]

        def bank_tile(k):
            return psum.tile([P, PASS], F32, name="bank%d" % k, tag="bank%d" % k, bufs=1)

        def channels_by_slot(bank):
            return bank[:].rearrange("p (m t) -> p t m", t=PACK)

        def slots(tile):
            return tile[:].rearrange("p (t m) -> p t m", t=PACK)

        def slots_by_market(bank):
            return bank[:].rearrange("p (t j) -> p j t", t=PACK)

        def markets(view):
            return view.rearrange("p (j t) -> p j t", t=PACK)

        wt_bf = [held("wt_bf%d" % b, [P, PASS * PACK], BF16) for b in range(HALVES)]
        wt_codes = [held("wt_codes%d" % b, [P, PASS], U32) for b in range(HALVES)]
        wt_plane = [held("wt_plane%d" % b, [P, PASS], U8) for b in range(HALVES)]

        def round_wt(b):
            step = P // WT_PARTS
            for part in range(WT_PARTS):
                ms = slice(part * step, (part + 1) * step)
                dst = wt_bf[b][:].rearrange("p (t m j) -> p m t j", t=PACK, j=PACK)[:, ms, :, :]
                src = wt_raw[b][:].rearrange("p j (m t) -> p m t j", t=PACK)[:, ms, :, :]
                if part == 0 or b == 0:
                    dst, src = dst.rearrange("p m t j -> p m j t"), src.rearrange("p m t j -> p m j t")
                if part == 0:
                    nc.scalar.copy(out=dst, in_=src)
                elif b == 1:
                    nc.gpsimd.tensor_scalar(out=dst, in0=src, scalar1=1.0, scalar2=0.0, op0=ALU.mult, op1=ALU.add)
                else:
                    nc.vector.tensor_copy(out=dst, in_=src)

        def quantise_wt(b):
            nc.vector.quantize_mx(out=wt_codes[b][:].bitcast(FP8X4), scales=wt_plane[b][:], in_=wt_bf[b][:])

        def stadium(jt, b):
            bank = bank_tile(STAD_BANKS[UNITS.index((jt, b))])
            codes = stad_codes[:, 2 * P * jt : 2 * P * (jt + 1)].bitcast(FP4X4)
            plane = stad_plane[:, jt * P : (jt + 1) * P]
            if (jt, b) in FUSED:
                nc.tensor.matmul_mx(
                    out=bank[:], lhsT=codes, lhsT_scale=plane,
                    rhs=wt_codes[b][:].bitcast(FP8X4), rhs_scale=wt_plane[b][:], start=True, stop=True,
                )
                nc.scalar.activation(out=gate[jt, b][:], in_=bank[:], func=ACT.Sigmoid, scale=2.0)
                return
            for t in range(PACK):
                nc.tensor.matmul_mx(
                    out=bank[:, t * P : (t + 1) * P],
                    lhsT=wt_codes[b][:, t * P : (t + 1) * P].bitcast(FP8X4),
                    lhsT_scale=wt_plane[b][:, t * P : (t + 1) * P],
                    rhs=codes, rhs_scale=plane, start=True, stop=True,
                )
            nc.scalar.activation(out=markets(gate[jt, b][:]), in_=slots_by_market(bank), func=ACT.Tanh)

        def side_pass(codes, planes, jt, b, bank, a):
            nc.tensor.matmul_mx(
                out=bank[:],
                lhsT=codes[a][jt].bitcast(FP8X4),
                lhsT_scale=planes[a][:, jt * P : (jt + 1) * P],
                rhs=ws_codes[:, a, 2 * b * PASS : 2 * (b + 1) * PASS].bitcast(FP4X4),
                rhs_scale=ws_plane[:, a * H + b * PASS : a * H + (b + 1) * PASS],
                start=(a == 0),
                stop=(a == K_PASSES - 1),
            )

        def gated_read(term, bank, jt, b, factor):
            nc.vector.scalar_tensor_tensor(
                out=slots(term[jt, b]), in0=channels_by_slot(bank), scalar=factor, in1=slots(gate[jt, b]),
                op0=ALU.mult, op1=ALU.mult,
            )

        side_bank = {}

        def home_first(jt, b):
            side_bank[jt, b] = bank_tile(HOME_BANKS[UNITS.index((jt, b))])
            side_pass(home_codes, home_planes, jt, b, side_bank[jt, b], 0)

        def home(jt, b):
            bank = side_bank[jt, b]
            side_pass(home_codes, home_planes, jt, b, bank, 1)
            if (jt, b) in FUSED:
                gated_read(home_term, bank, jt, b, 2.0)
            else:
                nc.scalar.activation(out=slots(home_term[jt, b]), in_=channels_by_slot(bank), func=ACT.Copy)

        def away_first(jt, b):
            side_bank[jt, b] = bank_tile(AWAY_BANKS[UNITS.index((jt, b))])
            side_pass(away_codes, away_planes, jt, b, side_bank[jt, b], 0)

        def away(jt, b):
            if (jt, b) not in FUSED:
                away_first(jt, b)
            bank = side_bank[jt, b]
            side_pass(away_codes, away_planes, jt, b, bank, 1)
            if (jt, b) in FUSED:
                gated_read(away_term, bank, jt, b, -2.0)
            elif (jt, b) in VECTOR_SUBTRACTS:
                nc.vector.tensor_tensor(
                    out=slots(away_term[jt, b]), in0=slots(home_term[jt, b]), in1=channels_by_slot(bank), op=ALU.subtract,
                )
            else:
                nc.scalar.activation(out=slots(away_term[jt, b]), in_=channels_by_slot(bank), func=ACT.Copy, scale=-1.0)

        sum_bank = {}

        def turn(term, jt, b, first, last):
            for t in range(PACK):
                nc.tensor.matmul(
                    out=sum_bank[jt, b][:, t * P : (t + 1) * P], lhsT=term[jt, b][:, t * P : (t + 1) * P], rhs=ident[:],
                    is_transpose=True, start=(first and t == 0), stop=(last and t == PACK - 1),
                )

        def open_sum(jt, b):
            sum_bank[jt, b] = bank_tile(SUM_BANKS[UNITS.index((jt, b))])

        def turn_and_add(jt, b):
            if (jt, b) in EARLY_SUMS:
                turn(away_term, jt, b, False, True)
            elif (jt, b) in VECTOR_SUBTRACTS:
                open_sum(jt, b)
                turn(away_term, jt, b, True, True)
            else:
                open_sum(jt, b)
                turn(home_term, jt, b, True, False)
                turn(away_term, jt, b, False, True)

        def market_ranges(jt, b):
            count = 2 if (jt, b) == LAST_UNIT else 1
            return [slice(i * P // count, (i + 1) * P // count) for i in range(count)]

        def scale_and_squash(jt, b):
            if (jt, b) in FUSED:
                nc.scalar.activation(out=markets(squashed[jt, b][:]), in_=slots_by_market(sum_bank[jt, b]), func=ACT.Tanh)
                return
            for js in market_ranges(jt, b):
                nc.vector.scalar_tensor_tensor(
                    out=markets(scaled[jt, b][:])[:, js, :], in0=markets(gate[jt, b][:])[:, js, :], scalar=1.0,
                    in1=slots_by_market(sum_bank[jt, b])[:, js, :], op0=ALU.add, op1=ALU.mult,
                )
                cols = slice(js.start * PACK, js.stop * PACK)
                nc.scalar.activation(out=squashed[jt, b][:, cols], in_=scaled[jt, b][:, cols], func=ACT.Tanh)

        def apply_gain(jt, b):
            engine = nc.gpsimd if b == 0 else nc.vector
            for js in market_ranges(jt, b):
                engine.tensor_tensor(
                    out=markets(h_bf[b][:, jt * PASS : (jt + 1) * PASS])[:, js, :],
                    in0=markets(squashed[jt, b][:])[:, js, :],
                    in1=gain[:, b : b + 1, :].to_broadcast([P, js.stop - js.start, PACK]), op=ALU.mult,
                )

        def quantise_h(b, first, last):
            nc.vector.quantize_mx(
                out=h_codes[b][:, first * P : (last + 1) * P].bitcast(FP8X4),
                scales=h_plane[b][:, first * P : (last + 1) * P],
                in_=h_bf[b][:, first * PASS : (last + 1) * PASS],
            )

        out_rows = out.rearrange("(nt p) j -> p nt j", p=P)

        def features(jt):
            parts = 2 if jt == JT - 1 else 1
            tiles = N // P // parts
            banks = [bank_tile(k) for k in OUT_BANKS[jt]]
            for b in range(HALVES):
                for nt in range(N // P):
                    part, place = divmod(nt, tiles)
                    nc.tensor.matmul_mx(
                        out=banks[part][:, place * P : (place + 1) * P],
                        lhsT=wo_codes[:, b, nt * P : (nt + 1) * P].bitcast(FP8X4),
                        lhsT_scale=wo_plane[:, b * N + nt * P : b * N + (nt + 1) * P],
                        rhs=h_codes[b][:, jt * P : (jt + 1) * P].bitcast(FP8X4),
                        rhs_scale=h_plane[b][:, jt * P : (jt + 1) * P],
                        start=(b == 0 and place == 0),
                        stop=(b == HALVES - 1 and place == tiles - 1),
                    )
            for part in range(parts):
                res = held("res%d%d" % (jt, part), [P, tiles, P], F32)
                sums = banks[part][:, 0 : tiles * P].rearrange("p (n j) -> p n j", j=P)
                if part == 0:
                    nc.scalar.copy(out=res[:], in_=sums)
                else:
                    nc.vector.tensor_copy(out=res[:], in_=sums)
                nc.sync.dma_start(out=out_rows[:, part * tiles : (part + 1) * tiles, jt * P : (jt + 1) * P], in_=res[:])

        home_list = load_list("home_list", offs)
        load_scale_rows(home_scale_rows, tab_scales, 0)
        stad_list = load_list("stad_list", offs3)
        stad_table = held("stad_table", [P, 2 * T3], U8)
        nc.sync.dma_start(out=stad_table[:].bitcast(I32), in_=tab3_words[0].bitcast(I32))
        load_plane(stad_table_plane, tab3_scales, range(LIVE - 1))
        wt_raw = [load_wt(0)]
        load_plane(stad_table_plane, tab3_scales, range(LIVE - 1, LIVE))
        ws_codes = load_ws()
        away_list = load_list("away_list", offs2)
        load_scale_rows(away_scale_rows, tab2_scales, 2 * QUAD)
        load_plane(ws_plane, ws_scales, range(LIVE // 2))
        home_table0 = load_words("home_table0", tab_words[0])
        load_plane(ws_plane, ws_scales, range(LIVE // 2, LIVE))
        home_planes = place_rows(home_plane, gather("home_picked_rows", home_scale_rows[:], home_list[:], U8)[:])
        home_table1 = load_words("home_table1", tab_words[1])
        away_table0 = load_words("away_table0", tab2_words[0])
        stad_codes = held("stad_codes", [P, 2 * S], U8)
        nc.vector.tensor_copy(out=stad_codes[:].bitcast(U16), in_=stad_table[:].bitcast(U16).indirect(stad_list[:]))
        stad_plane = gather("stad_plane", stad_table_plane[:], stad_list[:], U8)
        round_wt(0)
        quantise_wt(0)
        for jt in range(JT):
            stadium(jt, 0)
        away_picked = gather("away_picked_rows", away_scale_rows[:], away_list[:], U8)
        home_codes = [gather_words("home_codes0", home_table0, home_list, 2)]
        away_table1 = load_words("away_table1", tab2_words[1])
        away_planes = place_rows(away_plane, away_picked[2 * QUAD : P, :])
        for unit in sorted(UNITS, key=lambda u: (u[0] // 2, u[1])):
            home_first(*unit)
        home_codes.append(gather_words("home_codes1", home_table1, home_list, 2))
        wt_raw.append(load_wt(1))
        for unit in UNITS:
            home(*unit)
        for unit in EARLY_SUMS:
            open_sum(*unit)
            turn(home_term, *unit, True, False)
        gain = held("gain", [P, HALVES, PACK], F32)
        nc.sync.dma_start(out=gain[:], in_=gh.rearrange("(b p t) -> p b t", b=HALVES, t=PACK))
        wo_codes = held("wo_codes", [P, HALVES, N], I32)
        nc.sync.dma_start(out=wo_codes[:], in_=wo_words.rearrange("a p c i -> p a (c i)").bitcast(I32))
        wo_plane = zeroed_plane("wo_plane", HALVES * N)
        load_plane(wo_plane, wo_scales)

        away_codes = [gather_words("away_codes0", away_table0, away_list, 1)]
        for unit in FUSED:
            away_first(*unit)
        away_codes.append(gather_words("away_codes1", away_table1, away_list, 2))

        n = len(UNITS)
        for i in range(n + 4):
            if i < n:
                away(*UNITS[i])
            if i == 1:
                round_wt(1)
            if 1 <= i <= n:
                turn_and_add(*UNITS[i - 1])
            if 2 <= i <= n + 1:
                scale_and_squash(*UNITS[i - 2])
            if i == JT - 1:
                quantise_wt(1)
                stadium(*UNITS[JT])
            if JT < i < n:
                stadium(*UNITS[i])
            if 3 <= i <= n + 2:
                apply_gain(*UNITS[i - 3])
            if i == JT + 3:
                quantise_h(0, 0, JT - 1)
            if i > JT + 3:
                jt = UNITS[i - 4][0]
                quantise_h(1, jt, jt)
                features(jt)
